import numpy as np
import ml_dtypes


def mxq(x, axis, fmt="e4m3"):
    dtype, down = {"e4m3": (ml_dtypes.float8_e4m3fn, 7), "e5m2": (ml_dtypes.float8_e5m2, 14)}[fmt]
    v = np.moveaxis(np.asarray(x, np.float32).astype(ml_dtypes.bfloat16).astype(np.float64), axis, -1)
    blocks = v.reshape(v.shape[:-1] + (-1, 32))
    amax = np.abs(blocks).max(-1, keepdims=True)
    byte = np.maximum(np.where(amax > 0, np.frexp(amax)[1] - 1 + 127, 0) - down, 1)
    scale = np.exp2(byte - 127.0)
    codes = (blocks / scale).astype(np.float32).astype(dtype).astype(np.float64)
    return np.moveaxis((codes * scale).reshape(v.shape), -1, axis)


WIDE = False


def mx_kscale(k):
    if not WIDE:
        return np.ones(k)
    levels = np.array([18, -18])
    if k % 512:
        return np.exp2(np.random.permutation(np.resize(levels, k // 32))).repeat(32)
    a = np.empty((k // 512, 16))
    for p in range(k // 512):
        a[p, :8] = np.random.permutation(np.resize(levels, 8))
        for g in range(8):
            far = levels[np.abs(levels - a[p, g]) >= 10]
            a[p, g + 8] = far[np.random.randint(len(far))]
    return np.exp2(a.ravel()).repeat(32)


def f64(x):
    return np.asarray(x).astype(np.float64)


def striped(idx):
    return np.tile(np.asarray(idx).reshape(-1, 16).T, (8, 1)).astype(np.uint16)


def unstriped(offs):
    return offs[:16].T.reshape(-1).astype(np.int64)


B = 2


def sig(x):
    return 1.0 / (1.0 + np.exp(-x))


def setup_inputs():
    n = np.random.standard_normal
    uni = np.random.uniform
    idx = np.random.permutation(2048)[:1024]
    f_d = mx_kscale(512)
    f_e = mx_kscale(512)
    f_i = np.ones(2048)
    f_i[idx] = mx_kscale(1024)
    return {
        "xT": (n((512, 2048)) / np.sqrt(512) * f_d[:, None] * f_i[None, :]).astype(np.float32),
        "dyT": (n((512, 2048)) * f_e[:, None] * f_i[None, :]).astype(np.float32),
        "w1": (n((2, 512, 512)) / f_d[:, None]).astype(np.float32),
        "w2": (n((2, 512, 512)) / np.sqrt(512) / f_e[None, :]).astype(np.float32),
        "ts": np.tile(uni(0.75, 1.3, 2048) / np.sqrt(512) / f_i, (128, 1)).astype(np.float32),
        "tx": np.tile(uni(0.75, 1.3, 2048) / f_i, (128, 1)).astype(np.float32),
        "cf": (uni(0.75, 1.3, (512, 1))).astype(np.float32),
        "offs": striped(idx),
    }


def reference(xT, dyT, w1, w2, ts, tx, cf, offs):
    idx = unstriped(offs).reshape(B, 512)
    xT_i = f64(xT)[:, idx].transpose(1, 0, 2)
    dyT_i = f64(dyT)[:, idx].transpose(1, 0, 2)
    ts_i = f64(ts)[:1][:, idx].transpose(1, 0, 2)
    tx_i = f64(tx)[:1][:, idx].transpose(1, 0, 2)
    a = mxq(f64(w1), 1, "e4m3").transpose(0, 2, 1) @ mxq(xT_i, 1, "e4m3")
    z = f64(cf) * tx_i * a
    h = ts_i * z * sig(z)
    dh = mxq(f64(w2), 2, "e4m3") @ mxq(dyT_i, 1, "e5m2")
    da = f64(cf) * tx_i * ts_i * dh * sig(z) * (1.0 + z * (1.0 - sig(z)))
    out_0 = mxq(xT_i, 2, "e4m3") @ mxq(da, 2, "e5m2").transpose(0, 2, 1)
    out_1 = mxq(h, 2, "e4m3") @ mxq(dyT_i, 2, "e5m2").transpose(0, 2, 1)
    return out_0, out_1

@@ -1,0 +1,293 @@
+from contextlib import ExitStack
+
+import concourse.mybir as mybir
+from concourse.masks import make_identity
+
+F32 = mybir.dt.float32
+BF16 = mybir.dt.bfloat16
+U32 = mybir.dt.uint32
+U16 = mybir.dt.uint16
+U8 = mybir.dt.uint8
+E4M3 = mybir.dt.float8_e4m3fn_x4
+E5M2 = mybir.dt.float8_e5m2_x4
+ALU = mybir.AluOpType
+ACT = mybir.ActivationFunctionType
+
+P = 128
+PACK = 4
+N = 512
+EXPERTS = 2
+TOKENS = 2048
+FLOPS = 4 * 2 * EXPERTS * N * N * N
+
+
+def tile_attend_gxfull_sil_W_kernel(tc, xT, dyT, w1, w2, ts, tx, cf, offs, out_0, out_1):
+    nc = tc.nc
+    with ExitStack() as ctx:
+        held = ctx.enter_context(tc.tile_pool(name="held", bufs=1))
+        big = ctx.enter_context(tc.tile_pool(name="big", bufs=1))
+        psum = ctx.enter_context(tc.psum_pool(name="psum", bufs=1))
+
+        def big_tile(slot, name, width=PACK * N):
+            return big.tile([P, width], F32, name=name, tag=slot, align_bytes=64)
+
+        bank_tiles = {
+            kind: [psum.tile([P, N], F32, name="%s_%d" % (kind, j)) for j in range(4)] for kind in ("turn", "sums")
+        }
+        pair = [held.tile([P, 2 * PACK * N], BF16, name="pair_%d" % j, align_bytes=64) for j in range(4)]
+        taken = []
+
+        def bank(kind="turn"):
+            taken.append(kind)
+            return bank_tiles[kind][(taken.count(kind) - 1) % 4]
+
+        def half(j, k):
+            return pair[j][:, k * PACK * N : (k + 1) * PACK * N]
+
+        def quantize(src, fmt, name):
+            width = src.shape[1] // PACK
+            codes = held.tile([P, width], U32, name=name + "_codes", align_bytes=64)
+            scales = held.tile([P, width], U8, name=name + "_scales", align_bytes=64)
+            nc.vector.quantize_mx(out=codes[:].bitcast(fmt), scales=scales[:], in_=src)
+            return [(codes[:, k : k + N], scales[:, k : k + N], fmt) for k in range(0, width, N)]
+
+        def product(dst, stationary, j, moving):
+            cols = slice(j * P, (j + 1) * P)
+            nc.tensor.matmul_mx(
+                out=dst[:],
+                lhsT=stationary[0][:, cols].bitcast(stationary[2]),
+                lhsT_scale=stationary[1][:, cols],
+                rhs=moving[0].bitcast(moving[2]),
+                rhs_scale=moving[1],
+                start=True,
+                stop=True,
+            )
+
+        offsets = held.tile([P, EXPERTS * N // 16], U16, name="offsets")
+        nc.sync.dma_start(offsets[:], offs)
+
+        def listed(window, b):
+            return window[:].indirect(offsets[:, b * N // 16 : (b + 1) * N // 16])
+
+        ts_win = big_tile("ts", "ts_win")
+        tx_win = big_tile("tx", "tx_win")
+        nc.gpsimd.memset(tx_win[0 : P - 1, :], 0.0)
+        nc.vector.memset(ts_win[0 : P - 1, :], 0.0)
+        cf_cols = held.tile([P, PACK], F32, name="cf_cols")
+        nc.scalar.dma_start(tx_win[P - 1 : P, :], tx[0:1, :])
+        nc.scalar.dma_start(ts_win[P - 1 : P, :], ts[0:1, :])
+        nc.scalar.dma_start(cf_cols[:], cf.rearrange("(p j) o -> p (j o)", j=PACK))
+        ident = held.tile([P, P], F32, name="ident")
+        make_identity(nc, ident[:])
+
+        w1_raw = [big_tile("w1_%d" % b, "w1_raw") for b in range(EXPERTS)]
+        w2_raw = [big_tile("w2_%d" % b, "w2_raw") for b in range(EXPERTS)]
+        x_plane = [big_tile("x_%d" % t, "x_plane") for t in range(PACK)]
+        dy_plane = [big_tile("dy_%d" % t, "dy_plane") for t in range(PACK)]
+
+        def load_w1(b):
+            nc.sync.dma_start(w1_raw[b][:], w1[b].rearrange("(p j) f -> p (j f)", j=PACK))
+
+        def load_w2(b):
+            nc.sync.dma_start(
+                w2_raw[b][:].rearrange("p (c e) -> p c e", c=PACK), w2[b].rearrange("(c p) e -> p c e", c=PACK)
+            )
+
+        def load_planes(planes, src, which):
+            for t in which:
+                nc.sync.dma_start(planes[t][:], src.rearrange("(p t) n -> t p n", t=PACK)[t])
+
+        load_w1(0)
+        load_planes(x_plane, xT, range(PACK))
+        load_planes(dy_plane, dyT, (0,))
+        load_w1(1)
+        load_planes(dy_plane, dyT, (1, 2, 3))
+        load_w2(0)
+        load_w2(1)
+
+        cf_row = held.tile([P, N], F32, name="cf_row")
+        spread = bank()
+        for j in range(PACK):
+            nc.tensor.transpose(spread[:, j * P : (j + 1) * P], cf_cols[:, j : j + 1].to_broadcast([P, P]), ident[:])
+        nc.scalar.copy(cf_row[:].rearrange("p (m j) -> p m j", j=PACK), spread[:].rearrange("p (j m) -> p m j", j=PACK))
+
+        def token_columns(window, name):
+            picked = held.tile([P, EXPERTS * N], F32, name=name + "_picked")
+            nc.vector.tensor_copy(picked[:], window[:].indirect(offsets[:]))
+            cols = held.tile([P, EXPERTS * PACK], F32, name=name + "_cols")
+            for b in range(EXPERTS):
+                turned = bank()
+                for r in range(PACK):
+                    nc.tensor.transpose(turned[:, r * P : (r + 1) * P], picked[:, b * N + r : (b + 1) * N : PACK], ident[:])
+                nc.scalar.copy(cols[:, b * PACK : (b + 1) * PACK], turned[:, P - 1 : N : P])
+            return cols
+
+        def group_w1(b, g):
+            nc.scalar.copy(
+                g.rearrange("p (c i j) -> p c j i", i=4, j=PACK),
+                w1_raw[b][:].rearrange("p (j c i) -> p c j i", i=4, j=PACK),
+            )
+
+        def group_w2(b, g, kind):
+            for c in range(PACK):
+                turned = bank(kind)
+                for t in range(PACK):
+                    nc.tensor.transpose(turned[:, t * P : (t + 1) * P], w2_raw[b][:, c * N + t : (c + 1) * N : PACK], ident[:])
+                nc.scalar.copy(
+                    g[:, c * N : (c + 1) * N].rearrange("p (f t) -> p f t", t=PACK),
+                    turned[:].rearrange("p (t f) -> p f t", t=PACK),
+                )
+
+        def gather(planes, b, picked, which):
+            for t in which:
+                nc.vector.tensor_copy(picked[:, t * N : (t + 1) * N], listed(planes[t], b))
+
+        def along_features(picked, g):
+            nc.scalar.copy(
+                g.rearrange("p (r s t) -> p s t r", r=PACK, t=PACK),
+                picked[:].rearrange("p (t s r) -> p s t r", r=PACK, t=PACK),
+            )
+
+        def along_slots(picked, natural, g):
+            words = picked[:].bitcast(F32)
+            g_words = g.bitcast(F32)
+            for half in range(2):
+                turned = bank()
+                for tt in range(2):
+                    for v in range(2):
+                        t = 2 * half + tt
+                        k = 2 * tt + v
+                        nc.tensor.transpose(
+                            turned[:, k * P : (k + 1) * P], words[:, t * 256 + v : (t + 1) * 256 : 2], ident[:]
+                        )
+                if natural:
+                    nc.scalar.copy(
+                        g_words.rearrange("s (p h k) -> s h p k", h=2, k=4)[:, half],
+                        turned[:].rearrange("s (k p) -> s p k", k=4),
+                    )
+                else:
+                    nc.scalar.copy(
+                        g_words[:, half * N : (half + 1) * N].rearrange("s (tt p v) -> s tt p v", tt=2, v=2),
+                        turned[:].rearrange("s (tt v p) -> s tt p v", tt=2, v=2),
+                    )
+
+        def scaled_product(stationary, moving, cols, b, dst):
+            for r in range(PACK):
+                acc = bank("sums")
+                product(acc, stationary, r, moving)
+                nc.vector.scalar_tensor_tensor(
+                    dst[r], acc[:], cols[:, b * PACK + r : b * PACK + r + 1], cf_row[:], ALU.mult, ALU.mult
+                )
+
+        def interleaved(func, scale, dst, src):
+            nc.scalar.activation(
+                dst.rearrange("p (c i r) -> p c r i", i=4, r=PACK),
+                src.rearrange("p r (c i) -> p c r i", i=4),
+                func,
+                scale=scale,
+            )
+
+        def result(stationary, moving, rows, slot, name):
+            staged = big_tile(slot, name)
+            for j in range(PACK):
+                acc = bank("turn")
+                product(acc, stationary, j, moving)
+                nc.scalar.copy(staged[:, j * N : (j + 1) * N], acc[:])
+                nc.sync.dma_start(rows[j], staged[:, j * N : (j + 1) * N])
+
+        tx_cols = token_columns(tx_win, "tx")
+        ts_cols = token_columns(ts_win, "ts")
+        x_picked = [held.tile([P, PACK * N], BF16, name="x_picked_%d" % b, align_bytes=64) for b in range(EXPERTS)]
+        dy_picked = [held.tile([P, PACK * N], BF16, name="dy_picked_%d" % b, align_bytes=64) for b in range(EXPERTS)]
+        for b in range(EXPERTS):
+            gather(x_plane, b, x_picked[b], range(PACK))
+            group_w1(b, half(b, 0))
+        txts_cols = held.tile([P, EXPERTS * PACK], F32, name="txts_cols")
+        nc.gpsimd.tensor_tensor(txts_cols[:], tx_cols[:], ts_cols[:], ALU.mult)
+
+        z = [big_tile(slot, "z") for slot in ("tx", "ts")]
+        for b in range(EXPERTS):
+            along_features(x_picked[b], half(b, 1))
+            w1_q, x_feat = quantize(pair[b][:], E4M3, "first_%d" % b)
+            scaled_product(x_feat, w1_q, tx_cols, b, [z[b][:, r * N : (r + 1) * N] for r in range(PACK)])
+        gather(dy_plane, 0, dy_picked[0], range(PACK))
+        gather(dy_plane, 1, dy_picked[1], range(PACK))
+        for b in range(EXPERTS):
+            along_slots(x_picked[b], False, half(2, b))
+        x_slot = quantize(pair[2][:], E4M3, "x_slot")
+
+        silu = [big_tile("x_%d" % b, "silu") for b in range(EXPERTS)]
+        slope = [big_tile("dy_%d" % (2 + b), "slope") for b in range(EXPERTS)]
+        planes = [z[b][:].rearrange("p (r n) -> p r n", r=PACK) for b in range(EXPERTS)]
+        interleaved(ACT.Silu, 1.0, silu[0][:], planes[0])
+        interleaved(ACT.Silu, 1.0, silu[1][:], planes[1])
+
+        def hidden(b, g, cols):
+            nc.vector.tensor_tensor(
+                g[:, cols].rearrange("p (f r) -> p f r", r=PACK),
+                silu[b][:, cols].rearrange("p (f r) -> p f r", r=PACK),
+                ts_cols[:, b * PACK : (b + 1) * PACK].unsqueeze(1).to_broadcast([P, (cols.stop - cols.start) // PACK, PACK]),
+                ALU.mult,
+            )
+
+        def hidden_gradient(b, dy_feat, w2_q):
+            dh = big_tile("w1_%d" % b, "dh")
+            scaled_product(dy_feat, w2_q, txts_cols, b, [dh[:, r * N : (r + 1) * N] for r in range(PACK)])
+            return dh
+
+        def slope_less_one(b):
+            nc.vector.scalar_tensor_tensor(slope[b][:], silu[b][:], 1.0, slope[b][:], ALU.subtract, ALU.mult)
+
+        def first_gradient(b, dh, g):
+            nc.vector.scalar_tensor_tensor(
+                g.rearrange("p (f r) -> p f r", r=PACK),
+                slope[b][:].rearrange("p (f r) -> p f r", r=PACK),
+                1.0,
+                dh[:].rearrange("p (r f) -> p f r", r=PACK),
+                ALU.add,
+                ALU.mult,
+            )
+            return quantize(g, E5M2, "da_%d" % b)[0]
+
+        hidden(0, half(0, 0), slice(0, PACK * N))
+        along_features(dy_picked[0], half(1, 0))
+        group_w2(0, half(0, 1), "turn")
+        dy_feat = quantize(half(1, 0), E5M2, "dy_feat_0")[0]
+        h_q, w2_q = quantize(pair[0][:], E4M3, "h_w2")
+        dh0 = hidden_gradient(0, dy_feat, w2_q)
+        interleaved(ACT.Sigmoid, -1.0, slope[0][:], planes[0])
+        slope_less_one(0)
+        da0 = first_gradient(0, dh0, half(2, 0))
+        along_features(dy_picked[1], half(1, 1))
+        group_w2(1, half(2, 1), "sums")
+        dy_feat = quantize(half(1, 1), E5M2, "dy_feat_1")[0]
+        w2_q = quantize(half(2, 1), E4M3, "w2_1")[0]
+        interleaved(ACT.Sigmoid, -1.0, slope[1][:], planes[1])
+        slope_less_one(1)
+        dh1 = hidden_gradient(1, dy_feat, w2_q)
+        for b in range(EXPERTS):
+            along_slots(dy_picked[b], True, half(3, b))
+        dy_slot = quantize(pair[3][:], E5M2, "dy_slot")
+        result(x_slot[0], da0, out_0[0].rearrange("(p t) f -> t p f", t=PACK), "x_2", "staged")
+        g = half(0, 0)
+        da1 = first_gradient(1, dh1, g)
+        result(h_q, dy_slot[0], out_1[0].rearrange("(c p) e -> c p e", c=PACK), "x_3", "staged")
+        result(x_slot[1], da1, out_0[1].rearrange("(p t) f -> t p f", t=PACK), "dy_0", "staged")
+
+        codes = held.tile([P, N], U32, name="h_1_codes", align_bytes=64)
+        scales = held.tile([P, N], U8, name="h_1_scales", align_bytes=64)
+        staged = big_tile("dy_1", "staged")
+        rows = out_1[1].rearrange("(c p) e -> c p e", c=PACK)
+        for c in range(PACK):
+            hidden(1, g, slice(c * N, (c + 1) * N))
+            nc.vector.quantize_mx(
+                out=codes[:, c * P : (c + 1) * P].bitcast(E4M3), scales=scales[:, c * P : (c + 1) * P], in_=g[:, c * N : (c + 1) * N]
+            )
+        for c in range(PACK):
+            acc = bank("sums")
+            product(acc, (codes, scales, E4M3), c, dy_slot[1])
+            if c % 2:
+                nc.scalar.copy(staged[:, c * N : (c + 1) * N], acc[:])
+            else:
+                nc.vector.tensor_copy(staged[:, c * N : (c + 1) * N], acc[:])
+            nc.sync.dma_start(rows[c], staged[:, c * N : (c + 1) * N])

@@ -72,11 +72,15 @@ def tile_attend_gxfull_sil_W_kernel(tc, xT, dyT, w1, w2, ts, tx, cf, offs, out_0
         ts_win = big_tile("ts", "ts_win")
         tx_win = big_tile("tx", "tx_win")
         nc.gpsimd.memset(tx_win[0 : P - 1, :], 0.0)
+        warm = held.tile([P, 1], F32, name="warm")
+        nc.vector.memset(warm[:, 0:1], 0.0)
         nc.vector.memset(ts_win[0 : P - 1, :], 0.0)
         cf_cols = held.tile([P, PACK], F32, name="cf_cols")
         nc.scalar.dma_start(tx_win[P - 1 : P, :], tx[0:1, :])
         nc.scalar.dma_start(ts_win[P - 1 : P, :], ts[0:1, :])
         nc.scalar.dma_start(cf_cols[:], cf.rearrange("(p j) o -> p (j o)", j=PACK))
+        warmed = held.tile([P, 1], F32, name="warmed")
+        nc.scalar.activation(warmed[:], warm[:, 0:1], ACT.Sigmoid)
         ident = held.tile([P, P], F32, name="ident")
         make_identity(nc, ident[:])
 
@@ -124,8 +128,8 @@ def tile_attend_gxfull_sil_W_kernel(tc, xT, dyT, w1, w2, ts, tx, cf, offs, out_0
 
         def group_w1(b, g):
             nc.scalar.copy(
-                g.rearrange("p (c i j) -> p c j i", i=4, j=PACK),
-                w1_raw[b][:].rearrange("p (j c i) -> p c j i", i=4, j=PACK),
+                g.rearrange("p (c i j) -> p c j i", i=2, j=PACK),
+                w1_raw[b][:].rearrange("p (j c i) -> p c j i", i=2, j=PACK),
             )
 
         def group_w2(b, g, kind):
@@ -179,13 +183,11 @@ def tile_attend_gxfull_sil_W_kernel(tc, xT, dyT, w1, w2, ts, tx, cf, offs, out_0
                     dst[r], acc[:], cols[:, b * PACK + r : b * PACK + r + 1], cf_row[:], ALU.mult, ALU.mult
                 )
 
-        def interleaved(func, scale, dst, src):
-            nc.scalar.activation(
-                dst.rearrange("p (c i r) -> p c r i", i=4, r=PACK),
-                src.rearrange("p r (c i) -> p c r i", i=4),
-                func,
-                scale=scale,
-            )
+        def woven(dst):
+            return dst.rearrange("p (c i r) -> p c r i", i=2, r=PACK)
+
+        def strands(src, cols):
+            return src[:].rearrange("p (r n) -> p r n", r=PACK)[:, :, cols].rearrange("p r (c i) -> p c r i", i=2)
 
         def result(stationary, moving, rows, slot, name):
             staged = big_tile(slot, name)
@@ -204,6 +206,7 @@ def tile_attend_gxfull_sil_W_kernel(tc, xT, dyT, w1, w2, ts, tx, cf, offs, out_0
             group_w1(b, half(b, 0))
         txts_cols = held.tile([P, EXPERTS * PACK], F32, name="txts_cols")
         nc.gpsimd.tensor_tensor(txts_cols[:], tx_cols[:], ts_cols[:], ALU.mult)
+        nc.gpsimd.tensor_scalar(txts_cols[:], txts_cols[:], -1.0, 0.0, ALU.mult, ALU.add)
 
         z = [big_tile(slot, "z") for slot in ("tx", "ts")]
         for b in range(EXPERTS):
@@ -216,17 +219,16 @@ def tile_attend_gxfull_sil_W_kernel(tc, xT, dyT, w1, w2, ts, tx, cf, offs, out_0
             along_slots(x_picked[b], False, half(2, b))
         x_slot = quantize(pair[2][:], E4M3, "x_slot")
 
-        silu = [big_tile("x_%d" % b, "silu") for b in range(EXPERTS)]
-        slope = [big_tile("dy_%d" % (2 + b), "slope") for b in range(EXPERTS)]
-        planes = [z[b][:].rearrange("p (r n) -> p r n", r=PACK) for b in range(EXPERTS)]
-        interleaved(ACT.Silu, 1.0, silu[0][:], planes[0])
-        interleaved(ACT.Silu, 1.0, silu[1][:], planes[1])
+        slope = [big_tile("x_%d" % b, "slope") for b in range(EXPERTS)]
+        for b in range(EXPERTS):
+            nc.scalar.activation(slope[b][:], z[b][:], ACT.Sigmoid)
+        silu = []
 
         def hidden(b, g, cols):
             nc.vector.tensor_tensor(
-                g[:, cols].rearrange("p (f r) -> p f r", r=PACK),
-                silu[b][:, cols].rearrange("p (f r) -> p f r", r=PACK),
-                ts_cols[:, b * PACK : (b + 1) * PACK].unsqueeze(1).to_broadcast([P, (cols.stop - cols.start) // PACK, PACK]),
+                woven(g[:, cols.start * PACK : cols.stop * PACK]),
+                strands(silu[b], cols),
+                ts_cols[:, b * PACK : (b + 1) * PACK].unsqueeze(1).unsqueeze(3).to_broadcast([P, (cols.stop - cols.start) // 2, PACK, 2]),
                 ALU.mult,
             )
 
@@ -235,35 +237,33 @@ def tile_attend_gxfull_sil_W_kernel(tc, xT, dyT, w1, w2, ts, tx, cf, offs, out_0
             scaled_product(dy_feat, w2_q, txts_cols, b, [dh[:, r * N : (r + 1) * N] for r in range(PACK)])
             return dh
 
-        def slope_less_one(b):
-            nc.vector.scalar_tensor_tensor(slope[b][:], silu[b][:], 1.0, slope[b][:], ALU.subtract, ALU.mult)
+        def finish_slope(b, slot):
+            mirrored = big_tile(slot, "mirrored")
+            nc.scalar.activation(mirrored[:], z[b][:], ACT.Silu, scale=-1.0)
+            nc.vector.scalar_tensor_tensor(slope[b][:], mirrored[:], 1.0, slope[b][:], ALU.subtract, ALU.mult)
+
+        def make_silu(b, slot):
+            silu.append(big_tile(slot, "silu"))
+            nc.scalar.activation(silu[b][:], z[b][:], ACT.Silu)
 
         def first_gradient(b, dh, g):
-            nc.vector.scalar_tensor_tensor(
-                g.rearrange("p (f r) -> p f r", r=PACK),
-                slope[b][:].rearrange("p (f r) -> p f r", r=PACK),
-                1.0,
-                dh[:].rearrange("p (r f) -> p f r", r=PACK),
-                ALU.add,
-                ALU.mult,
-            )
+            nc.vector.tensor_tensor(woven(g), strands(slope[b], slice(0, N)), strands(dh, slice(0, N)), ALU.mult)
             return quantize(g, E5M2, "da_%d" % b)[0]
 
-        hidden(0, half(0, 0), slice(0, PACK * N))
         along_features(dy_picked[0], half(1, 0))
         group_w2(0, half(0, 1), "turn")
         dy_feat = quantize(half(1, 0), E5M2, "dy_feat_0")[0]
-        h_q, w2_q = quantize(pair[0][:], E4M3, "h_w2")
+        w2_q = quantize(half(0, 1), E4M3, "w2_0")[0]
         dh0 = hidden_gradient(0, dy_feat, w2_q)
-        interleaved(ACT.Sigmoid, -1.0, slope[0][:], planes[0])
-        slope_less_one(0)
+        finish_slope(0, "dy_2")
         da0 = first_gradient(0, dh0, half(2, 0))
+        make_silu(0, "dy_3")
+        hidden(0, half(0, 0), slice(0, N))
         along_features(dy_picked[1], half(1, 1))
-        group_w2(1, half(2, 1), "sums")
+        group_w2(1, half(0, 1), "sums")
         dy_feat = quantize(half(1, 1), E5M2, "dy_feat_1")[0]
-        w2_q = quantize(half(2, 1), E4M3, "w2_1")[0]
-        interleaved(ACT.Sigmoid, -1.0, slope[1][:], planes[1])
-        slope_less_one(1)
+        h_q, w2_q = quantize(pair[0][:], E4M3, "h_w2")
+        finish_slope(1, "w2_0")
         dh1 = hidden_gradient(1, dy_feat, w2_q)
         for b in range(EXPERTS):
             along_slots(dy_picked[b], True, half(3, b))
@@ -271,6 +271,7 @@ def tile_attend_gxfull_sil_W_kernel(tc, xT, dyT, w1, w2, ts, tx, cf, offs, out_0
         result(x_slot[0], da0, out_0[0].rearrange("(p t) f -> t p f", t=PACK), "x_2", "staged")
         g = half(0, 0)
         da1 = first_gradient(1, dh1, g)
+        make_silu(1, "w2_1")
         result(h_q, dy_slot[0], out_1[0].rearrange("(c p) e -> c p e", c=PACK), "x_3", "staged")
         result(x_slot[1], da1, out_0[1].rearrange("(p t) f -> t p f", t=PACK), "dy_0", "staged")
 
@@ -279,7 +280,7 @@ def tile_attend_gxfull_sil_W_kernel(tc, xT, dyT, w1, w2, ts, tx, cf, offs, out_0
         staged = big_tile("dy_1", "staged")
         rows = out_1[1].rearrange("(c p) e -> c p e", c=PACK)
         for c in range(PACK):
-            hidden(1, g, slice(c * N, (c + 1) * N))
+            hidden(1, g, slice(c * P, (c + 1) * P))
             nc.vector.quantize_mx(
                 out=codes[:, c * P : (c + 1) * P].bitcast(E4M3), scales=scales[:, c * P : (c + 1) * P], in_=g[:, c * N : (c + 1) * N]
             )

@@ -102,11 +102,12 @@ def tile_attend_gxfull_sil_W_kernel(tc, xT, dyT, w1, w2, ts, tx, cf, offs, out_0
                 nc.sync.dma_start(planes[t][:], src.rearrange("(p t) n -> t p n", t=PACK)[t])
 
         load_w1(0)
-        load_planes(x_plane, xT, range(PACK))
+        load_planes(x_plane, xT, (0, 1, 2, 3,))
         load_planes(dy_plane, dyT, (0,))
         load_w1(1)
-        load_planes(dy_plane, dyT, (1, 2, 3))
+        load_planes(dy_plane, dyT, (1,))
         load_w2(0)
+        load_planes(dy_plane, dyT, (2, 3,))
         load_w2(1)
 
         cf_row = held.tile([P, N], F32, name="cf_row")
@@ -132,14 +133,23 @@ def tile_attend_gxfull_sil_W_kernel(tc, xT, dyT, w1, w2, ts, tx, cf, offs, out_0
                 w1_raw[b][:].rearrange("p (j c i) -> p c j i", i=2, j=PACK),
             )
 
-        def group_w2(b, g, kind):
-            for c in range(PACK):
-                turned = bank(kind)
-                for t in range(PACK):
-                    nc.tensor.transpose(turned[:, t * P : (t + 1) * P], w2_raw[b][:, c * N + t : (c + 1) * N : PACK], ident[:])
+        def round_w2(b, rounded):
+            nc.scalar.copy(
+                rounded.rearrange("f (c u p x) -> f c p u x", c=PACK, u=2, x=2),
+                w2_raw[b][:].rearrange("f (c p u x) -> f c p u x", c=PACK, u=2, x=2),
+            )
+
+        def group_w2(rounded, g):
+            words = rounded.bitcast(F32)
+            g_words = g.bitcast(F32)
+            for side in range(2):
+                turned = bank()
+                for k in range(PACK):
+                    cols = slice((side * PACK + k) * P, (side * PACK + k + 1) * P)
+                    nc.tensor.transpose(turned[:, k * P : (k + 1) * P], words[:, cols], ident[:])
                 nc.scalar.copy(
-                    g[:, c * N : (c + 1) * N].rearrange("p (f t) -> p f t", t=PACK),
-                    turned[:].rearrange("p (t f) -> p f t", t=PACK),
+                    g_words[:, side * N : (side + 1) * N].rearrange("p (c f u) -> p c f u", c=2, u=2),
+                    turned[:].rearrange("p (c u f) -> p c f u", c=2, u=2),
                 )
 
         def gather(planes, b, picked, which):
@@ -204,66 +214,82 @@ def tile_attend_gxfull_sil_W_kernel(tc, xT, dyT, w1, w2, ts, tx, cf, offs, out_0
         for b in range(EXPERTS):
             gather(x_plane, b, x_picked[b], range(PACK))
             group_w1(b, half(b, 0))
-        txts_cols = held.tile([P, EXPERTS * PACK], F32, name="txts_cols")
+        width = EXPERTS * PACK
+        txts_cols = held.tile([P, width], F32, name="txts_cols")
+        minus_txts_cols = held.tile([P, width], F32, name="minus_txts_cols")
+        gates = held.tile([P, 2 * width], F32, name="gates")
         nc.gpsimd.tensor_tensor(txts_cols[:], tx_cols[:], ts_cols[:], ALU.mult)
-        nc.gpsimd.tensor_scalar(txts_cols[:], txts_cols[:], -1.0, 0.0, ALU.mult, ALU.add)
+        nc.gpsimd.tensor_scalar(minus_txts_cols[:], txts_cols[:], -1.0, 0.0, ALU.mult, ALU.add)
+        nc.gpsimd.tensor_scalar(gates[:, width:], ts_cols[:], 0.0, 0.0, ALU.is_equal, ALU.add)
+        nc.gpsimd.tensor_tensor(gates[:, :width], gates[:, width:], ts_cols[:], ALU.add)
+        nc.gpsimd.tensor_scalar(gates[:, width:], gates[:, :width], -1.0, 0.0, ALU.mult, ALU.add)
+        inverse = big_tile("x_3", "inverse", 2 * width)
+        nc.vector.reciprocal(inverse[:], gates[:])
 
+        for b in range(EXPERTS):
+            gather(dy_plane, b, dy_picked[b], (0,))
         z = [big_tile(slot, "z") for slot in ("tx", "ts")]
         for b in range(EXPERTS):
             along_features(x_picked[b], half(b, 1))
             w1_q, x_feat = quantize(pair[b][:], E4M3, "first_%d" % b)
-            scaled_product(x_feat, w1_q, tx_cols, b, [z[b][:, r * N : (r + 1) * N] for r in range(PACK)])
-        gather(dy_plane, 0, dy_picked[0], range(PACK))
-        gather(dy_plane, 1, dy_picked[1], range(PACK))
+            scaled_product(x_feat, w1_q, txts_cols, b, [z[b][:, r * N : (r + 1) * N] for r in range(PACK)])
+        for b in range(EXPERTS):
+            gather(dy_plane, b, dy_picked[b], range(1, PACK))
         for b in range(EXPERTS):
             along_slots(x_picked[b], False, half(2, b))
         x_slot = quantize(pair[2][:], E4M3, "x_slot")
 
-        slope = [big_tile("x_%d" % b, "slope") for b in range(EXPERTS)]
-        for b in range(EXPERTS):
-            nc.scalar.activation(slope[b][:], z[b][:], ACT.Sigmoid)
-        silu = []
+        def of_z(func, dst, b, first):
+            for r in range(PACK):
+                cols = slice(r * N, (r + 1) * N)
+                k = first + b * PACK + r
+                nc.scalar.activation(dst[:, cols], z[b][:, cols], func, scale=inverse[:, k : k + 1])
+
+        sigmoid = [big_tile("x_%d" % b, "sigmoid") for b in range(EXPERTS)]
+        rounded = [held.tile([P, PACK * N], BF16, name="rounded_%d" % b, align_bytes=64) for b in range(EXPERTS)]
+        of_z(ACT.Sigmoid, sigmoid[0], 0, 0)
+        round_w2(0, rounded[0][:])
+        of_z(ACT.Sigmoid, sigmoid[1], 1, 0)
+        slope = []
 
         def hidden(b, g, cols):
             nc.vector.tensor_tensor(
                 woven(g[:, cols.start * PACK : cols.stop * PACK]),
-                strands(silu[b], cols),
-                ts_cols[:, b * PACK : (b + 1) * PACK].unsqueeze(1).unsqueeze(3).to_broadcast([P, (cols.stop - cols.start) // 2, PACK, 2]),
+                strands(z[b], cols),
+                strands(sigmoid[b], cols),
                 ALU.mult,
             )
 
         def hidden_gradient(b, dy_feat, w2_q):
             dh = big_tile("w1_%d" % b, "dh")
-            scaled_product(dy_feat, w2_q, txts_cols, b, [dh[:, r * N : (r + 1) * N] for r in range(PACK)])
+            scaled_product(dy_feat, w2_q, minus_txts_cols, b, [dh[:, r * N : (r + 1) * N] for r in range(PACK)])
             return dh
 
         def finish_slope(b, slot):
-            mirrored = big_tile(slot, "mirrored")
-            nc.scalar.activation(mirrored[:], z[b][:], ACT.Silu, scale=-1.0)
-            nc.vector.scalar_tensor_tensor(slope[b][:], mirrored[:], 1.0, slope[b][:], ALU.subtract, ALU.mult)
-
-        def make_silu(b, slot):
-            silu.append(big_tile(slot, "silu"))
-            nc.scalar.activation(silu[b][:], z[b][:], ACT.Silu)
+            slope.append(big_tile(slot, "slope"))
+            of_z(ACT.Silu, slope[b], b, width)
+            nc.vector.scalar_tensor_tensor(slope[b][:], slope[b][:], 1.0, sigmoid[b][:], ALU.subtract, ALU.mult)
 
         def first_gradient(b, dh, g):
             nc.vector.tensor_tensor(woven(g), strands(slope[b], slice(0, N)), strands(dh, slice(0, N)), ALU.mult)
             return quantize(g, E5M2, "da_%d" % b)[0]
 
+        group_w2(rounded[0][:], half(0, 1))
+        finish_slope(0, "w2_0")
         along_features(dy_picked[0], half(1, 0))
-        group_w2(0, half(0, 1), "turn")
         dy_feat = quantize(half(1, 0), E5M2, "dy_feat_0")[0]
         w2_q = quantize(half(0, 1), E4M3, "w2_0")[0]
+        h_grouped = big.tile([P, PACK * N], BF16, name="h_grouped", tag="dy_3", align_bytes=64)
+        hidden(0, h_grouped[:], slice(0, N))
+        h_q = quantize(h_grouped[:], E4M3, "h_0")[0]
         dh0 = hidden_gradient(0, dy_feat, w2_q)
-        finish_slope(0, "dy_2")
         da0 = first_gradient(0, dh0, half(2, 0))
-        make_silu(0, "dy_3")
-        hidden(0, half(0, 0), slice(0, N))
         along_features(dy_picked[1], half(1, 1))
-        group_w2(1, half(0, 1), "sums")
+        round_w2(1, rounded[1][:])
+        group_w2(rounded[1][:], half(0, 1))
         dy_feat = quantize(half(1, 1), E5M2, "dy_feat_1")[0]
-        h_q, w2_q = quantize(pair[0][:], E4M3, "h_w2")
-        finish_slope(1, "w2_0")
+        w2_q = quantize(half(0, 1), E4M3, "w2_1")[0]
+        finish_slope(1, "dy_3")
         dh1 = hidden_gradient(1, dy_feat, w2_q)
         for b in range(EXPERTS):
             along_slots(dy_picked[b], True, half(3, b))
@@ -271,8 +297,7 @@ def tile_attend_gxfull_sil_W_kernel(tc, xT, dyT, w1, w2, ts, tx, cf, offs, out_0
         result(x_slot[0], da0, out_0[0].rearrange("(p t) f -> t p f", t=PACK), "x_2", "staged")
         g = half(0, 0)
         da1 = first_gradient(1, dh1, g)
-        make_silu(1, "w2_1")
-        result(h_q, dy_slot[0], out_1[0].rearrange("(c p) e -> c p e", c=PACK), "x_3", "staged")
+        result(h_q, dy_slot[0], out_1[0].rearrange("(c p) e -> c p e", c=PACK), "dy_2", "staged")
         result(x_slot[1], da1, out_0[1].rearrange("(p t) f -> t p f", t=PACK), "dy_0", "staged")
 
         codes = held.tile([P, N], U32, name="h_1_codes", align_bytes=64)

@@ -6,6 +6,7 @@ from concourse.masks import make_identity
 F32 = mybir.dt.float32
 BF16 = mybir.dt.bfloat16
 U32 = mybir.dt.uint32
+I32 = mybir.dt.int32
 U16 = mybir.dt.uint16
 U8 = mybir.dt.uint8
 E4M3 = mybir.dt.float8_e4m3fn_x4
@@ -71,10 +72,10 @@ def tile_attend_gxfull_sil_W_kernel(tc, xT, dyT, w1, w2, ts, tx, cf, offs, out_0
 
         ts_win = big_tile("ts", "ts_win")
         tx_win = big_tile("tx", "tx_win")
-        nc.gpsimd.memset(tx_win[0 : P - 1, :], 0.0)
         warm = held.tile([P, 1], F32, name="warm")
         nc.vector.memset(warm[:, 0:1], 0.0)
-        nc.vector.memset(ts_win[0 : P - 1, :], 0.0)
+        nc.vector.memset(tx_win[0 : P - 1, :].bitcast(I32), 0)
+        nc.vector.memset(ts_win[0 : P - 1, :].bitcast(I32), 0)
         cf_cols = held.tile([P, PACK], F32, name="cf_cols")
         nc.scalar.dma_start(tx_win[P - 1 : P, :], tx[0:1, :])
         nc.scalar.dma_start(ts_win[P - 1 : P, :], ts[0:1, :])
@@ -114,7 +115,9 @@ def tile_attend_gxfull_sil_W_kernel(tc, xT, dyT, w1, w2, ts, tx, cf, offs, out_0
         spread = bank()
         for j in range(PACK):
             nc.tensor.transpose(spread[:, j * P : (j + 1) * P], cf_cols[:, j : j + 1].to_broadcast([P, P]), ident[:])
+        minus_cf_row = held.tile([P, N], F32, name="minus_cf_row")
         nc.scalar.copy(cf_row[:].rearrange("p (m j) -> p m j", j=PACK), spread[:].rearrange("p (j m) -> p m j", j=PACK))
+        nc.scalar.activation(minus_cf_row[:], cf_row[:], ACT.Copy, scale=-1.0)
 
         def token_columns(window, name):
             picked = held.tile([P, EXPERTS * N], F32, name=name + "_picked")
@@ -159,11 +162,11 @@ def tile_attend_gxfull_sil_W_kernel(tc, xT, dyT, w1, w2, ts, tx, cf, offs, out_0
         def along_features(picked, g):
             nc.scalar.copy(
                 g.rearrange("p (r s t) -> p s t r", r=PACK, t=PACK),
-                picked[:].rearrange("p (t s r) -> p s t r", r=PACK, t=PACK),
+                picked.rearrange("p (t s r) -> p s t r", r=PACK, t=PACK),
             )
 
         def along_slots(picked, natural, g):
-            words = picked[:].bitcast(F32)
+            words = picked.bitcast(F32)
             g_words = g.bitcast(F32)
             for half in range(2):
                 turned = bank()
@@ -185,12 +188,12 @@ def tile_attend_gxfull_sil_W_kernel(tc, xT, dyT, w1, w2, ts, tx, cf, offs, out_0
                         turned[:].rearrange("s (tt v p) -> s tt p v", tt=2, v=2),
                     )
 
-        def scaled_product(stationary, moving, cols, b, dst):
+        def scaled_product(stationary, moving, row, b, dst):
             for r in range(PACK):
                 acc = bank("sums")
                 product(acc, stationary, r, moving)
                 nc.vector.scalar_tensor_tensor(
-                    dst[r], acc[:], cols[:, b * PACK + r : b * PACK + r + 1], cf_row[:], ALU.mult, ALU.mult
+                    dst[r], acc[:], txts_cols[:, b * PACK + r : b * PACK + r + 1], row[:], ALU.mult, ALU.mult
                 )
 
         def woven(dst):
@@ -209,38 +212,36 @@ def tile_attend_gxfull_sil_W_kernel(tc, xT, dyT, w1, w2, ts, tx, cf, offs, out_0
 
         tx_cols = token_columns(tx_win, "tx")
         ts_cols = token_columns(ts_win, "ts")
-        x_picked = [held.tile([P, PACK * N], BF16, name="x_picked_%d" % b, align_bytes=64) for b in range(EXPERTS)]
-        dy_picked = [held.tile([P, PACK * N], BF16, name="dy_picked_%d" % b, align_bytes=64) for b in range(EXPERTS)]
+        x_picked = [held.tile([P, PACK * N], BF16, name="x_picked_%d" % b, align_bytes=64)[:] for b in range(EXPERTS)]
+        dy_picked = [held.tile([P, PACK * N], BF16, name="dy_picked_0", align_bytes=64)[:], half(0, 0)]
         for b in range(EXPERTS):
             gather(x_plane, b, x_picked[b], range(PACK))
             group_w1(b, half(b, 0))
         width = EXPERTS * PACK
-        txts_cols = held.tile([P, width], F32, name="txts_cols")
-        minus_txts_cols = held.tile([P, width], F32, name="minus_txts_cols")
-        gates = held.tile([P, 2 * width], F32, name="gates")
-        nc.gpsimd.tensor_tensor(txts_cols[:], tx_cols[:], ts_cols[:], ALU.mult)
-        nc.gpsimd.tensor_scalar(minus_txts_cols[:], txts_cols[:], -1.0, 0.0, ALU.mult, ALU.add)
-        nc.gpsimd.tensor_scalar(gates[:, width:], ts_cols[:], 0.0, 0.0, ALU.is_equal, ALU.add)
-        nc.gpsimd.tensor_tensor(gates[:, :width], gates[:, width:], ts_cols[:], ALU.add)
-        nc.gpsimd.tensor_scalar(gates[:, width:], gates[:, :width], -1.0, 0.0, ALU.mult, ALU.add)
-        inverse = big_tile("x_3", "inverse", 2 * width)
-        nc.vector.reciprocal(inverse[:], gates[:])
+        small = big_tile("x_3", "small", 4 * width)
+        gates, txts_cols, inverse = small[:, :width], small[:, width : 2 * width], small[:, 2 * width :]
+        nc.vector.scalar_tensor_tensor(gates, ts_cols[:], 0.0, ts_cols[:], ALU.is_equal, ALU.add)
+        nc.vector.tensor_tensor(txts_cols, tx_cols[:], ts_cols[:], ALU.mult)
+        nc.vector.reciprocal(inverse[:, :width], gates)
+        nc.scalar.activation(inverse[:, width:], inverse[:, :width], ACT.Copy, scale=-1.0)
 
-        for b in range(EXPERTS):
-            gather(dy_plane, b, dy_picked[b], (0,))
         z = [big_tile(slot, "z") for slot in ("tx", "ts")]
         for b in range(EXPERTS):
             along_features(x_picked[b], half(b, 1))
-            w1_q, x_feat = quantize(pair[b][:], E4M3, "first_%d" % b)
-            scaled_product(x_feat, w1_q, txts_cols, b, [z[b][:, r * N : (r + 1) * N] for r in range(PACK)])
+            if b == 0:
+                w1_q, x_feat = quantize(pair[b][:], E4M3, "first_%d" % b)
+            else:
+                x_feat = quantize(half(b, 1), E4M3, "x_feat_%d" % b)[0]
+                w1_q = quantize(half(b, 0), E4M3, "w1_q_%d" % b)[0]
+            scaled_product(x_feat, w1_q, cf_row, b, [z[b][:, r * N : (r + 1) * N] for r in range(PACK)])
         for b in range(EXPERTS):
-            gather(dy_plane, b, dy_picked[b], range(1, PACK))
+            gather(dy_plane, b, dy_picked[b], range(PACK))
         for b in range(EXPERTS):
             along_slots(x_picked[b], False, half(2, b))
         x_slot = quantize(pair[2][:], E4M3, "x_slot")
 
-        def of_z(func, dst, b, first):
-            for r in range(PACK):
+        def of_z(func, dst, b, first, places=range(PACK)):
+            for r in places:
                 cols = slice(r * N, (r + 1) * N)
                 k = first + b * PACK + r
                 nc.scalar.activation(dst[:, cols], z[b][:, cols], func, scale=inverse[:, k : k + 1])
@@ -250,7 +251,8 @@ def tile_attend_gxfull_sil_W_kernel(tc, xT, dyT, w1, w2, ts, tx, cf, offs, out_0
         of_z(ACT.Sigmoid, sigmoid[0], 0, 0)
         round_w2(0, rounded[0][:])
         of_z(ACT.Sigmoid, sigmoid[1], 1, 0)
-        slope = []
+        mirrored = []
+        slope = pair[1][:].bitcast(F32)
 
         def hidden(b, g, cols):
             nc.vector.tensor_tensor(
@@ -261,41 +263,43 @@ def tile_attend_gxfull_sil_W_kernel(tc, xT, dyT, w1, w2, ts, tx, cf, offs, out_0
             )
 
         def hidden_gradient(b, dy_feat, w2_q):
-            dh = big_tile("w1_%d" % b, "dh")
-            scaled_product(dy_feat, w2_q, minus_txts_cols, b, [dh[:, r * N : (r + 1) * N] for r in range(PACK)])
+            dh = mirrored[b]
+            scaled_product(dy_feat, w2_q, minus_cf_row, b, [dh[:, r * N : (r + 1) * N] for r in range(PACK)])
             return dh
 
-        def finish_slope(b, slot):
-            slope.append(big_tile(slot, "slope"))
-            of_z(ACT.Silu, slope[b], b, width)
-            nc.vector.scalar_tensor_tensor(slope[b][:], slope[b][:], 1.0, sigmoid[b][:], ALU.subtract, ALU.mult)
+        def finish_slope(b, places):
+            of_z(ACT.Silu, mirrored[b], b, width, places)
+            nc.vector.scalar_tensor_tensor(slope, mirrored[b][:], 1.0, sigmoid[b][:], ALU.subtract, ALU.mult)
 
         def first_gradient(b, dh, g):
-            nc.vector.tensor_tensor(woven(g), strands(slope[b], slice(0, N)), strands(dh, slice(0, N)), ALU.mult)
+            nc.vector.tensor_tensor(woven(g), strands(slope, slice(0, N)), strands(dh, slice(0, N)), ALU.mult)
             return quantize(g, E5M2, "da_%d" % b)[0]
 
         group_w2(rounded[0][:], half(0, 1))
-        finish_slope(0, "w2_0")
+        mirrored.append(big_tile("w2_0", "mirrored"))
+        of_z(ACT.Silu, mirrored[0], 0, width, (0, 1))
         along_features(dy_picked[0], half(1, 0))
         dy_feat = quantize(half(1, 0), E5M2, "dy_feat_0")[0]
         w2_q = quantize(half(0, 1), E4M3, "w2_0")[0]
         h_grouped = big.tile([P, PACK * N], BF16, name="h_grouped", tag="dy_3", align_bytes=64)
         hidden(0, h_grouped[:], slice(0, N))
         h_q = quantize(h_grouped[:], E4M3, "h_0")[0]
+        finish_slope(0, (2, 3))
         dh0 = hidden_gradient(0, dy_feat, w2_q)
         da0 = first_gradient(0, dh0, half(2, 0))
-        along_features(dy_picked[1], half(1, 1))
+        along_features(dy_picked[1], half(2, 1))
         round_w2(1, rounded[1][:])
         group_w2(rounded[1][:], half(0, 1))
-        dy_feat = quantize(half(1, 1), E5M2, "dy_feat_1")[0]
+        dy_feat = quantize(half(2, 1), E5M2, "dy_feat_1")[0]
         w2_q = quantize(half(0, 1), E4M3, "w2_1")[0]
-        finish_slope(1, "dy_3")
+        mirrored.append(big_tile("dy_3", "mirrored"))
+        finish_slope(1, range(PACK))
         dh1 = hidden_gradient(1, dy_feat, w2_q)
         for b in range(EXPERTS):
             along_slots(dy_picked[b], True, half(3, b))
         dy_slot = quantize(pair[3][:], E5M2, "dy_slot")
         result(x_slot[0], da0, out_0[0].rearrange("(p t) f -> t p f", t=PACK), "x_2", "staged")
-        g = half(0, 0)
+        g = half(2, 0)
         da1 = first_gradient(1, dh1, g)
         result(h_q, dy_slot[0], out_1[0].rearrange("(c p) e -> c p e", c=PACK), "dy_2", "staged")
         result(x_slot[1], da1, out_0[1].rearrange("(p t) f -> t p f", t=PACK), "dy_0", "staged")

@@ -45,9 +45,10 @@ def tile_attend_gxfull_sil_W_kernel(tc, xT, dyT, w1, w2, ts, tx, cf, offs, out_0
         def half(j, k):
             return pair[j][:, k * PACK * N : (k + 1) * PACK * N]
 
-        def quantize(src, fmt, name):
+        def quantize(src, fmt, name, codes=None):
             width = src.shape[1] // PACK
-            codes = held.tile([P, width], U32, name=name + "_codes", align_bytes=64)
+            if codes is None:
+                codes = held.tile([P, width], U32, name=name + "_codes", align_bytes=64)
             scales = held.tile([P, width], U8, name=name + "_scales", align_bytes=64)
             nc.vector.quantize_mx(out=codes[:].bitcast(fmt), scales=scales[:], in_=src)
             return [(codes[:, k : k + N], scales[:, k : k + N], fmt) for k in range(0, width, N)]
@@ -137,7 +138,7 @@ def tile_attend_gxfull_sil_W_kernel(tc, xT, dyT, w1, w2, ts, tx, cf, offs, out_0
             )
 
         def round_w2(b, rounded):
-            nc.scalar.copy(
+            (nc.scalar.copy if b else nc.gpsimd.tensor_copy)(
                 rounded.rearrange("f (c u p x) -> f c p u x", c=PACK, u=2, x=2),
                 w2_raw[b][:].rearrange("f (c p u x) -> f c p u x", c=PACK, u=2, x=2),
             )
@@ -238,7 +239,8 @@ def tile_attend_gxfull_sil_W_kernel(tc, xT, dyT, w1, w2, ts, tx, cf, offs, out_0
             gather(dy_plane, b, dy_picked[b], range(PACK))
         for b in range(EXPERTS):
             along_slots(x_picked[b], False, half(2, b))
-        x_slot = quantize(pair[2][:], E4M3, "x_slot")
+        late_codes = big.tile([P, 3 * N], U32, name="late_codes", tag="dy_3", align_bytes=64)
+        x_slot = quantize(pair[2][:], E4M3, "x_slot", late_codes[:, : 2 * N])
 
         def of_z(func, dst, b, first, places=range(PACK)):
             for r in places:
@@ -249,7 +251,7 @@ def tile_attend_gxfull_sil_W_kernel(tc, xT, dyT, w1, w2, ts, tx, cf, offs, out_0
         sigmoid = [big_tile("x_%d" % b, "sigmoid") for b in range(EXPERTS)]
         rounded = [held.tile([P, PACK * N], BF16, name="rounded_%d" % b, align_bytes=64) for b in range(EXPERTS)]
         of_z(ACT.Sigmoid, sigmoid[0], 0, 0)
-        round_w2(0, rounded[0][:])
+        round_w2(0, half(1, 0))
         of_z(ACT.Sigmoid, sigmoid[1], 1, 0)
         mirrored = []
         slope = pair[1][:].bitcast(F32)
@@ -275,15 +277,17 @@ def tile_attend_gxfull_sil_W_kernel(tc, xT, dyT, w1, w2, ts, tx, cf, offs, out_0
             nc.vector.tensor_tensor(woven(g), strands(slope, slice(0, N)), strands(dh, slice(0, N)), ALU.mult)
             return quantize(g, E5M2, "da_%d" % b)[0]
 
-        group_w2(rounded[0][:], half(0, 1))
+        group_w2(half(1, 0), half(0, 1))
         mirrored.append(big_tile("w2_0", "mirrored"))
         of_z(ACT.Silu, mirrored[0], 0, width, (0, 1))
-        along_features(dy_picked[0], half(1, 0))
-        dy_feat = quantize(half(1, 0), E5M2, "dy_feat_0")[0]
-        w2_q = quantize(half(0, 1), E4M3, "w2_0")[0]
-        h_grouped = big.tile([P, PACK * N], BF16, name="h_grouped", tag="dy_3", align_bytes=64)
-        hidden(0, h_grouped[:], slice(0, N))
-        h_q = quantize(h_grouped[:], E4M3, "h_0")[0]
+        along_features(dy_picked[0], half(1, 1))
+        dy_feat = quantize(half(1, 1), E5M2, "dy_feat_0")[0]
+        w2_q = quantize(half(0, 1), E4M3, "w2_0", late_codes[:, 2 * N :])[0]
+        nc.gpsimd.tensor_tensor(rounded[0][:], z[0][:], sigmoid[0][:], ALU.mult)
+        nc.gpsimd.tensor_copy(
+            rounded[1][:].rearrange("p (n r) -> p n r", r=PACK), rounded[0][:].rearrange("p (r n) -> p n r", r=PACK)
+        )
+        h_q = quantize(rounded[1][:], E4M3, "h_0")[0]
         finish_slope(0, (2, 3))
         dh0 = hidden_gradient(0, dy_feat, w2_q)
         da0 = first_gradient(0, dh0, half(2, 0))
@@ -292,7 +296,7 @@ def tile_attend_gxfull_sil_W_kernel(tc, xT, dyT, w1, w2, ts, tx, cf, offs, out_0
         group_w2(rounded[1][:], half(0, 1))
         dy_feat = quantize(half(2, 1), E5M2, "dy_feat_1")[0]
         w2_q = quantize(half(0, 1), E4M3, "w2_1")[0]
-        mirrored.append(big_tile("dy_3", "mirrored"))
+        mirrored.append(big_tile("w2_1", "mirrored"))
         finish_slope(1, range(PACK))
         dh1 = hidden_gradient(1, dy_feat, w2_q)
         for b in range(EXPERTS):

@@ -91,26 +91,130 @@ def tile_attend_gxfull_sil_W_kernel(tc, xT, dyT, w1, w2, ts, tx, cf, offs, out_0
         x_plane = [big_tile("x_%d" % t, "x_plane") for t in range(PACK)]
         dy_plane = [big_tile("dy_%d" % t, "dy_plane") for t in range(PACK)]
 
-        def load_w1(b):
+        for t in range(PACK):
+            nc.sync.dma_start(x_plane[t][:], xT.rearrange("(p t) n -> t p n", t=PACK)[t])
+        for b in range(EXPERTS):
             nc.sync.dma_start(w1_raw[b][:], w1[b].rearrange("(p j) f -> p (j f)", j=PACK))
-
-        def load_w2(b):
+        for t in range(PACK):
+            nc.sync.dma_start(dy_plane[t][:], dyT.rearrange("(p t) n -> t p n", t=PACK)[t])
+        for b in range(EXPERTS):
             nc.sync.dma_start(
                 w2_raw[b][:].rearrange("p (c e) -> p c e", c=PACK), w2[b].rearrange("(c p) e -> p c e", c=PACK)
             )
 
-        def load_planes(planes, src, which):
-            for t in which:
-                nc.sync.dma_start(planes[t][:], src.rearrange("(p t) n -> t p n", t=PACK)[t])
+        vector_copy, scalar_copy = nc.vector.tensor_copy, nc.scalar.copy
 
-        load_w1(0)
-        load_planes(x_plane, xT, (0, 1, 2, 3,))
-        load_planes(dy_plane, dyT, (0,))
-        load_w1(1)
-        load_planes(dy_plane, dyT, (1,))
-        load_w2(0)
-        load_planes(dy_plane, dyT, (2, 3,))
-        load_w2(1)
+        def scalar_gather(dst, src):
+            nc.scalar.activation(dst, src, ACT.Copy)
+
+        def grouped(name):
+            return held.tile([P, PACK * N], BF16, name=name, align_bytes=64)[:]
+
+        def token_columns(window, name):
+            picked = held.tile([P, EXPERTS * N], F32, name=name + "_picked")
+            scalar_gather(picked[:], window[:].indirect(offsets[:]))
+            cols = held.tile([P, EXPERTS * PACK], F32, name=name + "_cols")
+            for b in range(EXPERTS):
+                turned = bank()
+                for r in range(PACK):
+                    nc.tensor.transpose(turned[:, r * P : (r + 1) * P], picked[:, b * N + r : (b + 1) * N : PACK], ident[:])
+                nc.scalar.copy(cols[:, b * PACK : (b + 1) * PACK], turned[:, P - 1 : N : P])
+            return cols
+
+        def group_w1(copy, b, g):
+            copy(
+                g.rearrange("p (c i j) -> p c j i", i=2, j=PACK),
+                w1_raw[b][:].rearrange("p (j c i) -> p c j i", i=2, j=PACK),
+            )
+
+        def round_w2(copy, b, rounded):
+            copy(
+                rounded.rearrange("f (c u p x) -> f c p u x", c=PACK, u=2, x=2),
+                w2_raw[b][:].rearrange("f (c p u x) -> f c p u x", c=PACK, u=2, x=2),
+            )
+
+        def group_w2(copy, rounded, g):
+            words = rounded.bitcast(F32)
+            g_words = g.bitcast(F32)
+            for side in range(2):
+                turned = bank()
+                for k in range(PACK):
+                    cols = slice((side * PACK + k) * P, (side * PACK + k + 1) * P)
+                    nc.tensor.transpose(turned[:, k * P : (k + 1) * P], words[:, cols], ident[:])
+                copy(
+                    g_words[:, side * N : (side + 1) * N].rearrange("p (c f u) -> p c f u", c=2, u=2),
+                    turned[:].rearrange("p (c u f) -> p c f u", c=2, u=2),
+                )
+
+        def gather(copy, planes, picked, t, b):
+            copy(picked[b][:, t * N : (t + 1) * N], listed(planes[t], b))
+
+        def along_features(copy, picked, g):
+            copy(
+                g.rearrange("p (r s t) -> p s t r", r=PACK, t=PACK),
+                picked.rearrange("p (t s r) -> p s t r", r=PACK, t=PACK),
+            )
+
+        def along_slots(copy, picked, natural, g, side):
+            words = picked.bitcast(F32)
+            g_words = g.bitcast(F32)
+            turned = bank()
+            for tt in range(2):
+                for v in range(2):
+                    t = 2 * side + tt
+                    k = 2 * tt + v
+                    nc.tensor.transpose(
+                        turned[:, k * P : (k + 1) * P], words[:, t * 256 + v : (t + 1) * 256 : 2], ident[:]
+                    )
+            if natural:
+                copy(
+                    g_words.rearrange("s (p h k) -> s h p k", h=2, k=4)[:, side],
+                    turned[:].rearrange("s (k p) -> s p k", k=4),
+                )
+            else:
+                copy(
+                    g_words[:, side * N : (side + 1) * N].rearrange("s (tt p v) -> s tt p v", tt=2, v=2),
+                    turned[:].rearrange("s (tt v p) -> s tt p v", tt=2, v=2),
+                )
+
+        def scaled_product(stationary, moving, row, b, dst):
+            for r in range(PACK):
+                acc = bank("sums")
+                product(acc, stationary, r, moving)
+                nc.vector.scalar_tensor_tensor(
+                    dst[:, r * N : (r + 1) * N], acc[:], txts_cols[:, b * PACK + r : b * PACK + r + 1], row[:], ALU.mult, ALU.mult
+                )
+
+        def woven(dst):
+            return dst.rearrange("p (c i r) -> p c r i", i=2, r=PACK)
+
+        def strands(src, cols):
+            return src[:].rearrange("p (r n) -> p r n", r=PACK)[:, :, cols].rearrange("p r (c i) -> p c r i", i=2)
+
+        def woven_product(g, left, right, cols=slice(0, N)):
+            nc.vector.tensor_tensor(
+                woven(g[:, cols.start * PACK : cols.stop * PACK]), strands(left, cols), strands(right, cols), ALU.mult
+            )
+
+        def result(copies, stationary, moving, rows, slot, kind):
+            staged = big_tile(slot, "staged")
+            for j in range(PACK):
+                acc = bank(kind)
+                product(acc, stationary, j, moving)
+                copies[j](staged[:, j * N : (j + 1) * N], acc[:])
+                nc.sync.dma_start(rows[j], staged[:, j * N : (j + 1) * N])
+
+        def of_z(func, dst, b, first):
+            for r in range(PACK):
+                cols = slice(r * N, (r + 1) * N)
+                k = first + b * PACK + r
+                nc.scalar.activation(dst[:, cols], z[b][:, cols], func, scale=inverse[:, k : k + 1])
+
+        def slope_of(b):
+            nc.vector.scalar_tensor_tensor(mirrored[b][:], mirrored[b][:], 1.0, sigmoid[b][:], ALU.subtract, ALU.mult)
+
+        tx_cols = token_columns(tx_win, "tx")
+        ts_cols = token_columns(ts_win, "ts")
 
         cf_row = held.tile([P, N], F32, name="cf_row")
         spread = bank()
@@ -120,106 +224,18 @@ def tile_attend_gxfull_sil_W_kernel(tc, xT, dyT, w1, w2, ts, tx, cf, offs, out_0
         nc.scalar.copy(cf_row[:].rearrange("p (m j) -> p m j", j=PACK), spread[:].rearrange("p (j m) -> p m j", j=PACK))
         nc.scalar.activation(minus_cf_row[:], cf_row[:], ACT.Copy, scale=-1.0)
 
-        def token_columns(window, name):
-            picked = held.tile([P, EXPERTS * N], F32, name=name + "_picked")
-            nc.vector.tensor_copy(picked[:], window[:].indirect(offsets[:]))
-            cols = held.tile([P, EXPERTS * PACK], F32, name=name + "_cols")
+        x_picked = [grouped("x_picked_%d" % b) for b in range(EXPERTS)]
+        dy_picked = [grouped("dy_picked_%d" % b) for b in range(EXPERTS)]
+        for t in range(PACK - 1):
             for b in range(EXPERTS):
-                turned = bank()
-                for r in range(PACK):
-                    nc.tensor.transpose(turned[:, r * P : (r + 1) * P], picked[:, b * N + r : (b + 1) * N : PACK], ident[:])
-                nc.scalar.copy(cols[:, b * PACK : (b + 1) * PACK], turned[:, P - 1 : N : P])
-            return cols
-
-        def group_w1(b, g):
-            nc.scalar.copy(
-                g.rearrange("p (c i j) -> p c j i", i=2, j=PACK),
-                w1_raw[b][:].rearrange("p (j c i) -> p c j i", i=2, j=PACK),
-            )
-
-        def round_w2(b, rounded):
-            (nc.scalar.copy if b else nc.gpsimd.tensor_copy)(
-                rounded.rearrange("f (c u p x) -> f c p u x", c=PACK, u=2, x=2),
-                w2_raw[b][:].rearrange("f (c p u x) -> f c p u x", c=PACK, u=2, x=2),
-            )
-
-        def group_w2(rounded, g):
-            words = rounded.bitcast(F32)
-            g_words = g.bitcast(F32)
-            for side in range(2):
-                turned = bank()
-                for k in range(PACK):
-                    cols = slice((side * PACK + k) * P, (side * PACK + k + 1) * P)
-                    nc.tensor.transpose(turned[:, k * P : (k + 1) * P], words[:, cols], ident[:])
-                nc.scalar.copy(
-                    g_words[:, side * N : (side + 1) * N].rearrange("p (c f u) -> p c f u", c=2, u=2),
-                    turned[:].rearrange("p (c u f) -> p c f u", c=2, u=2),
-                )
-
-        def gather(planes, b, picked, which):
-            for t in which:
-                nc.vector.tensor_copy(picked[:, t * N : (t + 1) * N], listed(planes[t], b))
-
-        def along_features(picked, g):
-            nc.scalar.copy(
-                g.rearrange("p (r s t) -> p s t r", r=PACK, t=PACK),
-                picked.rearrange("p (t s r) -> p s t r", r=PACK, t=PACK),
-            )
-
-        def along_slots(picked, natural, g):
-            words = picked.bitcast(F32)
-            g_words = g.bitcast(F32)
-            for half in range(2):
-                turned = bank()
-                for tt in range(2):
-                    for v in range(2):
-                        t = 2 * half + tt
-                        k = 2 * tt + v
-                        nc.tensor.transpose(
-                            turned[:, k * P : (k + 1) * P], words[:, t * 256 + v : (t + 1) * 256 : 2], ident[:]
-                        )
-                if natural:
-                    nc.scalar.copy(
-                        g_words.rearrange("s (p h k) -> s h p k", h=2, k=4)[:, half],
-                        turned[:].rearrange("s (k p) -> s p k", k=4),
-                    )
-                else:
-                    nc.scalar.copy(
-                        g_words[:, half * N : (half + 1) * N].rearrange("s (tt p v) -> s tt p v", tt=2, v=2),
-                        turned[:].rearrange("s (tt v p) -> s tt p v", tt=2, v=2),
-                    )
-
-        def scaled_product(stationary, moving, row, b, dst):
-            for r in range(PACK):
-                acc = bank("sums")
-                product(acc, stationary, r, moving)
-                nc.vector.scalar_tensor_tensor(
-                    dst[r], acc[:], txts_cols[:, b * PACK + r : b * PACK + r + 1], row[:], ALU.mult, ALU.mult
-                )
-
-        def woven(dst):
-            return dst.rearrange("p (c i r) -> p c r i", i=2, r=PACK)
-
-        def strands(src, cols):
-            return src[:].rearrange("p (r n) -> p r n", r=PACK)[:, :, cols].rearrange("p r (c i) -> p c r i", i=2)
-
-        def result(stationary, moving, rows, slot, name):
-            staged = big_tile(slot, name)
-            for j in range(PACK):
-                acc = bank("turn")
-                product(acc, stationary, j, moving)
-                nc.scalar.copy(staged[:, j * N : (j + 1) * N], acc[:])
-                nc.sync.dma_start(rows[j], staged[:, j * N : (j + 1) * N])
-
-        tx_cols = token_columns(tx_win, "tx")
-        ts_cols = token_columns(ts_win, "ts")
-        x_picked = [held.tile([P, PACK * N], BF16, name="x_picked_%d" % b, align_bytes=64)[:] for b in range(EXPERTS)]
-        dy_picked = [held.tile([P, PACK * N], BF16, name="dy_picked_0", align_bytes=64)[:], half(0, 0)]
+                gather(vector_copy, x_plane, x_picked, t, b)
         for b in range(EXPERTS):
-            gather(x_plane, b, x_picked[b], range(PACK))
-            group_w1(b, half(b, 0))
+            along_slots(scalar_copy, x_picked[b], False, half(2, b), 0)
+        gather(vector_copy, x_plane, x_picked, 3, 0)
+        gather(scalar_gather, x_plane, x_picked, 3, 1)
+
         width = EXPERTS * PACK
-        small = big_tile("x_3", "small", 4 * width)
+        small = held.tile([P, 4 * width], F32, name="small")
         gates, txts_cols, inverse = small[:, :width], small[:, width : 2 * width], small[:, 2 * width :]
         nc.vector.scalar_tensor_tensor(gates, ts_cols[:], 0.0, ts_cols[:], ALU.is_equal, ALU.add)
         nc.vector.tensor_tensor(txts_cols, tx_cols[:], ts_cols[:], ALU.mult)
@@ -227,101 +243,73 @@ def tile_attend_gxfull_sil_W_kernel(tc, xT, dyT, w1, w2, ts, tx, cf, offs, out_0
         nc.scalar.activation(inverse[:, width:], inverse[:, :width], ACT.Copy, scale=-1.0)
 
         z = [big_tile(slot, "z") for slot in ("tx", "ts")]
+        along_features(vector_copy, x_picked[0], half(0, 1))
+        along_features(scalar_copy, x_picked[1], half(1, 1))
+        group_w1(vector_copy, 0, half(0, 0))
+        x_feat = [quantize(half(0, 1), E4M3, "x_feat_0")[0]]
+        w1_q = [quantize(half(0, 0), E4M3, "w1_q_0")[0]]
+        x_feat.append(quantize(half(1, 1), E4M3, "x_feat_1")[0])
+        group_w1(scalar_copy, 1, half(1, 0))
+        scaled_product(x_feat[0], w1_q[0], cf_row, 0, z[0])
+        w1_q.append(quantize(half(1, 0), E4M3, "w1_q_1")[0])
         for b in range(EXPERTS):
-            along_features(x_picked[b], half(b, 1))
-            if b == 0:
-                w1_q, x_feat = quantize(pair[b][:], E4M3, "first_%d" % b)
-            else:
-                x_feat = quantize(half(b, 1), E4M3, "x_feat_%d" % b)[0]
-                w1_q = quantize(half(b, 0), E4M3, "w1_q_%d" % b)[0]
-            scaled_product(x_feat, w1_q, cf_row, b, [z[b][:, r * N : (r + 1) * N] for r in range(PACK)])
+            along_slots(scalar_copy, x_picked[b], False, half(2, b), 1)
         for b in range(EXPERTS):
-            gather(dy_plane, b, dy_picked[b], range(PACK))
-        for b in range(EXPERTS):
-            along_slots(x_picked[b], False, half(2, b))
-        late_codes = big.tile([P, 3 * N], U32, name="late_codes", tag="dy_3", align_bytes=64)
-        x_slot = quantize(pair[2][:], E4M3, "x_slot", late_codes[:, : 2 * N])
-
-        def of_z(func, dst, b, first, places=range(PACK)):
-            for r in places:
-                cols = slice(r * N, (r + 1) * N)
-                k = first + b * PACK + r
-                nc.scalar.activation(dst[:, cols], z[b][:, cols], func, scale=inverse[:, k : k + 1])
+            gather(scalar_gather, dy_plane, dy_picked, 0, b)
+        scaled_product(x_feat[1], w1_q[1], cf_row, 1, z[1])
+        x_slot = quantize(pair[2][:], E4M3, "x_slot")
 
         sigmoid = [big_tile("x_%d" % b, "sigmoid") for b in range(EXPERTS)]
-        rounded = [held.tile([P, PACK * N], BF16, name="rounded_%d" % b, align_bytes=64) for b in range(EXPERTS)]
+        mirrored = [big_tile("x_%d" % (2 + b), "mirrored") for b in range(EXPERTS)]
         of_z(ACT.Sigmoid, sigmoid[0], 0, 0)
-        round_w2(0, half(1, 0))
-        of_z(ACT.Sigmoid, sigmoid[1], 1, 0)
-        mirrored = []
-        slope = pair[1][:].bitcast(F32)
-
-        def hidden(b, g, cols):
-            nc.vector.tensor_tensor(
-                woven(g[:, cols.start * PACK : cols.stop * PACK]),
-                strands(z[b], cols),
-                strands(sigmoid[b], cols),
-                ALU.mult,
-            )
-
-        def hidden_gradient(b, dy_feat, w2_q):
-            dh = mirrored[b]
-            scaled_product(dy_feat, w2_q, minus_cf_row, b, [dh[:, r * N : (r + 1) * N] for r in range(PACK)])
-            return dh
-
-        def finish_slope(b, places):
-            of_z(ACT.Silu, mirrored[b], b, width, places)
-            nc.vector.scalar_tensor_tensor(slope, mirrored[b][:], 1.0, sigmoid[b][:], ALU.subtract, ALU.mult)
-
-        def first_gradient(b, dh, g):
-            nc.vector.tensor_tensor(woven(g), strands(slope, slice(0, N)), strands(dh, slice(0, N)), ALU.mult)
-            return quantize(g, E5M2, "da_%d" % b)[0]
-
-        group_w2(half(1, 0), half(0, 1))
-        mirrored.append(big_tile("w2_0", "mirrored"))
-        of_z(ACT.Silu, mirrored[0], 0, width, (0, 1))
-        along_features(dy_picked[0], half(1, 1))
-        dy_feat = quantize(half(1, 1), E5M2, "dy_feat_0")[0]
-        w2_q = quantize(half(0, 1), E4M3, "w2_0", late_codes[:, 2 * N :])[0]
-        nc.gpsimd.tensor_tensor(rounded[0][:], z[0][:], sigmoid[0][:], ALU.mult)
-        nc.gpsimd.tensor_copy(
-            rounded[1][:].rearrange("p (n r) -> p n r", r=PACK), rounded[0][:].rearrange("p (r n) -> p n r", r=PACK)
-        )
-        h_q = quantize(rounded[1][:], E4M3, "h_0")[0]
-        finish_slope(0, (2, 3))
-        dh0 = hidden_gradient(0, dy_feat, w2_q)
-        da0 = first_gradient(0, dh0, half(2, 0))
-        along_features(dy_picked[1], half(2, 1))
-        round_w2(1, rounded[1][:])
-        group_w2(rounded[1][:], half(0, 1))
-        dy_feat = quantize(half(2, 1), E5M2, "dy_feat_1")[0]
-        w2_q = quantize(half(0, 1), E4M3, "w2_1")[0]
-        mirrored.append(big_tile("w2_1", "mirrored"))
-        finish_slope(1, range(PACK))
-        dh1 = hidden_gradient(1, dy_feat, w2_q)
         for b in range(EXPERTS):
-            along_slots(dy_picked[b], True, half(3, b))
-        dy_slot = quantize(pair[3][:], E5M2, "dy_slot")
-        result(x_slot[0], da0, out_0[0].rearrange("(p t) f -> t p f", t=PACK), "x_2", "staged")
-        g = half(2, 0)
-        da1 = first_gradient(1, dh1, g)
-        result(h_q, dy_slot[0], out_1[0].rearrange("(c p) e -> c p e", c=PACK), "dy_2", "staged")
-        result(x_slot[1], da1, out_0[1].rearrange("(p t) f -> t p f", t=PACK), "dy_0", "staged")
+            gather(scalar_gather, dy_plane, dy_picked, 1, b)
+        of_z(ACT.Sigmoid, sigmoid[1], 1, 0)
+        woven_product(half(0, 1), z[0], sigmoid[0])
+        for t in (2, 3):
+            for b in range(EXPERTS):
+                gather(vector_copy, dy_plane, dy_picked, t, b)
+        h_q = [quantize(half(0, 1), E4M3, "h_0")[0]]
+        of_z(ACT.Silu, mirrored[0], 0, width)
+        along_features(vector_copy, dy_picked[0], half(0, 0))
+        round_w2(vector_copy, 0, x_picked[0])
+        dy_feat = [quantize(half(0, 0), E5M2, "dy_feat_0")[0]]
+        w2_grouped = [grouped("w2_grouped_%d" % b) for b in range(EXPERTS)]
+        group_w2(scalar_copy, x_picked[0], w2_grouped[0])
+        slope_of(0)
+        w2_q = [quantize(w2_grouped[0], E4M3, "w2_0")[0]]
+        for side in range(2):
+            along_slots(scalar_copy, dy_picked[0], True, half(3, 0), side)
+        of_z(ACT.Silu, mirrored[1], 1, width)
+        dh = [big_tile("w1_%d" % b, "dh") for b in range(EXPERTS)]
+        scaled_product(dy_feat[0], w2_q[0], minus_cf_row, 0, dh[0])
+        dy_slot = [quantize(half(3, 0), E5M2, "dy_slot_0")[0]]
+        woven_product(half(2, 0), mirrored[0], dh[0])
+        along_features(scalar_copy, dy_picked[1], half(1, 0))
+        round_w2(scalar_copy, 1, x_picked[1])
+        group_w2(scalar_copy, x_picked[1], w2_grouped[1])
+        slope_of(1)
+        da = [quantize(half(2, 0), E5M2, "da_0")[0]]
+        dy_feat.append(quantize(half(1, 0), E5M2, "dy_feat_1")[0])
+        w2_q.append(quantize(w2_grouped[1], E4M3, "w2_1")[0])
+        for side in range(2):
+            along_slots(scalar_copy, dy_picked[1], True, half(3, 1), side)
+        scaled_product(dy_feat[1], w2_q[1], minus_cf_row, 1, dh[1])
+        result([scalar_copy] * PACK, h_q[0], dy_slot[0], out_1[0].rearrange("(c p) e -> c p e", c=PACK), "dy_0", "turn")
+        result([scalar_copy] * PACK, x_slot[0], da[0], out_0[0].rearrange("(p t) f -> t p f", t=PACK), "dy_1", "turn")
+        woven_product(half(2, 1), mirrored[1], dh[1])
+        dy_slot.append(quantize(half(3, 1), E5M2, "dy_slot_1")[0])
+        da.append(quantize(half(2, 1), E5M2, "da_1")[0])
+        result([scalar_copy] * PACK, x_slot[1], da[1], out_0[1].rearrange("(p t) f -> t p f", t=PACK), "dy_2", "turn")
 
+        g = half(1, 1)
         codes = held.tile([P, N], U32, name="h_1_codes", align_bytes=64)
         scales = held.tile([P, N], U8, name="h_1_scales", align_bytes=64)
-        staged = big_tile("dy_1", "staged")
-        rows = out_1[1].rearrange("(c p) e -> c p e", c=PACK)
         for c in range(PACK):
-            hidden(1, g, slice(c * P, (c + 1) * P))
+            woven_product(g, z[1], sigmoid[1], slice(c * P, (c + 1) * P))
             nc.vector.quantize_mx(
                 out=codes[:, c * P : (c + 1) * P].bitcast(E4M3), scales=scales[:, c * P : (c + 1) * P], in_=g[:, c * N : (c + 1) * N]
             )
-        for c in range(PACK):
-            acc = bank("sums")
-            product(acc, (codes, scales, E4M3), c, dy_slot[1])
-            if c % 2:
-                nc.scalar.copy(staged[:, c * N : (c + 1) * N], acc[:])
-            else:
-                nc.vector.tensor_copy(staged[:, c * N : (c + 1) * N], acc[:])
-            nc.sync.dma_start(rows[c], staged[:, c * N : (c + 1) * N])
+        result(
+            [vector_copy, scalar_copy] * 2, (codes, scales, E4M3), dy_slot[1], out_1[1].rearrange("(c p) e -> c p e", c=PACK), "dy_3", "sums"
+        )

@@ -32,15 +32,8 @@ def tile_attend_gxfull_sil_W_kernel(tc, xT, dyT, w1, w2, ts, tx, cf, offs, out_0
         def big_tile(slot, name, width=PACK * N):
             return big.tile([P, width], F32, name=name, tag=slot, align_bytes=64)
 
-        bank_tiles = {
-            kind: [psum.tile([P, N], F32, name="%s_%d" % (kind, j)) for j in range(4)] for kind in ("turn", "sums")
-        }
+        bank = [psum.tile([P, N], F32, name="bank_%d" % j) for j in range(8)]
         pair = [held.tile([P, 2 * PACK * N], BF16, name="pair_%d" % j, align_bytes=64) for j in range(4)]
-        taken = []
-
-        def bank(kind="turn"):
-            taken.append(kind)
-            return bank_tiles[kind][(taken.count(kind) - 1) % 4]
 
         def half(j, k):
             return pair[j][:, k * PACK * N : (k + 1) * PACK * N]
@@ -95,14 +88,20 @@ def tile_attend_gxfull_sil_W_kernel(tc, xT, dyT, w1, w2, ts, tx, cf, offs, out_0
             nc.sync.dma_start(x_plane[t][:], xT.rearrange("(p t) n -> t p n", t=PACK)[t])
         for b in range(EXPERTS):
             nc.sync.dma_start(w1_raw[b][:], w1[b].rearrange("(p j) f -> p (j f)", j=PACK))
-        for t in range(PACK):
+        def load_dy(t):
             nc.sync.dma_start(dy_plane[t][:], dyT.rearrange("(p t) n -> t p n", t=PACK)[t])
-        for b in range(EXPERTS):
+
+        def load_w2(b):
             nc.sync.dma_start(
                 w2_raw[b][:].rearrange("p (c e) -> p c e", c=PACK), w2[b].rearrange("(c p) e -> p c e", c=PACK)
             )
 
-        vector_copy, scalar_copy = nc.vector.tensor_copy, nc.scalar.copy
+        load_w2(0)
+        for t in range(PACK):
+            load_dy(t)
+        load_w2(1)
+
+        vector_copy, scalar_copy, gpsimd_copy = nc.vector.tensor_copy, nc.scalar.copy, nc.gpsimd.tensor_copy
 
         def scalar_gather(dst, src):
             nc.scalar.activation(dst, src, ACT.Copy)
@@ -110,16 +109,21 @@ def tile_attend_gxfull_sil_W_kernel(tc, xT, dyT, w1, w2, ts, tx, cf, offs, out_0
         def grouped(name):
             return held.tile([P, PACK * N], BF16, name=name, align_bytes=64)[:]
 
-        def token_columns(window, name):
+        def gather_tokens(window, name):
             picked = held.tile([P, EXPERTS * N], F32, name=name + "_picked")
             scalar_gather(picked[:], window[:].indirect(offsets[:]))
-            cols = held.tile([P, EXPERTS * PACK], F32, name=name + "_cols")
+            return picked
+
+        def turn_tokens(picked, banks):
             for b in range(EXPERTS):
-                turned = bank()
                 for r in range(PACK):
-                    nc.tensor.transpose(turned[:, r * P : (r + 1) * P], picked[:, b * N + r : (b + 1) * N : PACK], ident[:])
-                nc.scalar.copy(cols[:, b * PACK : (b + 1) * PACK], turned[:, P - 1 : N : P])
-            return cols
+                    nc.tensor.transpose(
+                        bank[banks[b]][:, r * P : (r + 1) * P], picked[:, b * N + r : (b + 1) * N : PACK], ident[:]
+                    )
+
+        def token_columns(cols, banks):
+            for b in range(EXPERTS):
+                nc.scalar.copy(cols[:, b * PACK : (b + 1) * PACK], bank[banks[b]][:, P - 1 : N : P])
 
         def group_w1(copy, b, g):
             copy(
@@ -133,11 +137,11 @@ def tile_attend_gxfull_sil_W_kernel(tc, xT, dyT, w1, w2, ts, tx, cf, offs, out_0
                 w2_raw[b][:].rearrange("f (c p u x) -> f c p u x", c=PACK, u=2, x=2),
             )
 
-        def group_w2(copy, rounded, g):
+        def group_w2(copy, rounded, g, banks):
             words = rounded.bitcast(F32)
             g_words = g.bitcast(F32)
             for side in range(2):
-                turned = bank()
+                turned = bank[banks[side]]
                 for k in range(PACK):
                     cols = slice((side * PACK + k) * P, (side * PACK + k + 1) * P)
                     nc.tensor.transpose(turned[:, k * P : (k + 1) * P], words[:, cols], ident[:])
@@ -147,42 +151,41 @@ def tile_attend_gxfull_sil_W_kernel(tc, xT, dyT, w1, w2, ts, tx, cf, offs, out_0
                 )
 
         def gather(copy, planes, picked, t, b):
-            copy(picked[b][:, t * N : (t + 1) * N], listed(planes[t], b))
+            copy(picked[b][:, t], listed(planes[t], b))
 
         def along_features(copy, picked, g):
-            copy(
-                g.rearrange("p (r s t) -> p s t r", r=PACK, t=PACK),
-                picked.rearrange("p (t s r) -> p s t r", r=PACK, t=PACK),
+            copy(g.rearrange("p (r s t) -> p s t r", r=PACK, t=PACK), picked.rearrange("p t (s r) -> p s t r", r=PACK))
+
+        def x_along_slots(t, which):
+            words = x_both[:, t].bitcast(F32)
+            turned = bank[which]
+            for b in range(EXPERTS):
+                for v in range(2):
+                    k = 2 * b + v
+                    nc.tensor.transpose(turned[:, k * P : (k + 1) * P], words[:, b * 256 + v : (b + 1) * 256 : 2], ident[:])
+            nc.scalar.copy(
+                pair[2][:].bitcast(F32).rearrange("s (b t p v) -> s t b p v", b=EXPERTS, t=PACK, v=2)[:, t],
+                turned[:].rearrange("s (b v p) -> s b p v", b=EXPERTS, v=2),
             )
 
-        def along_slots(copy, picked, natural, g, side):
-            words = picked.bitcast(F32)
-            g_words = g.bitcast(F32)
-            turned = bank()
+        def dy_along_slots(copy, picked, g, side, which):
+            turned = bank[which]
             for tt in range(2):
+                words = picked[:, 2 * side + tt].bitcast(F32)
                 for v in range(2):
-                    t = 2 * side + tt
                     k = 2 * tt + v
-                    nc.tensor.transpose(
-                        turned[:, k * P : (k + 1) * P], words[:, t * 256 + v : (t + 1) * 256 : 2], ident[:]
-                    )
-            if natural:
-                copy(
-                    g_words.rearrange("s (p h k) -> s h p k", h=2, k=4)[:, side],
-                    turned[:].rearrange("s (k p) -> s p k", k=4),
-                )
-            else:
-                copy(
-                    g_words[:, side * N : (side + 1) * N].rearrange("s (tt p v) -> s tt p v", tt=2, v=2),
-                    turned[:].rearrange("s (tt v p) -> s tt p v", tt=2, v=2),
-                )
+                    nc.tensor.transpose(turned[:, k * P : (k + 1) * P], words[:, v::2], ident[:])
+            copy(
+                g.bitcast(F32).rearrange("s (p h k) -> s h p k", h=2, k=4)[:, side],
+                turned[:].rearrange("s (k p) -> s p k", k=4),
+            )
 
-        def scaled_product(stationary, moving, row, b, dst):
+        def scaled_product(stationary, moving, cols, b, dst, first):
             for r in range(PACK):
-                acc = bank("sums")
+                acc = bank[first + r]
                 product(acc, stationary, r, moving)
                 nc.vector.scalar_tensor_tensor(
-                    dst[:, r * N : (r + 1) * N], acc[:], txts_cols[:, b * PACK + r : b * PACK + r + 1], row[:], ALU.mult, ALU.mult
+                    dst[:, r * N : (r + 1) * N], acc[:], cols[:, b * PACK + r : b * PACK + r + 1], cf_row[:], ALU.mult, ALU.mult
                 )
 
         def woven(dst):
@@ -191,125 +194,156 @@ def tile_attend_gxfull_sil_W_kernel(tc, xT, dyT, w1, w2, ts, tx, cf, offs, out_0
         def strands(src, cols):
             return src[:].rearrange("p (r n) -> p r n", r=PACK)[:, :, cols].rearrange("p r (c i) -> p c r i", i=2)
 
-        def woven_product(g, left, right, cols=slice(0, N)):
-            nc.vector.tensor_tensor(
-                woven(g[:, cols.start * PACK : cols.stop * PACK]), strands(left, cols), strands(right, cols), ALU.mult
-            )
+        def woven_product(g, left, right, cols=slice(0, N), engine=nc.vector):
+            engine.tensor_tensor(woven(g), strands(left, cols), strands(right, cols), ALU.mult)
 
-        def result(copies, stationary, moving, rows, slot, kind):
+        def quantize_part(src, fmt, whole, cols):
+            nc.vector.quantize_mx(out=whole[0][:, cols].bitcast(fmt), scales=whole[1][:, cols], in_=src)
+
+        def operand(name, fmt):
+            codes = held.tile([P, N], U32, name=name + "_codes", align_bytes=64)
+            scales = held.tile([P, N], U8, name=name + "_scales", align_bytes=64)
+            return codes[:], scales[:], fmt
+
+        def result(copies, stationary, moving, rows, slot, first):
             staged = big_tile(slot, "staged")
             for j in range(PACK):
-                acc = bank(kind)
+                acc = bank[first + j]
                 product(acc, stationary, j, moving)
                 copies[j](staged[:, j * N : (j + 1) * N], acc[:])
                 nc.sync.dma_start(rows[j], staged[:, j * N : (j + 1) * N])
 
-        def of_z(func, dst, b, first):
+        def of_z(func, dst, b):
             for r in range(PACK):
                 cols = slice(r * N, (r + 1) * N)
-                k = first + b * PACK + r
+                k = b * PACK + r
                 nc.scalar.activation(dst[:, cols], z[b][:, cols], func, scale=inverse[:, k : k + 1])
 
         def slope_of(b):
-            nc.vector.scalar_tensor_tensor(mirrored[b][:], mirrored[b][:], 1.0, sigmoid[b][:], ALU.subtract, ALU.mult)
+            nc.vector.scalar_tensor_tensor(slope, mirrored[b][:], 1.0, sigmoid[b][:], ALU.subtract, ALU.mult)
 
-        tx_cols = token_columns(tx_win, "tx")
-        ts_cols = token_columns(ts_win, "ts")
+        tx_picked = gather_tokens(tx_win, "tx")
+        ts_picked = gather_tokens(ts_win, "ts")
+        turn_tokens(tx_picked, (0, 1))
+
 
         cf_row = held.tile([P, N], F32, name="cf_row")
-        spread = bank()
+        spread = bank[4]
         for j in range(PACK):
             nc.tensor.transpose(spread[:, j * P : (j + 1) * P], cf_cols[:, j : j + 1].to_broadcast([P, P]), ident[:])
-        minus_cf_row = held.tile([P, N], F32, name="minus_cf_row")
         nc.scalar.copy(cf_row[:].rearrange("p (m j) -> p m j", j=PACK), spread[:].rearrange("p (j m) -> p m j", j=PACK))
-        nc.scalar.activation(minus_cf_row[:], cf_row[:], ACT.Copy, scale=-1.0)
 
-        x_picked = [grouped("x_picked_%d" % b) for b in range(EXPERTS)]
-        dy_picked = [grouped("dy_picked_%d" % b) for b in range(EXPERTS)]
+        x_both = held.tile([P, PACK, EXPERTS * N], BF16, name="x_both", align_bytes=64)
+        x_picked = [x_both[:, :, b * N : (b + 1) * N] for b in range(EXPERTS)]
         for t in range(PACK - 1):
-            for b in range(EXPERTS):
-                gather(vector_copy, x_plane, x_picked, t, b)
-        for b in range(EXPERTS):
-            along_slots(scalar_copy, x_picked[b], False, half(2, b), 0)
+            vector_copy(x_both[:, t], x_plane[t][:].indirect(offsets[:]))
+        x_along_slots(0, 5)
+        x_along_slots(1, 2)
+        turn_tokens(ts_picked, (2, 3))
         gather(vector_copy, x_plane, x_picked, 3, 0)
         gather(scalar_gather, x_plane, x_picked, 3, 1)
 
         width = EXPERTS * PACK
-        small = held.tile([P, 4 * width], F32, name="small")
-        gates, txts_cols, inverse = small[:, :width], small[:, width : 2 * width], small[:, 2 * width :]
-        nc.vector.scalar_tensor_tensor(gates, ts_cols[:], 0.0, ts_cols[:], ALU.is_equal, ALU.add)
-        nc.vector.tensor_tensor(txts_cols, tx_cols[:], ts_cols[:], ALU.mult)
-        nc.vector.reciprocal(inverse[:, :width], gates)
-        nc.scalar.activation(inverse[:, width:], inverse[:, :width], ACT.Copy, scale=-1.0)
+        columns = big_tile("x_3", "columns", 6 * width)
+        tx_cols, ts_cols, gates, txts_cols, minus_txts_cols, inverse = (
+            columns[:, k * width : (k + 1) * width] for k in range(6)
+        )
+        token_columns(tx_cols, (0, 1))
+        token_columns(ts_cols, (2, 3))
+        along_features(vector_copy, x_picked[0], half(0, 1))
+        nc.vector.scalar_tensor_tensor(gates, ts_cols, 0.0, ts_cols, ALU.is_equal, ALU.add)
+        nc.vector.tensor_tensor(txts_cols, tx_cols, ts_cols, ALU.mult)
+        along_features(scalar_copy, x_picked[1], half(1, 1))
+        early_codes = big.tile([P, N], U32, name="early_codes", tag="early_codes", align_bytes=64)
+        x_feat = [quantize(half(0, 1), E4M3, "x_feat_0", early_codes)[0]]
+        nc.vector.reciprocal(inverse, gates)
+        group_w1(vector_copy, 0, half(0, 0))
+        first_codes = big.tile([P, 2 * N], U32, name="first_codes", tag="first_codes", align_bytes=64)
+        x_feat.append(quantize(half(1, 1), E4M3, "x_feat_1", first_codes[:, :N])[0])
+        w1_q = [quantize(half(0, 0), E4M3, "w1_q_0")[0]]
+        x_along_slots(2, 0)
+        x_along_slots(3, 1)
+        group_w1(scalar_copy, 1, half(1, 0))
+        nc.scalar.activation(minus_txts_cols, txts_cols, ACT.Copy, scale=-1.0)
+        x_slot = [quantize(half(2, 0), E4M3, "x_slot_0")[0]]
 
         z = [big_tile(slot, "z") for slot in ("tx", "ts")]
-        along_features(vector_copy, x_picked[0], half(0, 1))
-        along_features(scalar_copy, x_picked[1], half(1, 1))
-        group_w1(vector_copy, 0, half(0, 0))
-        x_feat = [quantize(half(0, 1), E4M3, "x_feat_0")[0]]
-        w1_q = [quantize(half(0, 0), E4M3, "w1_q_0")[0]]
-        x_feat.append(quantize(half(1, 1), E4M3, "x_feat_1")[0])
-        group_w1(scalar_copy, 1, half(1, 0))
-        scaled_product(x_feat[0], w1_q[0], cf_row, 0, z[0])
-        w1_q.append(quantize(half(1, 0), E4M3, "w1_q_1")[0])
-        for b in range(EXPERTS):
-            along_slots(scalar_copy, x_picked[b], False, half(2, b), 1)
-        for b in range(EXPERTS):
-            gather(scalar_gather, dy_plane, dy_picked, 0, b)
-        scaled_product(x_feat[1], w1_q[1], cf_row, 1, z[1])
-        x_slot = quantize(pair[2][:], E4M3, "x_slot")
-
         sigmoid = [big_tile("x_%d" % b, "sigmoid") for b in range(EXPERTS)]
-        mirrored = [big_tile("x_%d" % (2 + b), "mirrored") for b in range(EXPERTS)]
-        of_z(ACT.Sigmoid, sigmoid[0], 0, 0)
-        for b in range(EXPERTS):
-            gather(scalar_gather, dy_plane, dy_picked, 1, b)
-        of_z(ACT.Sigmoid, sigmoid[1], 1, 0)
-        woven_product(half(0, 1), z[0], sigmoid[0])
-        for t in (2, 3):
-            for b in range(EXPERTS):
-                gather(vector_copy, dy_plane, dy_picked, t, b)
-        h_q = [quantize(half(0, 1), E4M3, "h_0")[0]]
-        of_z(ACT.Silu, mirrored[0], 0, width)
+        mirrored = [big_tile(slot, "mirrored") for slot in ("x_2", "w1_0")]
+        slope = pair[0][:].bitcast(F32)
+        low, high = slice(0, N // 2), slice(N // 2, N)
+        part = PACK * N // 2
+        dy_picked = [grouped("dy_picked_0").rearrange("p (t n) -> p t n", t=PACK)]
+        round_w2(gpsimd_copy, 0, half(2, 0))
+        scaled_product(x_feat[0], w1_q[0], txts_cols, 0, z[0], 4)
+        w1_q.append(quantize(half(1, 0), E4M3, "w1_q_1", first_codes[:, N:])[0])
+        slot_codes = big.tile([P, N], U32, name="slot_codes", tag="early_codes", align_bytes=64)
+        x_slot.append(quantize(half(2, 1), E4M3, "x_slot_1", slot_codes)[0])
+        gather(scalar_gather, dy_plane, dy_picked, 0, 0)
+        of_z(ACT.Sigmoid, sigmoid[0], 0)
+        woven_product(half(2, 1)[:, :part], z[0], sigmoid[0], low, nc.gpsimd)
+        scaled_product(x_feat[1], w1_q[1], txts_cols, 1, z[1], 0)
+        gather(scalar_gather, dy_plane, dy_picked, 1, 0)
+        of_z(ACT.Sigmoid, sigmoid[1], 1)
+        nc.scalar.activation(inverse, inverse, ACT.Copy, scale=-1.0)
+        hidden = big.tile([P, PACK * N], BF16, name="hidden", tag="first_codes", align_bytes=64)
+        woven_product(hidden[:, :part], z[0], sigmoid[0], high)
+        gather(vector_copy, dy_plane, dy_picked, 2, 0)
+        group_w2(scalar_copy, half(2, 0), half(1, 1), (0, 1))
+        h_q = [operand("h_%d" % b, E4M3) for b in range(EXPERTS)]
+        quantize_part(half(2, 1)[:, :part], E4M3, h_q[0], low)
+        quantize_part(hidden[:, :part], E4M3, h_q[0], high)
+        woven_product(hidden[:, part:], z[1], sigmoid[1], low)
+        gather(vector_copy, dy_plane, dy_picked, 3, 0)
+        of_z(ACT.Silu, mirrored[0], 0)
+        quantize_part(hidden[:, part:], E4M3, h_q[1], low)
         along_features(vector_copy, dy_picked[0], half(0, 0))
-        round_w2(vector_copy, 0, x_picked[0])
+        w2_q = [quantize(half(1, 1), E4M3, "w2_0")[0]]
         dy_feat = [quantize(half(0, 0), E5M2, "dy_feat_0")[0]]
-        w2_grouped = [grouped("w2_grouped_%d" % b) for b in range(EXPERTS)]
-        group_w2(scalar_copy, x_picked[0], w2_grouped[0])
+        late_picked = big.tile([P, PACK, N], BF16, name="late_picked", tag="tx", align_bytes=64)
+        dy_picked.append(late_picked[:])
         slope_of(0)
-        w2_q = [quantize(w2_grouped[0], E4M3, "w2_0")[0]]
+        after_slope = big_tile("x_2", "after_slope", PACK * N + PACK * N // 2)
+        dh, late_rounded = after_slope[:, : PACK * N], after_slope[:, PACK * N :].bitcast(BF16)
+        round_w2(gpsimd_copy, 1, late_rounded)
+        scaled_product(dy_feat[0], w2_q[0], minus_txts_cols, 0, dh, 4)
+        for t in range(PACK):
+            gather(scalar_gather, dy_plane, dy_picked, t, 1)
         for side in range(2):
-            along_slots(scalar_copy, dy_picked[0], True, half(3, 0), side)
-        of_z(ACT.Silu, mirrored[1], 1, width)
-        dh = [big_tile("w1_%d" % b, "dh") for b in range(EXPERTS)]
-        scaled_product(dy_feat[0], w2_q[0], minus_cf_row, 0, dh[0])
-        dy_slot = [quantize(half(3, 0), E5M2, "dy_slot_0")[0]]
-        woven_product(half(2, 0), mirrored[0], dh[0])
+            dy_along_slots(scalar_copy, dy_picked[0], half(3, 0), side, 2 + side)
+        woven_product(half(2, 0), slope, dh)
         along_features(scalar_copy, dy_picked[1], half(1, 0))
-        round_w2(scalar_copy, 1, x_picked[1])
-        group_w2(scalar_copy, x_picked[1], w2_grouped[1])
-        slope_of(1)
-        da = [quantize(half(2, 0), E5M2, "da_0")[0]]
+        group_w2(scalar_copy, late_rounded, half(1, 1), (4, 5))
+        of_z(ACT.Silu, mirrored[1], 1)
+        dy_slot = [quantize(half(3, 0), E5M2, "dy_slot_0")[0]]
+        da = quantize(half(2, 0), E5M2, "da_0")[0]
         dy_feat.append(quantize(half(1, 0), E5M2, "dy_feat_1")[0])
-        w2_q.append(quantize(w2_grouped[1], E4M3, "w2_1")[0])
+        w2_q.append(quantize(half(1, 1), E4M3, "w2_1")[0])
         for side in range(2):
-            along_slots(scalar_copy, dy_picked[1], True, half(3, 1), side)
-        scaled_product(dy_feat[1], w2_q[1], minus_cf_row, 1, dh[1])
-        result([scalar_copy] * PACK, h_q[0], dy_slot[0], out_1[0].rearrange("(c p) e -> c p e", c=PACK), "dy_0", "turn")
-        result([scalar_copy] * PACK, x_slot[0], da[0], out_0[0].rearrange("(p t) f -> t p f", t=PACK), "dy_1", "turn")
-        woven_product(half(2, 1), mirrored[1], dh[1])
+            dy_along_slots(scalar_copy, dy_picked[1], half(3, 1), side, 6 + side)
+        slope_of(1)
+        after_slope = big_tile("w1_0", "after_slope", PACK * N + PACK * N // 4)
+        dh, late_hidden = after_slope[:, : PACK * N], after_slope[:, PACK * N :].bitcast(BF16)
+        woven_product(late_hidden, z[1], sigmoid[1], high, nc.gpsimd)
+        result([scalar_copy] * PACK, h_q[0], dy_slot[0], out_1[0].rearrange("(c p) e -> c p e", c=PACK), "dy_0", 0)
+        scaled_product(dy_feat[1], w2_q[1], minus_txts_cols, 1, dh, 4)
+        result([scalar_copy] * PACK, x_slot[0], da, out_0[0].rearrange("(p t) f -> t p f", t=PACK), "dy_1", 0)
         dy_slot.append(quantize(half(3, 1), E5M2, "dy_slot_1")[0])
-        da.append(quantize(half(2, 1), E5M2, "da_1")[0])
-        result([scalar_copy] * PACK, x_slot[1], da[1], out_0[1].rearrange("(p t) f -> t p f", t=PACK), "dy_2", "turn")
+        quantize_part(late_hidden, E4M3, h_q[1], high)
+        result([scalar_copy] * PACK, h_q[1], dy_slot[1], out_1[1].rearrange("(c p) e -> c p e", c=PACK), "dy_2", 0)
 
-        g = half(1, 1)
-        codes = held.tile([P, N], U32, name="h_1_codes", align_bytes=64)
-        scales = held.tile([P, N], U8, name="h_1_scales", align_bytes=64)
-        for c in range(PACK):
-            woven_product(g, z[1], sigmoid[1], slice(c * P, (c + 1) * P))
-            nc.vector.quantize_mx(
-                out=codes[:, c * P : (c + 1) * P].bitcast(E4M3), scales=scales[:, c * P : (c + 1) * P], in_=g[:, c * N : (c + 1) * N]
-            )
-        result(
-            [vector_copy, scalar_copy] * 2, (codes, scales, E4M3), dy_slot[1], out_1[1].rearrange("(c p) e -> c p e", c=PACK), "dy_3", "sums"
-        )
+        g = half(2, 1)
+        da = operand("da_1", E5M2)
+        staged = big_tile("dy_3", "staged")
+        rows = out_0[1].rearrange("(p t) f -> p t f", t=PACK)
+        for c, cols in enumerate((low, high)):
+            woven_product(g[:, c * part : (c + 1) * part], slope, dh, cols)
+        for c, cols in enumerate((low, high)):
+            quantize_part(g[:, c * part : (c + 1) * part], E5M2, da, cols)
+            for u in range(2):
+                acc = bank[4 + 2 * c + u]
+                for v in range(2):
+                    product(acc[:, v * N // 2 : (v + 1) * N // 2], x_slot[1], 2 * u + v, (da[0][:, cols], da[1][:, cols], E5M2))
+                piece = staged[:, (2 * c + u) * N : (2 * c + u + 1) * N]
+                (nc.scalar.copy if c == 1 and u == 1 else nc.vector.tensor_copy)(piece, acc[:])
+                nc.sync.dma_start(rows[:, 2 * u : 2 * u + 2, cols], piece.rearrange("p (v f) -> p v f", v=2))

@@ -33,7 +33,7 @@ def tile_attend_gxfull_sil_W_kernel(tc, xT, dyT, w1, w2, ts, tx, cf, offs, out_0
             return big.tile([P, width], F32, name=name, tag=slot, align_bytes=64)
 
         bank = [psum.tile([P, N], F32, name="bank_%d" % j) for j in range(8)]
-        pair = [held.tile([P, 2 * PACK * N], BF16, name="pair_%d" % j, align_bytes=64) for j in range(4)]
+        pair = {j: held.tile([P, 2 * PACK * N], BF16, name="pair_%d" % j, align_bytes=64) for j in (0, 1, 3)}
 
         def half(j, k):
             return pair[j][:, k * PACK * N : (k + 1) * PACK * N]
@@ -180,12 +180,12 @@ def tile_attend_gxfull_sil_W_kernel(tc, xT, dyT, w1, w2, ts, tx, cf, offs, out_0
                 turned[:].rearrange("s (k p) -> s p k", k=4),
             )
 
-        def scaled_product(stationary, moving, cols, b, dst, first):
+        def scaled_product(stationary, moving, cols, dst, first):
             for r in range(PACK):
                 acc = bank[first + r]
                 product(acc, stationary, r, moving)
                 nc.vector.scalar_tensor_tensor(
-                    dst[:, r * N : (r + 1) * N], acc[:], cols[:, b * PACK + r : b * PACK + r + 1], cf_row[:], ALU.mult, ALU.mult
+                    dst[:, r * N : (r + 1) * N], acc[:], cols[:, r : r + 1], cf_row[:], ALU.mult, ALU.mult
                 )
 
         def woven(dst):
@@ -225,6 +225,7 @@ def tile_attend_gxfull_sil_W_kernel(tc, xT, dyT, w1, w2, ts, tx, cf, offs, out_0
         tx_picked = gather_tokens(tx_win, "tx")
         ts_picked = gather_tokens(ts_win, "ts")
         turn_tokens(tx_picked, (0, 1))
+        pair.setdefault(2, big.tile([P, 2 * PACK * N], BF16, name="pair_2", tag="ts", align_bytes=64))
 
 
         cf_row = held.tile([P, N], F32, name="cf_row")
@@ -244,9 +245,9 @@ def tile_attend_gxfull_sil_W_kernel(tc, xT, dyT, w1, w2, ts, tx, cf, offs, out_0
         gather(scalar_gather, x_plane, x_picked, 3, 1)
 
         width = EXPERTS * PACK
-        columns = big_tile("x_3", "columns", 6 * width)
-        tx_cols, ts_cols, gates, txts_cols, minus_txts_cols, inverse = (
-            columns[:, k * width : (k + 1) * width] for k in range(6)
+        columns = big_tile("x_3", "columns", PACK * N + 5 * width)
+        tx_cols, ts_cols, gates, txts_cols, inverse = (
+            columns[:, PACK * N + k * width : PACK * N + (k + 1) * width] for k in range(5)
         )
         token_columns(tx_cols, (0, 1))
         token_columns(ts_cols, (2, 3))
@@ -264,77 +265,75 @@ def tile_attend_gxfull_sil_W_kernel(tc, xT, dyT, w1, w2, ts, tx, cf, offs, out_0
         x_along_slots(2, 0)
         x_along_slots(3, 1)
         group_w1(scalar_copy, 1, half(1, 0))
-        nc.scalar.activation(minus_txts_cols, txts_cols, ACT.Copy, scale=-1.0)
+        minus_cols = [big.tile([P, PACK], F32, name="minus_cols", tag="minus_%d" % b, align_bytes=64) for b in range(EXPERTS)]
+        for b in range(EXPERTS):
+            nc.scalar.activation(minus_cols[b][:], txts_cols[:, b * PACK : (b + 1) * PACK], ACT.Copy, scale=-1.0)
         x_slot = [quantize(half(2, 0), E4M3, "x_slot_0")[0]]
 
-        z = [big_tile(slot, "z") for slot in ("tx", "ts")]
-        sigmoid = [big_tile("x_%d" % b, "sigmoid") for b in range(EXPERTS)]
-        mirrored = [big_tile(slot, "mirrored") for slot in ("x_2", "w1_0")]
+        z = [big_tile("tx", "z"), columns[:, : PACK * N]]
         slope = pair[0][:].bitcast(F32)
         low, high = slice(0, N // 2), slice(N // 2, N)
         part = PACK * N // 2
-        dy_picked = [grouped("dy_picked_0").rearrange("p (t n) -> p t n", t=PACK)]
+        dy_both = held.tile([P, PACK, EXPERTS * N], BF16, name="dy_both", align_bytes=64)
+        dy_picked = [dy_both[:, :, b * N : (b + 1) * N] for b in range(EXPERTS)]
         round_w2(gpsimd_copy, 0, half(2, 0))
-        scaled_product(x_feat[0], w1_q[0], txts_cols, 0, z[0], 4)
+        scaled_product(x_feat[0], w1_q[0], txts_cols[:, :PACK], z[0], 4)
         w1_q.append(quantize(half(1, 0), E4M3, "w1_q_1", first_codes[:, N:])[0])
         slot_codes = big.tile([P, N], U32, name="slot_codes", tag="early_codes", align_bytes=64)
         x_slot.append(quantize(half(2, 1), E4M3, "x_slot_1", slot_codes)[0])
-        gather(scalar_gather, dy_plane, dy_picked, 0, 0)
+        sigmoid = [big_tile("x_0", "sigmoid")]
         of_z(ACT.Sigmoid, sigmoid[0], 0)
-        woven_product(half(2, 1)[:, :part], z[0], sigmoid[0], low, nc.gpsimd)
-        scaled_product(x_feat[1], w1_q[1], txts_cols, 1, z[1], 0)
-        gather(scalar_gather, dy_plane, dy_picked, 1, 0)
+        scalar_gather(dy_both[:, 0], dy_plane[0][:].indirect(offsets[:]))
+        scaled_product(x_feat[1], w1_q[1], txts_cols[:, PACK:], z[1], 0)
+        sigmoid.append(big_tile("dy_0", "sigmoid"))
         of_z(ACT.Sigmoid, sigmoid[1], 1)
         nc.scalar.activation(inverse, inverse, ACT.Copy, scale=-1.0)
         hidden = big.tile([P, PACK * N], BF16, name="hidden", tag="first_codes", align_bytes=64)
-        woven_product(hidden[:, :part], z[0], sigmoid[0], high)
-        gather(vector_copy, dy_plane, dy_picked, 2, 0)
+        woven_product(hidden[:], z[0], sigmoid[0])
         group_w2(scalar_copy, half(2, 0), half(1, 1), (0, 1))
-        h_q = [operand("h_%d" % b, E4M3) for b in range(EXPERTS)]
-        quantize_part(half(2, 1)[:, :part], E4M3, h_q[0], low)
-        quantize_part(hidden[:, :part], E4M3, h_q[0], high)
-        woven_product(hidden[:, part:], z[1], sigmoid[1], low)
+        scalar_gather(dy_both[:, 1], dy_plane[1][:].indirect(offsets[:]))
+        gather(vector_copy, dy_plane, dy_picked, 2, 0)
+        h_q = [quantize(hidden[:], E4M3, "h_0")[0]]
+        woven_product(half(2, 1), z[1], sigmoid[1])
         gather(vector_copy, dy_plane, dy_picked, 3, 0)
+        mirrored = [big_tile("dy_1", "mirrored")]
         of_z(ACT.Silu, mirrored[0], 0)
-        quantize_part(hidden[:, part:], E4M3, h_q[1], low)
+        h_q.append(quantize(half(2, 1), E4M3, "h_1")[0])
         along_features(vector_copy, dy_picked[0], half(0, 0))
         w2_q = [quantize(half(1, 1), E4M3, "w2_0")[0]]
         dy_feat = [quantize(half(0, 0), E5M2, "dy_feat_0")[0]]
-        late_picked = big.tile([P, PACK, N], BF16, name="late_picked", tag="tx", align_bytes=64)
-        dy_picked.append(late_picked[:])
         slope_of(0)
-        after_slope = big_tile("x_2", "after_slope", PACK * N + PACK * N // 2)
+        after_slope = big_tile("dy_1", "after_slope", PACK * N + PACK * N // 2)
         dh, late_rounded = after_slope[:, : PACK * N], after_slope[:, PACK * N :].bitcast(BF16)
         round_w2(gpsimd_copy, 1, late_rounded)
-        scaled_product(dy_feat[0], w2_q[0], minus_txts_cols, 0, dh, 4)
-        for t in range(PACK):
+        scaled_product(dy_feat[0], w2_q[0], minus_cols[0], dh, 4)
+        for t in (2, 3):
             gather(scalar_gather, dy_plane, dy_picked, t, 1)
         for side in range(2):
             dy_along_slots(scalar_copy, dy_picked[0], half(3, 0), side, 2 + side)
         woven_product(half(2, 0), slope, dh)
         along_features(scalar_copy, dy_picked[1], half(1, 0))
-        group_w2(scalar_copy, late_rounded, half(1, 1), (4, 5))
+        mirrored.append(big_tile("tx", "mirrored"))
         of_z(ACT.Silu, mirrored[1], 1)
-        dy_slot = [quantize(half(3, 0), E5M2, "dy_slot_0")[0]]
+        group_w2(scalar_copy, late_rounded, half(1, 1), (4, 5))
+        late_codes = big.tile([P, 2 * N], U32, name="late_codes", tag="minus_0", align_bytes=64)
+        dy_slot = [quantize(half(3, 0), E5M2, "dy_slot_0", late_codes[:, :N])[0]]
         da = quantize(half(2, 0), E5M2, "da_0")[0]
-        dy_feat.append(quantize(half(1, 0), E5M2, "dy_feat_1")[0])
+        dy_feat.append(quantize(half(1, 0), E5M2, "dy_feat_1", late_codes[:, N:])[0])
         w2_q.append(quantize(half(1, 1), E4M3, "w2_1")[0])
         for side in range(2):
             dy_along_slots(scalar_copy, dy_picked[1], half(3, 1), side, 6 + side)
-        slope_of(1)
-        after_slope = big_tile("w1_0", "after_slope", PACK * N + PACK * N // 4)
-        dh, late_hidden = after_slope[:, : PACK * N], after_slope[:, PACK * N :].bitcast(BF16)
-        woven_product(late_hidden, z[1], sigmoid[1], high, nc.gpsimd)
-        result([scalar_copy] * PACK, h_q[0], dy_slot[0], out_1[0].rearrange("(c p) e -> c p e", c=PACK), "dy_0", 0)
-        scaled_product(dy_feat[1], w2_q[1], minus_txts_cols, 1, dh, 4)
-        result([scalar_copy] * PACK, x_slot[0], da, out_0[0].rearrange("(p t) f -> t p f", t=PACK), "dy_1", 0)
         dy_slot.append(quantize(half(3, 1), E5M2, "dy_slot_1")[0])
-        quantize_part(late_hidden, E4M3, h_q[1], high)
-        result([scalar_copy] * PACK, h_q[1], dy_slot[1], out_1[1].rearrange("(c p) e -> c p e", c=PACK), "dy_2", 0)
+        slope_of(1)
+        dh = big_tile("tx", "dh")
+        result([scalar_copy] * PACK, h_q[0], dy_slot[0], out_1[0].rearrange("(c p) e -> c p e", c=PACK), "x_1", 0)
+        scaled_product(dy_feat[1], w2_q[1], minus_cols[1], dh, 4)
+        result([scalar_copy] * PACK, x_slot[0], da, out_0[0].rearrange("(p t) f -> t p f", t=PACK), "x_2", 0)
+        result([scalar_copy] * PACK, h_q[1], dy_slot[1], out_1[1].rearrange("(c p) e -> c p e", c=PACK), "w1_0", 0)
 
         g = half(2, 1)
         da = operand("da_1", E5M2)
-        staged = big_tile("dy_3", "staged")
+        staged = big_tile("w1_1", "staged")
         rows = out_0[1].rearrange("(p t) f -> p t f", t=PACK)
         for c, cols in enumerate((low, high)):
             woven_product(g[:, c * part : (c + 1) * part], slope, dh, cols)
@@ -345,5 +344,5 @@ def tile_attend_gxfull_sil_W_kernel(tc, xT, dyT, w1, w2, ts, tx, cf, offs, out_0
                 for v in range(2):
                     product(acc[:, v * N // 2 : (v + 1) * N // 2], x_slot[1], 2 * u + v, (da[0][:, cols], da[1][:, cols], E5M2))
                 piece = staged[:, (2 * c + u) * N : (2 * c + u + 1) * N]
-                (nc.scalar.copy if c == 1 and u == 1 else nc.vector.tensor_copy)(piece, acc[:])
+                (nc.scalar.copy if u == 1 else nc.vector.tensor_copy)(piece, acc[:])
                 nc.sync.dma_start(rows[:, 2 * u : 2 * u + 2, cols], piece.rearrange("p (v f) -> p v f", v=2))

@@ -127,8 +127,8 @@ def tile_attend_gxfull_sil_W_kernel(tc, xT, dyT, w1, w2, ts, tx, cf, offs, out_0
 
         def group_w1(copy, b, g):
             copy(
-                g.rearrange("p (c i j) -> p c j i", i=2, j=PACK),
-                w1_raw[b][:].rearrange("p (j c i) -> p c j i", i=2, j=PACK),
+                g.rearrange("p (c i j) -> p c j i", i=PACK, j=PACK),
+                w1_raw[b][:].rearrange("p (j c i) -> p c j i", i=PACK, j=PACK),
             )
 
         def round_w2(copy, b, rounded):
@@ -154,7 +154,10 @@ def tile_attend_gxfull_sil_W_kernel(tc, xT, dyT, w1, w2, ts, tx, cf, offs, out_0
             copy(picked[b][:, t], listed(planes[t], b))
 
         def along_features(copy, picked, g):
-            copy(g.rearrange("p (r s t) -> p s t r", r=PACK, t=PACK), picked.rearrange("p t (s r) -> p s t r", r=PACK))
+            copy(
+                g.rearrange("p (r s i t) -> p s r i t", r=PACK, i=2, t=PACK),
+                picked.rearrange("p t (s i r) -> p s r i t", r=PACK, i=2),
+            )
 
         def x_along_slots(t, which):
             words = x_both[:, t].bitcast(F32)
@@ -189,10 +192,10 @@ def tile_attend_gxfull_sil_W_kernel(tc, xT, dyT, w1, w2, ts, tx, cf, offs, out_0
                 )
 
         def woven(dst):
-            return dst.rearrange("p (c i r) -> p c r i", i=2, r=PACK)
+            return dst.rearrange("p (c i r) -> p c r i", i=PACK, r=PACK)
 
         def strands(src, cols):
-            return src[:].rearrange("p (r n) -> p r n", r=PACK)[:, :, cols].rearrange("p r (c i) -> p c r i", i=2)
+            return src[:].rearrange("p (r n) -> p r n", r=PACK)[:, :, cols].rearrange("p r (c i) -> p c r i", i=PACK)
 
         def woven_product(g, left, right, cols=slice(0, N), engine=nc.vector):
             engine.tensor_tensor(woven(g), strands(left, cols), strands(right, cols), ALU.mult)

@@ -132,10 +132,7 @@ def tile_attend_gxfull_sil_W_kernel(tc, xT, dyT, w1, w2, ts, tx, cf, offs, out_0
             )
 
         def round_w2(copy, b, rounded):
-            copy(
-                rounded.rearrange("f (c u p x) -> f c p u x", c=PACK, u=2, x=2),
-                w2_raw[b][:].rearrange("f (c p u x) -> f c p u x", c=PACK, u=2, x=2),
-            )
+            copy(rounded, w2_raw[b][:])
 
         def group_w2(copy, rounded, g, banks):
             words = rounded.bitcast(F32)
@@ -143,8 +140,8 @@ def tile_attend_gxfull_sil_W_kernel(tc, xT, dyT, w1, w2, ts, tx, cf, offs, out_0
             for side in range(2):
                 turned = bank[banks[side]]
                 for k in range(PACK):
-                    cols = slice((side * PACK + k) * P, (side * PACK + k + 1) * P)
-                    nc.tensor.transpose(turned[:, k * P : (k + 1) * P], words[:, cols], ident[:])
+                    first = (2 * side + k // 2) * 2 * P
+                    nc.tensor.transpose(turned[:, k * P : (k + 1) * P], words[:, first + k % 2 : first + 2 * P : 2], ident[:])
                 copy(
                     g_words[:, side * N : (side + 1) * N].rearrange("p (c f u) -> p c f u", c=2, u=2),
                     turned[:].rearrange("p (c u f) -> p c f u", c=2, u=2),

@@ -44,7 +44,8 @@ def tile_attend_gxfull_sil_W_kernel(tc, xT, dyT, w1, w2, ts, tx, cf, offs, out_0
                 codes = held.tile([P, width], U32, name=name + "_codes", align_bytes=64)
             scales = held.tile([P, width], U8, name=name + "_scales", align_bytes=64)
             nc.vector.quantize_mx(out=codes[:].bitcast(fmt), scales=scales[:], in_=src)
-            return [(codes[:, k : k + N], scales[:, k : k + N], fmt) for k in range(0, width, N)]
+            step = min(width, N)
+            return [(codes[:, k : k + step], scales[:, k : k + step], fmt) for k in range(0, width, step)]
 
         def product(dst, stationary, j, moving):
             cols = slice(j * P, (j + 1) * P)
@@ -86,8 +87,10 @@ def tile_attend_gxfull_sil_W_kernel(tc, xT, dyT, w1, w2, ts, tx, cf, offs, out_0
 
         for t in range(PACK):
             nc.sync.dma_start(x_plane[t][:], xT.rearrange("(p t) n -> t p n", t=PACK)[t])
-        for b in range(EXPERTS):
+
+        def load_w1(b):
             nc.sync.dma_start(w1_raw[b][:], w1[b].rearrange("(p j) f -> p (j f)", j=PACK))
+
         def load_dy(t):
             nc.sync.dma_start(dy_plane[t][:], dyT.rearrange("(p t) n -> t p n", t=PACK)[t])
 
@@ -96,6 +99,8 @@ def tile_attend_gxfull_sil_W_kernel(tc, xT, dyT, w1, w2, ts, tx, cf, offs, out_0
                 w2_raw[b][:].rearrange("p (c e) -> p c e", c=PACK), w2[b].rearrange("(c p) e -> p c e", c=PACK)
             )
 
+        load_w1(0)
+        load_w1(1)
         load_w2(0)
         for t in range(PACK):
             load_dy(t)
@@ -125,10 +130,10 @@ def tile_attend_gxfull_sil_W_kernel(tc, xT, dyT, w1, w2, ts, tx, cf, offs, out_0
             for b in range(EXPERTS):
                 nc.scalar.copy(cols[:, b * PACK : (b + 1) * PACK], bank[banks[b]][:, P - 1 : N : P])
 
-        def group_w1(copy, b, g):
+        def group_w1(copy, b, g, cols=slice(0, N)):
             copy(
-                g.rearrange("p (c i j) -> p c j i", i=PACK, j=PACK),
-                w1_raw[b][:].rearrange("p (j c i) -> p c j i", i=PACK, j=PACK),
+                g[:, cols.start * PACK : cols.stop * PACK].rearrange("p (c i j) -> p c j i", i=PACK, j=PACK),
+                w1_raw[b][:].rearrange("p (j f) -> p j f", j=PACK)[:, :, cols].rearrange("p j (c i) -> p c j i", i=PACK),
             )
 
         def round_w2(copy, b, rounded):
@@ -194,8 +199,15 @@ def tile_attend_gxfull_sil_W_kernel(tc, xT, dyT, w1, w2, ts, tx, cf, offs, out_0
         def strands(src, cols):
             return src[:].rearrange("p (r n) -> p r n", r=PACK)[:, :, cols].rearrange("p r (c i) -> p c r i", i=PACK)
 
-        def woven_product(g, left, right, cols=slice(0, N), engine=nc.vector):
-            engine.tensor_tensor(woven(g), strands(left, cols), strands(right, cols), ALU.mult)
+        def woven_product(g, left, right, cols=slice(0, N)):
+            nc.vector.tensor_tensor(woven(g), strands(left, cols), strands(right, cols), ALU.mult)
+
+        def paired_product(g, left, right, cols):
+            left, right = (
+                src[:].rearrange("p (r n) -> p r n", r=PACK)[:, :, cols].rearrange("p r (c i) -> p c r i", i=2)
+                for src in (left, right)
+            )
+            nc.gpsimd.tensor_tensor(g.rearrange("p (c i r) -> p c r i", i=2, r=PACK), left, right, ALU.mult)
 
         def quantize_part(src, fmt, whole, cols):
             nc.vector.quantize_mx(out=whole[0][:, cols].bitcast(fmt), scales=whole[1][:, cols], in_=src)
@@ -209,7 +221,8 @@ def tile_attend_gxfull_sil_W_kernel(tc, xT, dyT, w1, w2, ts, tx, cf, offs, out_0
             staged = big_tile(slot, "staged")
             for j in range(PACK):
                 acc = bank[first + j]
-                product(acc, stationary, j, moving)
+                per_part = PACK // len(stationary)
+                product(acc, stationary[j // per_part], j % per_part, moving)
                 copies[j](staged[:, j * N : (j + 1) * N], acc[:])
                 nc.sync.dma_start(rows[j], staged[:, j * N : (j + 1) * N])
 
@@ -219,7 +232,7 @@ def tile_attend_gxfull_sil_W_kernel(tc, xT, dyT, w1, w2, ts, tx, cf, offs, out_0
                 k = b * PACK + r
                 nc.scalar.activation(dst[:, cols], z[b][:, cols], func, scale=inverse[:, k : k + 1])
 
-        def slope_of(b):
+        def slope_of(b, slope):
             nc.vector.scalar_tensor_tensor(slope, mirrored[b][:], 1.0, sigmoid[b][:], ALU.subtract, ALU.mult)
 
         tx_picked = gather_tokens(tx_win, "tx")
@@ -236,11 +249,13 @@ def tile_attend_gxfull_sil_W_kernel(tc, xT, dyT, w1, w2, ts, tx, cf, offs, out_0
 
         x_both = held.tile([P, PACK, EXPERTS * N], BF16, name="x_both", align_bytes=64)
         x_picked = [x_both[:, :, b * N : (b + 1) * N] for b in range(EXPERTS)]
-        for t in range(PACK - 1):
+        for t in range(2):
             vector_copy(x_both[:, t], x_plane[t][:].indirect(offsets[:]))
+        gather(vector_copy, x_plane, x_picked, 2, 0)
         x_along_slots(0, 5)
         x_along_slots(1, 2)
         turn_tokens(ts_picked, (2, 3))
+        gather(scalar_gather, x_plane, x_picked, 2, 1)
         gather(vector_copy, x_plane, x_picked, 3, 0)
         gather(scalar_gather, x_plane, x_picked, 3, 1)
 
@@ -259,90 +274,112 @@ def tile_attend_gxfull_sil_W_kernel(tc, xT, dyT, w1, w2, ts, tx, cf, offs, out_0
         x_feat = [quantize(half(0, 1), E4M3, "x_feat_0", early_codes)[0]]
         nc.vector.reciprocal(inverse, gates)
         group_w1(vector_copy, 0, half(0, 0))
-        first_codes = big.tile([P, 2 * N], U32, name="first_codes", tag="first_codes", align_bytes=64)
-        x_feat.append(quantize(half(1, 1), E4M3, "x_feat_1", first_codes[:, :N])[0])
         w1_q = [quantize(half(0, 0), E4M3, "w1_q_0")[0]]
+        first_codes = big.tile([P, N], U32, name="first_codes", tag="first_codes", align_bytes=64)
+        x_feat.append(quantize(half(1, 1), E4M3, "x_feat_1", first_codes)[0])
         x_along_slots(2, 0)
         x_along_slots(3, 1)
-        group_w1(scalar_copy, 1, half(1, 0))
+        w1_grouped = big.tile([P, PACK * N], BF16, name="w1_grouped", tag="w1_grouped", align_bytes=64)
+        group_w1(scalar_copy, 1, w1_grouped[:])
         minus_cols = [big.tile([P, PACK], F32, name="minus_cols", tag="minus_%d" % b, align_bytes=64) for b in range(EXPERTS)]
         for b in range(EXPERTS):
             nc.scalar.activation(minus_cols[b][:], txts_cols[:, b * PACK : (b + 1) * PACK], ACT.Copy, scale=-1.0)
-        x_slot = [quantize(half(2, 0), E4M3, "x_slot_0")[0]]
 
-        z = [big_tile("tx", "z"), columns[:, : PACK * N]]
+        x_slot = quantize(pair[2][:], E4M3, "x_slot")
+        low = slice(0, N // 2)
+        whole, part = PACK * N, PACK * N // 2
+        after_slots = big_tile("ts", "after_slots", whole + part)
+        z = [after_slots[:, :whole], columns[:, :whole]]
+        rounded = after_slots[:, whole:].bitcast(BF16)
         slope = pair[0][:].bitcast(F32)
-        low, high = slice(0, N // 2), slice(N // 2, N)
-        part = PACK * N // 2
         dy_both = held.tile([P, PACK, EXPERTS * N], BF16, name="dy_both", align_bytes=64)
         dy_picked = [dy_both[:, :, b * N : (b + 1) * N] for b in range(EXPERTS)]
-        round_w2(gpsimd_copy, 0, half(2, 0))
+        round_w2(gpsimd_copy, 0, rounded)
         scaled_product(x_feat[0], w1_q[0], txts_cols[:, :PACK], z[0], 4)
-        w1_q.append(quantize(half(1, 0), E4M3, "w1_q_1", first_codes[:, N:])[0])
-        slot_codes = big.tile([P, N], U32, name="slot_codes", tag="early_codes", align_bytes=64)
-        x_slot.append(quantize(half(2, 1), E4M3, "x_slot_1", slot_codes)[0])
+        w1_codes = big.tile([P, N], U32, name="w1_codes", tag="early_codes", align_bytes=64)
+        w1_q.append(quantize(w1_grouped[:], E4M3, "w1_q_1", w1_codes)[0])
         sigmoid = [big_tile("x_0", "sigmoid")]
         of_z(ACT.Sigmoid, sigmoid[0], 0)
         scalar_gather(dy_both[:, 0], dy_plane[0][:].indirect(offsets[:]))
+        first_block = big.tile([P, N], BF16, name="first_block", tag="w1_grouped", align_bytes=64)
+        paired_product(first_block[:], z[0], sigmoid[0], slice(0, P))
         scaled_product(x_feat[1], w1_q[1], txts_cols[:, PACK:], z[1], 0)
         sigmoid.append(big_tile("dy_0", "sigmoid"))
         of_z(ACT.Sigmoid, sigmoid[1], 1)
         nc.scalar.activation(inverse, inverse, ACT.Copy, scale=-1.0)
-        hidden = big.tile([P, PACK * N], BF16, name="hidden", tag="first_codes", align_bytes=64)
-        woven_product(hidden[:], z[0], sigmoid[0])
-        group_w2(scalar_copy, half(2, 0), half(1, 1), (0, 1))
+        hidden = big.tile([P, 3 * N], BF16, name="hidden", tag="first_codes", align_bytes=64)
+        woven_product(hidden[:], z[0], sigmoid[0], slice(P, N))
+        group_w2(scalar_copy, rounded, half(1, 1), (0, 1))
         scalar_gather(dy_both[:, 1], dy_plane[1][:].indirect(offsets[:]))
         gather(vector_copy, dy_plane, dy_picked, 2, 0)
-        h_q = [quantize(hidden[:], E4M3, "h_0")[0]]
-        woven_product(half(2, 1), z[1], sigmoid[1])
+        h_q = [operand("h_0", E4M3)]
+        quantize_part(first_block[:], E4M3, h_q[0], slice(0, P))
+        quantize_part(hidden[:], E4M3, h_q[0], slice(P, N))
+        woven_product(half(1, 0)[:, : 3 * N], z[1], sigmoid[1], slice(0, 3 * P))
         gather(vector_copy, dy_plane, dy_picked, 3, 0)
         mirrored = [big_tile("dy_1", "mirrored")]
         of_z(ACT.Silu, mirrored[0], 0)
-        h_q.append(quantize(half(2, 1), E4M3, "h_1")[0])
+        h_second = operand("h_1", E4M3)
+        quantize_part(half(1, 0)[:, : 3 * N], E4M3, h_second, slice(0, 3 * P))
         along_features(vector_copy, dy_picked[0], half(0, 0))
         w2_q = [quantize(half(1, 1), E4M3, "w2_0")[0]]
         dy_feat = [quantize(half(0, 0), E5M2, "dy_feat_0")[0]]
-        slope_of(0)
-        after_slope = big_tile("dy_1", "after_slope", PACK * N + PACK * N // 2)
-        dh, late_rounded = after_slope[:, : PACK * N], after_slope[:, PACK * N :].bitcast(BF16)
+        slope_of(0, slope)
+        after_slope = big_tile("dy_1", "after_slope", whole + part)
+        dh, late_rounded = after_slope[:, :whole], after_slope[:, whole:].bitcast(BF16)
         round_w2(gpsimd_copy, 1, late_rounded)
         scaled_product(dy_feat[0], w2_q[0], minus_cols[0], dh, 4)
         for t in (2, 3):
             gather(scalar_gather, dy_plane, dy_picked, t, 1)
         for side in range(2):
             dy_along_slots(scalar_copy, dy_picked[0], half(3, 0), side, 2 + side)
-        woven_product(half(2, 0), slope, dh)
         along_features(scalar_copy, dy_picked[1], half(1, 0))
-        mirrored.append(big_tile("tx", "mirrored"))
+        mirrored.append(big_tile("ts", "mirrored"))
         of_z(ACT.Silu, mirrored[1], 1)
         group_w2(scalar_copy, late_rounded, half(1, 1), (4, 5))
         late_codes = big.tile([P, 2 * N], U32, name="late_codes", tag="minus_0", align_bytes=64)
         dy_slot = [quantize(half(3, 0), E5M2, "dy_slot_0", late_codes[:, :N])[0]]
-        da = quantize(half(2, 0), E5M2, "da_0")[0]
+        gradient = big.tile([P, whole], BF16, name="gradient", tag="first_codes", align_bytes=64)
+        woven_product(gradient[:], slope, dh)
         dy_feat.append(quantize(half(1, 0), E5M2, "dy_feat_1", late_codes[:, N:])[0])
+        da = quantize(gradient[:], E5M2, "da_0")[0]
         w2_q.append(quantize(half(1, 1), E4M3, "w2_1")[0])
         for side in range(2):
             dy_along_slots(scalar_copy, dy_picked[1], half(3, 1), side, 6 + side)
         dy_slot.append(quantize(half(3, 1), E5M2, "dy_slot_1")[0])
-        slope_of(1)
-        dh = big_tile("tx", "dh")
-        result([scalar_copy] * PACK, h_q[0], dy_slot[0], out_1[0].rearrange("(c p) e -> c p e", c=PACK), "x_1", 0)
+        slope_of(1, slope)
+        after_slope = big_tile("ts", "after_slope", whole + N // 2)
+        dh, last_block = after_slope[:, :whole], after_slope[:, whole:].bitcast(BF16)
+        paired_product(last_block, z[1], sigmoid[1], slice(3 * P, N))
+        result([scalar_copy] * PACK, h_q[:1], dy_slot[0], out_1[0].rearrange("(c p) e -> c p e", c=PACK), "x_1", 0)
         scaled_product(dy_feat[1], w2_q[1], minus_cols[1], dh, 4)
-        result([scalar_copy] * PACK, x_slot[0], da, out_0[0].rearrange("(p t) f -> t p f", t=PACK), "x_2", 0)
-        result([scalar_copy] * PACK, h_q[1], dy_slot[1], out_1[1].rearrange("(c p) e -> c p e", c=PACK), "w1_0", 0)
+        result([scalar_copy] * PACK, x_slot[:1], da, out_0[0].rearrange("(p t) f -> t p f", t=PACK), "x_2", 0)
+        last_codes = big.tile([P, P], U32, name="last_codes", tag="minus_1", align_bytes=64)
+        blocks = [tuple(part_[:, c * P : (c + 1) * P] for part_ in h_second[:2]) + (E4M3,) for c in range(PACK - 1)]
+        blocks.extend(quantize(last_block, E4M3, "h_1_last", last_codes))
+        result([scalar_copy] * PACK, blocks, dy_slot[1], out_1[1].rearrange("(c p) e -> c p e", c=PACK), "w1_0", 0)
 
-        g = half(2, 1)
         da = operand("da_1", E5M2)
-        staged = big_tile("w1_1", "staged")
+        staged = big_tile("dy_2", "staged")
         rows = out_0[1].rearrange("(p t) f -> p t f", t=PACK)
-        for c, cols in enumerate((low, high)):
-            woven_product(g[:, c * part : (c + 1) * part], slope, dh, cols)
-        for c, cols in enumerate((low, high)):
-            quantize_part(g[:, c * part : (c + 1) * part], E5M2, da, cols)
-            for u in range(2):
-                acc = bank[4 + 2 * c + u]
-                for v in range(2):
-                    product(acc[:, v * N // 2 : (v + 1) * N // 2], x_slot[1], 2 * u + v, (da[0][:, cols], da[1][:, cols], E5M2))
-                piece = staged[:, (2 * c + u) * N : (2 * c + u + 1) * N]
-                (nc.scalar.copy if u == 1 else nc.vector.tensor_copy)(piece, acc[:])
-                nc.sync.dma_start(rows[:, 2 * u : 2 * u + 2, cols], piece.rearrange("p (v f) -> p v f", v=2))
+        g = half(1, 0)
+        pieces = (low, slice(N // 2, 3 * N // 4), slice(3 * N // 4, N))
+        free = list(range(4, 8))
+        for cols in pieces:
+            src = g[:, cols.start * PACK : cols.stop * PACK]
+            woven_product(src, slope, dh, cols)
+            quantize_part(src, E5M2, da, cols)
+        for cols in pieces:
+            n = cols.stop - cols.start
+            per_bank = N // n
+            for first in range(0, PACK, per_bank):
+                which = free.pop(0)
+                for v in range(per_bank):
+                    product(bank[which][:, v * n : (v + 1) * n], x_slot[1], first + v, (da[0][:, cols], da[1][:, cols], E5M2))
+                if len(free) == 1:
+                    piece = g[:, part:].bitcast(F32)
+                    vector_copy(piece, bank[which][:])
+                else:
+                    piece = staged[:, (which - 4) * N : (which - 3) * N]
+                    scalar_copy(piece, bank[which][:])
+                nc.sync.dma_start(rows[:, first : first + per_bank, cols], piece.rearrange("p (v f) -> p v f", v=per_bank))

@@ -136,16 +136,15 @@ def tile_attend_gxfull_sil_W_kernel(tc, xT, dyT, w1, w2, ts, tx, cf, offs, out_0
                 w1_raw[b][:].rearrange("p (j f) -> p j f", j=PACK)[:, :, cols].rearrange("p j (c i) -> p c j i", i=PACK),
             )
 
-        def round_w2(copy, b, rounded):
-            copy(rounded, w2_raw[b][:])
+        def round_w2(copy, b, rounded, cols=slice(0, PACK * N)):
+            copy(rounded, w2_raw[b][:, cols])
 
         def group_w2(copy, rounded, g, banks):
-            words = rounded.bitcast(F32)
             g_words = g.bitcast(F32)
             for side in range(2):
-                turned = bank[banks[side]]
+                turned, words = bank[banks[side]], rounded[side].bitcast(F32)
                 for k in range(PACK):
-                    first = (2 * side + k // 2) * 2 * P
+                    first = k // 2 * 2 * P
                     nc.tensor.transpose(turned[:, k * P : (k + 1) * P], words[:, first + k % 2 : first + 2 * P : 2], ident[:])
                 copy(
                     g_words[:, side * N : (side + 1) * N].rearrange("p (c f u) -> p c f u", c=2, u=2),
@@ -185,12 +184,12 @@ def tile_attend_gxfull_sil_W_kernel(tc, xT, dyT, w1, w2, ts, tx, cf, offs, out_0
                 turned[:].rearrange("s (k p) -> s p k", k=4),
             )
 
-        def scaled_product(stationary, moving, cols, dst, first):
-            for r in range(PACK):
+        def scaled_product(stationary, moving, cols, dst, first, places=range(PACK)):
+            for r in places:
                 acc = bank[first + r]
                 product(acc, stationary, r, moving)
                 nc.vector.scalar_tensor_tensor(
-                    dst[:, r * N : (r + 1) * N], acc[:], cols[:, r : r + 1], cf_row[:], ALU.mult, ALU.mult
+                    dst[:, r * N : (r + 1) * N], acc[:], cols[r], cf_row[:], ALU.mult, ALU.mult
                 )
 
         def woven(dst):
@@ -269,9 +268,10 @@ def tile_attend_gxfull_sil_W_kernel(tc, xT, dyT, w1, w2, ts, tx, cf, offs, out_0
         along_features(vector_copy, x_picked[0], half(0, 1))
         nc.vector.scalar_tensor_tensor(gates, ts_cols, 0.0, ts_cols, ALU.is_equal, ALU.add)
         nc.vector.tensor_tensor(txts_cols, tx_cols, ts_cols, ALU.mult)
+        first_cols = big.tile([P, 2], F32, name="first_cols", tag="first_cols", align_bytes=64)
+        nc.vector.tensor_tensor(first_cols[:], tx_cols[:, :2], ts_cols[:, :2], ALU.mult)
         along_features(scalar_copy, x_picked[1], half(1, 1))
-        early_codes = big.tile([P, N], U32, name="early_codes", tag="early_codes", align_bytes=64)
-        x_feat = [quantize(half(0, 1), E4M3, "x_feat_0", early_codes)[0]]
+        x_feat = [quantize(half(0, 1), E4M3, "x_feat_0")[0]]
         nc.vector.reciprocal(inverse, gates)
         group_w1(vector_copy, 0, half(0, 0))
         w1_q = [quantize(half(0, 0), E4M3, "w1_q_0")[0]]
@@ -279,8 +279,9 @@ def tile_attend_gxfull_sil_W_kernel(tc, xT, dyT, w1, w2, ts, tx, cf, offs, out_0
         x_feat.append(quantize(half(1, 1), E4M3, "x_feat_1", first_codes)[0])
         x_along_slots(2, 0)
         x_along_slots(3, 1)
-        w1_grouped = big.tile([P, PACK * N], BF16, name="w1_grouped", tag="w1_grouped", align_bytes=64)
-        group_w1(scalar_copy, 1, w1_grouped[:])
+        first_z = big_tile("tx", "first_z", (PACK + 1) * N)
+        w1_grouped = first_z[:, (PACK - 1) * N :].bitcast(BF16)
+        group_w1(scalar_copy, 1, w1_grouped)
         minus_cols = [big.tile([P, PACK], F32, name="minus_cols", tag="minus_%d" % b, align_bytes=64) for b in range(EXPERTS)]
         for b in range(EXPERTS):
             nc.scalar.activation(minus_cols[b][:], txts_cols[:, b * PACK : (b + 1) * PACK], ACT.Copy, scale=-1.0)
@@ -288,23 +289,29 @@ def tile_attend_gxfull_sil_W_kernel(tc, xT, dyT, w1, w2, ts, tx, cf, offs, out_0
         x_slot = quantize(pair[2][:], E4M3, "x_slot")
         low = slice(0, N // 2)
         whole, part = PACK * N, PACK * N // 2
-        after_slots = big_tile("ts", "after_slots", whole + part)
-        z = [after_slots[:, :whole], columns[:, :whole]]
-        rounded = after_slots[:, whole:].bitcast(BF16)
+        z = [first_z[:, :whole], columns[:, :whole]]
+        rounded = [big.tile([P, part], BF16, name="rounded", tag="ts", align_bytes=64)[:], first_z[:, whole:].bitcast(BF16)]
+
+        def by_place(cols, first=0):
+            return [cols[:, k : k + 1] for k in range(first, min(first + PACK, cols.shape[1]))]
+
         slope = pair[0][:].bitcast(F32)
         dy_both = held.tile([P, PACK, EXPERTS * N], BF16, name="dy_both", align_bytes=64)
         dy_picked = [dy_both[:, :, b * N : (b + 1) * N] for b in range(EXPERTS)]
-        round_w2(gpsimd_copy, 0, rounded)
-        scaled_product(x_feat[0], w1_q[0], txts_cols[:, :PACK], z[0], 4)
-        w1_codes = big.tile([P, N], U32, name="w1_codes", tag="early_codes", align_bytes=64)
-        w1_q.append(quantize(w1_grouped[:], E4M3, "w1_q_1", w1_codes)[0])
+        round_w2(gpsimd_copy, 0, rounded[0], slice(0, part))
+        scaled_product(x_feat[0], w1_q[0], by_place(first_cols)[:2] + by_place(txts_cols)[2:], z[0], 4, range(PACK - 1))
+        w1_codes = big.tile([P, N], U32, name="w1_codes", tag="first_cols", align_bytes=64)
+        w1_q.append(quantize(w1_grouped, E4M3, "w1_q_1", w1_codes)[0])
+        scaled_product(x_feat[0], w1_q[0], by_place(txts_cols), z[0], 4, [PACK - 1])
+        round_w2(gpsimd_copy, 0, rounded[1], slice(part, whole))
         sigmoid = [big_tile("x_0", "sigmoid")]
         of_z(ACT.Sigmoid, sigmoid[0], 0)
-        scalar_gather(dy_both[:, 0], dy_plane[0][:].indirect(offsets[:]))
-        first_block = big.tile([P, N], BF16, name="first_block", tag="w1_grouped", align_bytes=64)
+        gather(scalar_gather, dy_plane, dy_picked, 0, 0)
+        first_block = big.tile([P, N], BF16, name="first_block", tag="first_block", align_bytes=64)
         paired_product(first_block[:], z[0], sigmoid[0], slice(0, P))
-        scaled_product(x_feat[1], w1_q[1], txts_cols[:, PACK:], z[1], 0)
-        sigmoid.append(big_tile("dy_0", "sigmoid"))
+        scaled_product(x_feat[1], w1_q[1], by_place(txts_cols, PACK), z[1], 0)
+        gather(vector_copy, dy_plane, dy_picked, 0, 1)
+        sigmoid.append(big_tile("w1_1", "sigmoid"))
         of_z(ACT.Sigmoid, sigmoid[1], 1)
         nc.scalar.activation(inverse, inverse, ACT.Copy, scale=-1.0)
         hidden = big.tile([P, 3 * N], BF16, name="hidden", tag="first_codes", align_bytes=64)
@@ -328,15 +335,15 @@ def tile_attend_gxfull_sil_W_kernel(tc, xT, dyT, w1, w2, ts, tx, cf, offs, out_0
         after_slope = big_tile("dy_1", "after_slope", whole + part)
         dh, late_rounded = after_slope[:, :whole], after_slope[:, whole:].bitcast(BF16)
         round_w2(gpsimd_copy, 1, late_rounded)
-        scaled_product(dy_feat[0], w2_q[0], minus_cols[0], dh, 4)
+        scaled_product(dy_feat[0], w2_q[0], by_place(minus_cols[0]), dh, 4)
         for t in (2, 3):
             gather(scalar_gather, dy_plane, dy_picked, t, 1)
         for side in range(2):
             dy_along_slots(scalar_copy, dy_picked[0], half(3, 0), side, 2 + side)
         along_features(scalar_copy, dy_picked[1], half(1, 0))
-        mirrored.append(big_tile("ts", "mirrored"))
+        mirrored.append(big_tile("tx", "mirrored"))
         of_z(ACT.Silu, mirrored[1], 1)
-        group_w2(scalar_copy, late_rounded, half(1, 1), (4, 5))
+        group_w2(scalar_copy, [late_rounded[:, :part], late_rounded[:, part:]], half(1, 1), (4, 5))
         late_codes = big.tile([P, 2 * N], U32, name="late_codes", tag="minus_0", align_bytes=64)
         dy_slot = [quantize(half(3, 0), E5M2, "dy_slot_0", late_codes[:, :N])[0]]
         gradient = big.tile([P, whole], BF16, name="gradient", tag="first_codes", align_bytes=64)
@@ -348,11 +355,11 @@ def tile_attend_gxfull_sil_W_kernel(tc, xT, dyT, w1, w2, ts, tx, cf, offs, out_0
             dy_along_slots(scalar_copy, dy_picked[1], half(3, 1), side, 6 + side)
         dy_slot.append(quantize(half(3, 1), E5M2, "dy_slot_1")[0])
         slope_of(1, slope)
-        after_slope = big_tile("ts", "after_slope", whole + N // 2)
+        after_slope = big_tile("tx", "after_slope", whole + N // 2)
         dh, last_block = after_slope[:, :whole], after_slope[:, whole:].bitcast(BF16)
         paired_product(last_block, z[1], sigmoid[1], slice(3 * P, N))
         result([scalar_copy] * PACK, h_q[:1], dy_slot[0], out_1[0].rearrange("(c p) e -> c p e", c=PACK), "x_1", 0)
-        scaled_product(dy_feat[1], w2_q[1], minus_cols[1], dh, 4)
+        scaled_product(dy_feat[1], w2_q[1], by_place(minus_cols[1]), dh, 4)
         result([scalar_copy] * PACK, x_slot[:1], da, out_0[0].rearrange("(p t) f -> t p f", t=PACK), "x_2", 0)
         last_codes = big.tile([P, P], U32, name="last_codes", tag="minus_1", align_bytes=64)
         blocks = [tuple(part_[:, c * P : (c + 1) * P] for part_ in h_second[:2]) + (E4M3,) for c in range(PACK - 1)]
@@ -363,7 +370,7 @@ def tile_attend_gxfull_sil_W_kernel(tc, xT, dyT, w1, w2, ts, tx, cf, offs, out_0
         staged = big_tile("dy_2", "staged")
         rows = out_0[1].rearrange("(p t) f -> p t f", t=PACK)
         g = half(1, 0)
-        pieces = (low, slice(N // 2, 3 * N // 4), slice(3 * N // 4, N))
+        pieces = [slice(c * P, (c + 1) * P) for c in range(PACK)]
         free = list(range(4, 8))
         for cols in pieces:
             src = g[:, cols.start * PACK : cols.stop * PACK]

@@ -17,8 +17,9 @@ ACT = mybir.ActivationFunctionType
 P = 128
 PACK = 4
 N = 512
+WIDE = PACK * N
 EXPERTS = 2
-TOKENS = 2048
+KIB = 1024
 FLOPS = 4 * 2 * EXPERTS * N * N * N
 
 
@@ -26,35 +27,36 @@ def tile_attend_gxfull_sil_W_kernel(tc, xT, dyT, w1, w2, ts, tx, cf, offs, out_0
     nc = tc.nc
     with ExitStack() as ctx:
         held = ctx.enter_context(tc.tile_pool(name="held", bufs=1))
-        big = ctx.enter_context(tc.tile_pool(name="big", bufs=1))
+        arena = ctx.enter_context(tc.tile_pool(name="arena", bufs=1))
         psum = ctx.enter_context(tc.psum_pool(name="psum", bufs=1))
 
-        def big_tile(slot, name, width=PACK * N):
-            return big.tile([P, width], F32, name=name, tag=slot, align_bytes=64)
+        def placed(name, at, dtype=F32, width=WIDE):
+            return arena.tile([P, width], dtype, name=name, offset=int(at * KIB), align_bytes=64)
+
+        X_AT, DY_AT, W1_AT, W2_AT, TS_AT, TX_AT, XB_AT, FREE_AT = 0, 32, 64, 80, 96, 104, 112, 120
 
         bank = [psum.tile([P, N], F32, name="bank_%d" % j) for j in range(8)]
-        pair = {j: held.tile([P, 2 * PACK * N], BF16, name="pair_%d" % j, align_bytes=64) for j in (0, 1, 3)}
+        vector_copy, scalar_copy, gpsimd_copy = nc.vector.tensor_copy, nc.scalar.copy, nc.gpsimd.tensor_copy
 
-        def half(j, k):
-            return pair[j][:, k * PACK * N : (k + 1) * PACK * N]
+        def operand(name, fmt, at=None):
+            if at is None:
+                codes = held.tile([P, N], U32, name=name + "_codes", align_bytes=64)
+            else:
+                codes = placed(name + "_codes", at, U32, N)
+            scales = held.tile([P, N], U8, name=name + "_scales", align_bytes=64)
+            return codes[:], scales[:], fmt
 
-        def quantize(src, fmt, name, codes=None):
-            width = src.shape[1] // PACK
-            if codes is None:
-                codes = held.tile([P, width], U32, name=name + "_codes", align_bytes=64)
-            scales = held.tile([P, width], U8, name=name + "_scales", align_bytes=64)
-            nc.vector.quantize_mx(out=codes[:].bitcast(fmt), scales=scales[:], in_=src)
-            step = min(width, N)
-            return [(codes[:, k : k + step], scales[:, k : k + step], fmt) for k in range(0, width, step)]
+        def quantize(src, dst, cols=slice(0, N)):
+            nc.vector.quantize_mx(out=dst[0][:, cols].bitcast(dst[2]), scales=dst[1][:, cols], in_=src)
 
-        def product(dst, stationary, j, moving):
-            cols = slice(j * P, (j + 1) * P)
+        def product(dst, stationary, j, moving, cols=slice(0, N)):
+            rows = slice(j * P, (j + 1) * P)
             nc.tensor.matmul_mx(
-                out=dst[:],
-                lhsT=stationary[0][:, cols].bitcast(stationary[2]),
-                lhsT_scale=stationary[1][:, cols],
-                rhs=moving[0].bitcast(moving[2]),
-                rhs_scale=moving[1],
+                out=dst,
+                lhsT=stationary[0][:, rows].bitcast(stationary[2]),
+                lhsT_scale=stationary[1][:, rows],
+                rhs=moving[0][:, cols].bitcast(moving[2]),
+                rhs_scale=moving[1][:, cols],
                 start=True,
                 stop=True,
             )
@@ -65,138 +67,138 @@ def tile_attend_gxfull_sil_W_kernel(tc, xT, dyT, w1, w2, ts, tx, cf, offs, out_0
         def listed(window, b):
             return window[:].indirect(offsets[:, b * N // 16 : (b + 1) * N // 16])
 
-        ts_win = big_tile("ts", "ts_win")
-        tx_win = big_tile("tx", "tx_win")
+        def scalar_gather(dst, src):
+            nc.scalar.activation(dst, src, ACT.Copy)
+
+        ts_win, tx_win = placed("ts_win", TS_AT), placed("tx_win", TX_AT)
         warm = held.tile([P, 1], F32, name="warm")
-        nc.vector.memset(warm[:, 0:1], 0.0)
-        nc.vector.memset(tx_win[0 : P - 1, :].bitcast(I32), 0)
+        nc.vector.memset(warm[:], 0.0)
+        nc.gpsimd.memset(tx_win[0 : P - 1, :].bitcast(I32), 0)
         nc.vector.memset(ts_win[0 : P - 1, :].bitcast(I32), 0)
         cf_cols = held.tile([P, PACK], F32, name="cf_cols")
         nc.scalar.dma_start(tx_win[P - 1 : P, :], tx[0:1, :])
         nc.scalar.dma_start(ts_win[P - 1 : P, :], ts[0:1, :])
         nc.scalar.dma_start(cf_cols[:], cf.rearrange("(p j) o -> p (j o)", j=PACK))
         warmed = held.tile([P, 1], F32, name="warmed")
-        nc.scalar.activation(warmed[:], warm[:, 0:1], ACT.Sigmoid)
+        nc.scalar.activation(warmed[:], warm[:], ACT.Sigmoid)
         ident = held.tile([P, P], F32, name="ident")
         make_identity(nc, ident[:])
 
-        w1_raw = [big_tile("w1_%d" % b, "w1_raw") for b in range(EXPERTS)]
-        w2_raw = [big_tile("w2_%d" % b, "w2_raw") for b in range(EXPERTS)]
-        x_plane = [big_tile("x_%d" % t, "x_plane") for t in range(PACK)]
-        dy_plane = [big_tile("dy_%d" % t, "dy_plane") for t in range(PACK)]
+        x_plane = [placed("x_plane", X_AT + 8 * t) for t in range(PACK)]
+        dy_plane = [placed("dy_plane", DY_AT + 8 * t) for t in range(PACK)]
+        w1_raw = [placed("w1_raw", W1_AT + 8 * b) for b in range(EXPERTS)]
+        w2_raw = [placed("w2_raw", W2_AT + 8 * b) for b in range(EXPERTS)]
 
-        for t in range(PACK):
-            nc.sync.dma_start(x_plane[t][:], xT.rearrange("(p t) n -> t p n", t=PACK)[t])
+        def load_plane(planes, src, t):
+            nc.sync.dma_start(planes[t][:], src.rearrange("(p t) n -> t p n", t=PACK)[t])
 
         def load_w1(b):
             nc.sync.dma_start(w1_raw[b][:], w1[b].rearrange("(p j) f -> p (j f)", j=PACK))
-
-        def load_dy(t):
-            nc.sync.dma_start(dy_plane[t][:], dyT.rearrange("(p t) n -> t p n", t=PACK)[t])
 
         def load_w2(b):
             nc.sync.dma_start(
                 w2_raw[b][:].rearrange("p (c e) -> p c e", c=PACK), w2[b].rearrange("(c p) e -> p c e", c=PACK)
             )
 
+        for t in range(PACK):
+            load_plane(x_plane, xT, t)
         load_w1(0)
         load_w1(1)
+        load_plane(dy_plane, dyT, 0)
+        load_plane(dy_plane, dyT, 1)
         load_w2(0)
-        for t in range(PACK):
-            load_dy(t)
+        load_plane(dy_plane, dyT, 2)
+        load_plane(dy_plane, dyT, 3)
         load_w2(1)
 
-        vector_copy, scalar_copy, gpsimd_copy = nc.vector.tensor_copy, nc.scalar.copy, nc.gpsimd.tensor_copy
+        def gather_tokens(gather, window, name):
+            picked = held.tile([P, EXPERTS * N], F32, name=name)
+            gather(picked[:], window[:].indirect(offsets[:]))
+            dealt = held.tile([P, EXPERTS * N], F32, name=name + "_dealt")
+            gpsimd_copy(
+                dealt[:].rearrange("p (b r c i) -> p b c r i", b=EXPERTS, r=PACK, i=PACK),
+                picked[:].rearrange("p (b c i r) -> p b c r i", b=EXPERTS, r=PACK, i=PACK),
+            )
+            return dealt
 
-        def scalar_gather(dst, src):
-            nc.scalar.activation(dst, src, ACT.Copy)
-
-        def grouped(name):
-            return held.tile([P, PACK * N], BF16, name=name, align_bytes=64)[:]
-
-        def gather_tokens(window, name):
-            picked = held.tile([P, EXPERTS * N], F32, name=name + "_picked")
-            scalar_gather(picked[:], window[:].indirect(offsets[:]))
-            return picked
-
-        def turn_tokens(picked, banks):
+        def token_columns(dealt, cols, banks):
             for b in range(EXPERTS):
                 for r in range(PACK):
-                    nc.tensor.transpose(
-                        bank[banks[b]][:, r * P : (r + 1) * P], picked[:, b * N + r : (b + 1) * N : PACK], ident[:]
-                    )
+                    first = b * N + r * P
+                    nc.tensor.transpose(bank[banks[b]][:, r * P : (r + 1) * P], dealt[:, first : first + P], ident[:])
+                scalar_copy(cols[:, b * PACK : (b + 1) * PACK], bank[banks[b]][:, P - 1 : N : P])
 
-        def token_columns(cols, banks):
-            for b in range(EXPERTS):
-                nc.scalar.copy(cols[:, b * PACK : (b + 1) * PACK], bank[banks[b]][:, P - 1 : N : P])
-
-        def group_w1(copy, b, g, cols=slice(0, N)):
+        def group_w1(copy, b, g, cols, run=PACK):
             copy(
-                g[:, cols.start * PACK : cols.stop * PACK].rearrange("p (c i j) -> p c j i", i=PACK, j=PACK),
-                w1_raw[b][:].rearrange("p (j f) -> p j f", j=PACK)[:, :, cols].rearrange("p j (c i) -> p c j i", i=PACK),
+                g[:, cols.start * PACK : cols.stop * PACK].rearrange("p (c i j) -> p c j i", i=run, j=PACK),
+                w1_raw[b][:].rearrange("p (j f) -> p j f", j=PACK)[:, :, cols].rearrange("p j (c i) -> p c j i", i=run),
             )
 
-        def round_w2(copy, b, rounded, cols=slice(0, PACK * N)):
-            copy(rounded, w2_raw[b][:, cols])
-
-        def group_w2(copy, rounded, g, banks):
-            g_words = g.bitcast(F32)
+        def turn_w2(rounded, g, banks):
+            g_words, words = g[:].bitcast(F32), rounded[:].bitcast(F32)
             for side in range(2):
-                turned, words = bank[banks[side]], rounded[side].bitcast(F32)
+                turned = bank[banks[side]]
                 for k in range(PACK):
-                    first = k // 2 * 2 * P
+                    first = (2 * side + k // 2) * 2 * P
                     nc.tensor.transpose(turned[:, k * P : (k + 1) * P], words[:, first + k % 2 : first + 2 * P : 2], ident[:])
-                copy(
+                scalar_copy(
                     g_words[:, side * N : (side + 1) * N].rearrange("p (c f u) -> p c f u", c=2, u=2),
                     turned[:].rearrange("p (c u f) -> p c f u", c=2, u=2),
                 )
 
-        def gather(copy, planes, picked, t, b):
-            copy(picked[b][:, t], listed(planes[t], b))
-
-        def along_features(copy, picked, g):
+        def along_features(copy, picked, g, places=slice(0, PACK)):
             copy(
-                g.rearrange("p (r s i t) -> p s r i t", r=PACK, i=2, t=PACK),
-                picked.rearrange("p t (s i r) -> p s r i t", r=PACK, i=2),
+                g[:, places.start * N : places.stop * N].rearrange("p (r s i t) -> p s r i t", s=P // 2, i=2, t=PACK),
+                picked.rearrange("p t (s i r) -> p s r i t", r=PACK, i=2)[:, :, places],
             )
 
-        def x_along_slots(t, which):
+        def x_along_slots(copy, t, which):
             words = x_both[:, t].bitcast(F32)
             turned = bank[which]
             for b in range(EXPERTS):
                 for v in range(2):
                     k = 2 * b + v
                     nc.tensor.transpose(turned[:, k * P : (k + 1) * P], words[:, b * 256 + v : (b + 1) * 256 : 2], ident[:])
-            nc.scalar.copy(
-                pair[2][:].bitcast(F32).rearrange("s (b t p v) -> s t b p v", b=EXPERTS, t=PACK, v=2)[:, t],
+            copy(
+                x_turned[t // 2][:].bitcast(F32).rearrange("s (t b p v) -> s t b p v", t=2, b=EXPERTS, v=2)[:, t % 2],
                 turned[:].rearrange("s (b v p) -> s b p v", b=EXPERTS, v=2),
             )
 
-        def dy_along_slots(copy, picked, g, side, which):
-            turned = bank[which]
-            for tt in range(2):
-                words = picked[:, 2 * side + tt].bitcast(F32)
-                for v in range(2):
-                    k = 2 * tt + v
-                    nc.tensor.transpose(turned[:, k * P : (k + 1) * P], words[:, v::2], ident[:])
-            copy(
-                g.bitcast(F32).rearrange("s (p h k) -> s h p k", h=2, k=4)[:, side],
-                turned[:].rearrange("s (k p) -> s p k", k=4),
-            )
+        def turn_dy(picked, banks):
+            for side in range(2):
+                for tt in range(2):
+                    words = picked[:, 2 * side + tt].bitcast(F32)
+                    for v in range(2):
+                        k = 2 * tt + v
+                        nc.tensor.transpose(bank[banks[side]][:, k * P : (k + 1) * P], words[:, v::2], ident[:])
 
-        def scaled_product(stationary, moving, cols, dst, first, places=range(PACK)):
-            for r in places:
-                acc = bank[first + r]
-                product(acc, stationary, r, moving)
+        def dy_along_slots(copy, g, banks):
+            for side in range(2):
+                copy(
+                    g[:].bitcast(F32).rearrange("s (p h k) -> s h p k", h=2, k=4)[:, side],
+                    bank[banks[side]][:].rearrange("s (k p) -> s p k", k=4),
+                )
+
+        def products(stationary, moving):
+            for r in range(PACK):
+                product(bank[r][:], stationary, r, moving)
+
+        def scaled(dst, cols):
+            for r in range(PACK):
                 nc.vector.scalar_tensor_tensor(
-                    dst[:, r * N : (r + 1) * N], acc[:], cols[r], cf_row[:], ALU.mult, ALU.mult
+                    dst[:, r * N : (r + 1) * N], bank[r][:], cols[:, r : r + 1], cf_row[:], ALU.mult, ALU.mult
                 )
 
         def woven(dst):
             return dst.rearrange("p (c i r) -> p c r i", i=PACK, r=PACK)
 
-        def strands(src, cols):
+        def strands(src, cols=slice(0, N)):
             return src[:].rearrange("p (r n) -> p r n", r=PACK)[:, :, cols].rearrange("p r (c i) -> p c r i", i=PACK)
+
+        def of_z(func, dst, b, scale):
+            for r in range(PACK):
+                cols = slice(r * N, (r + 1) * N)
+                nc.scalar.activation(dst[:, cols], y[b][:, cols], func, scale=scale[:, b * PACK + r : b * PACK + r + 1])
 
         def woven_product(g, left, right, cols=slice(0, N)):
             nc.vector.tensor_tensor(woven(g), strands(left, cols), strands(right, cols), ALU.mult)
@@ -208,185 +210,188 @@ def tile_attend_gxfull_sil_W_kernel(tc, xT, dyT, w1, w2, ts, tx, cf, offs, out_0
             )
             nc.gpsimd.tensor_tensor(g.rearrange("p (c i r) -> p c r i", i=2, r=PACK), left, right, ALU.mult)
 
-        def quantize_part(src, fmt, whole, cols):
-            nc.vector.quantize_mx(out=whole[0][:, cols].bitcast(fmt), scales=whole[1][:, cols], in_=src)
+        def slope_of(dst, b):
+            nc.vector.scalar_tensor_tensor(dst[:], mirrored[b][:], 1.0, sigmoid[b][:], ALU.subtract, ALU.mult)
 
-        def operand(name, fmt):
-            codes = held.tile([P, N], U32, name=name + "_codes", align_bytes=64)
-            scales = held.tile([P, N], U8, name=name + "_scales", align_bytes=64)
-            return codes[:], scales[:], fmt
-
-        def result(copies, stationary, moving, rows, slot, first):
-            staged = big_tile(slot, "staged")
+        def result(stationary, moving, rows, staged, banks):
             for j in range(PACK):
-                acc = bank[first + j]
-                per_part = PACK // len(stationary)
-                product(acc, stationary[j // per_part], j % per_part, moving)
-                copies[j](staged[:, j * N : (j + 1) * N], acc[:])
+                acc = bank[banks[j]]
+                product(acc[:], stationary[j][0], stationary[j][1], moving)
+                scalar_copy(staged[:, j * N : (j + 1) * N], acc[:])
                 nc.sync.dma_start(rows[j], staged[:, j * N : (j + 1) * N])
 
-        def of_z(func, dst, b):
-            for r in range(PACK):
-                cols = slice(r * N, (r + 1) * N)
-                k = b * PACK + r
-                nc.scalar.activation(dst[:, cols], z[b][:, cols], func, scale=inverse[:, k : k + 1])
-
-        def slope_of(b, slope):
-            nc.vector.scalar_tensor_tensor(slope, mirrored[b][:], 1.0, sigmoid[b][:], ALU.subtract, ALU.mult)
-
-        tx_picked = gather_tokens(tx_win, "tx")
-        ts_picked = gather_tokens(ts_win, "ts")
-        turn_tokens(tx_picked, (0, 1))
-        pair.setdefault(2, big.tile([P, 2 * PACK * N], BF16, name="pair_2", tag="ts", align_bytes=64))
-
-
-        cf_row = held.tile([P, N], F32, name="cf_row")
-        spread = bank[4]
-        for j in range(PACK):
-            nc.tensor.transpose(spread[:, j * P : (j + 1) * P], cf_cols[:, j : j + 1].to_broadcast([P, P]), ident[:])
-        nc.scalar.copy(cf_row[:].rearrange("p (m j) -> p m j", j=PACK), spread[:].rearrange("p (j m) -> p m j", j=PACK))
-
-        x_both = held.tile([P, PACK, EXPERTS * N], BF16, name="x_both", align_bytes=64)
-        x_picked = [x_both[:, :, b * N : (b + 1) * N] for b in range(EXPERTS)]
-        for t in range(2):
-            vector_copy(x_both[:, t], x_plane[t][:].indirect(offsets[:]))
-        gather(vector_copy, x_plane, x_picked, 2, 0)
-        x_along_slots(0, 5)
-        x_along_slots(1, 2)
-        turn_tokens(ts_picked, (2, 3))
-        gather(scalar_gather, x_plane, x_picked, 2, 1)
-        gather(vector_copy, x_plane, x_picked, 3, 0)
-        gather(scalar_gather, x_plane, x_picked, 3, 1)
-
+        tx_dealt = gather_tokens(scalar_gather, tx_win, "tx_picked")
+        ts_dealt = gather_tokens(vector_copy, ts_win, "ts_picked")
         width = EXPERTS * PACK
-        columns = big_tile("x_3", "columns", PACK * N + 5 * width)
-        tx_cols, ts_cols, gates, txts_cols, inverse = (
-            columns[:, PACK * N + k * width : PACK * N + (k + 1) * width] for k in range(5)
-        )
-        token_columns(tx_cols, (0, 1))
-        token_columns(ts_cols, (2, 3))
-        along_features(vector_copy, x_picked[0], half(0, 1))
-        nc.vector.scalar_tensor_tensor(gates, ts_cols, 0.0, ts_cols, ALU.is_equal, ALU.add)
-        nc.vector.tensor_tensor(txts_cols, tx_cols, ts_cols, ALU.mult)
-        first_cols = big.tile([P, 2], F32, name="first_cols", tag="first_cols", align_bytes=64)
-        nc.vector.tensor_tensor(first_cols[:], tx_cols[:, :2], ts_cols[:, :2], ALU.mult)
-        along_features(scalar_copy, x_picked[1], half(1, 1))
-        x_feat = [quantize(half(0, 1), E4M3, "x_feat_0")[0]]
+        tx_cols = held.tile([P, width], F32, name="tx_cols")
+        ts_cols = held.tile([P, width], F32, name="ts_cols")
+        cf_row = held.tile([P, N], F32, name="cf_row")
+        for j in range(PACK):
+            nc.tensor.transpose(bank[2][:, j * P : (j + 1) * P], cf_cols[:, j : j + 1].to_broadcast([P, P]), ident[:])
+
+        x_both = placed("x_both", TS_AT, BF16, 2 * WIDE)[:].rearrange("p (t n) -> p t n", t=PACK)
+        x_picked = [x_both[:, :, b * N : (b + 1) * N] for b in range(EXPERTS)]
+        x_turned = [placed("x_turned", FREE_AT, BF16)]
+        x_grouped = [placed("x_grouped", FREE_AT + 4, BF16)]
+        w1_grouped = placed("w1_grouped", FREE_AT + 16, BF16)
+
+        def gather_x(t):
+            vector_copy(x_picked[0][:, t], listed(x_plane[t], 0))
+            scalar_gather(x_picked[1][:, t], listed(x_plane[t], 1))
+
+        gather_x(0)
+        scalar_copy(cf_row[:].rearrange("p (m j) -> p m j", j=PACK), bank[2][:].rearrange("p (j m) -> p m j", j=PACK))
+        gather_x(1)
+        x_along_slots(scalar_copy, 0, 4)
+        token_columns(tx_dealt, tx_cols, (0, 1))
+        x_along_slots(scalar_copy, 1, 5)
+        token_columns(ts_dealt, ts_cols, (2, 3))
+        gather_x(2)
+        columns = held.tile([P, 5 * width], F32, name="columns")
+        both, minus_both, gates, inverse, minus_inverse = (columns[:, k * width : (k + 1) * width] for k in range(5))
+        nc.vector.scalar_tensor_tensor(gates, ts_cols[:], 0.0, ts_cols[:], ALU.is_equal, ALU.add)
+        nc.vector.tensor_tensor(both, tx_cols[:], ts_cols[:], ALU.mult)
         nc.vector.reciprocal(inverse, gates)
-        group_w1(vector_copy, 0, half(0, 0))
-        w1_q = [quantize(half(0, 0), E4M3, "w1_q_0")[0]]
-        first_codes = big.tile([P, N], U32, name="first_codes", tag="first_codes", align_bytes=64)
-        x_feat.append(quantize(half(1, 1), E4M3, "x_feat_1", first_codes)[0])
-        x_along_slots(2, 0)
-        x_along_slots(3, 1)
-        first_z = big_tile("tx", "first_z", (PACK + 1) * N)
-        w1_grouped = first_z[:, (PACK - 1) * N :].bitcast(BF16)
-        group_w1(scalar_copy, 1, w1_grouped)
-        minus_cols = [big.tile([P, PACK], F32, name="minus_cols", tag="minus_%d" % b, align_bytes=64) for b in range(EXPERTS)]
-        for b in range(EXPERTS):
-            nc.scalar.activation(minus_cols[b][:], txts_cols[:, b * PACK : (b + 1) * PACK], ACT.Copy, scale=-1.0)
+        nc.vector.tensor_scalar(minus_both, both, -1.0, None, ALU.mult)
+        nc.vector.tensor_scalar(minus_inverse, inverse, -1.0, None, ALU.mult)
+        x_slot = [operand("x_slot_0", E4M3)]
+        quantize(x_turned[0][:], x_slot[0])
+        gather_x(3)
+        along_features(vector_copy, x_picked[0], x_grouped[0], slice(0, PACK - 1))
+        along_features(scalar_copy, x_picked[0], x_grouped[0], slice(PACK - 1, PACK))
+        low, high = slice(0, N // 2), slice(N // 2, N)
+        group_w1(scalar_copy, 0, w1_grouped, high)
+        group_w1(vector_copy, 0, w1_grouped, low)
+        x_feat = [operand("x_feat_0", E4M3)]
+        w1_q = [operand("w1_q_0", E4M3)]
+        quantize(x_grouped[0][:], x_feat[0])
+        x_grouped.append(placed("x_grouped", W1_AT, BF16))
+        along_features(scalar_copy, x_picked[1], x_grouped[1])
+        quantize(w1_grouped[:], w1_q[0])
 
-        x_slot = quantize(pair[2][:], E4M3, "x_slot")
-        low = slice(0, N // 2)
-        whole, part = PACK * N, PACK * N // 2
-        z = [first_z[:, :whole], columns[:, :whole]]
-        rounded = [big.tile([P, part], BF16, name="rounded", tag="ts", align_bytes=64)[:], first_z[:, whole:].bitcast(BF16)]
+        def planes(name, at):
+            return placed(name, at, BF16)[:].rearrange("p (t n) -> p t n", t=PACK)
 
-        def by_place(cols, first=0):
-            return [cols[:, k : k + 1] for k in range(first, min(first + PACK, cols.shape[1]))]
+        def of_expert(cols, b):
+            return cols[:, b * PACK : (b + 1) * PACK]
 
-        slope = pair[0][:].bitcast(F32)
-        dy_both = held.tile([P, PACK, EXPERTS * N], BF16, name="dy_both", align_bytes=64)
-        dy_picked = [dy_both[:, :, b * N : (b + 1) * N] for b in range(EXPERTS)]
-        round_w2(gpsimd_copy, 0, rounded[0], slice(0, part))
-        scaled_product(x_feat[0], w1_q[0], by_place(first_cols)[:2] + by_place(txts_cols)[2:], z[0], 4, range(PACK - 1))
-        w1_codes = big.tile([P, N], U32, name="w1_codes", tag="first_cols", align_bytes=64)
-        w1_q.append(quantize(w1_grouped, E4M3, "w1_q_1", w1_codes)[0])
-        scaled_product(x_feat[0], w1_q[0], by_place(txts_cols), z[0], 4, [PACK - 1])
-        round_w2(gpsimd_copy, 0, rounded[1], slice(part, whole))
-        sigmoid = [big_tile("x_0", "sigmoid")]
-        of_z(ACT.Sigmoid, sigmoid[0], 0)
-        gather(scalar_gather, dy_plane, dy_picked, 0, 0)
-        first_block = big.tile([P, N], BF16, name="first_block", tag="first_block", align_bytes=64)
-        paired_product(first_block[:], z[0], sigmoid[0], slice(0, P))
-        scaled_product(x_feat[1], w1_q[1], by_place(txts_cols, PACK), z[1], 0)
-        gather(vector_copy, dy_plane, dy_picked, 0, 1)
-        sigmoid.append(big_tile("w1_1", "sigmoid"))
-        of_z(ACT.Sigmoid, sigmoid[1], 1)
-        nc.scalar.activation(inverse, inverse, ACT.Copy, scale=-1.0)
-        hidden = big.tile([P, 3 * N], BF16, name="hidden", tag="first_codes", align_bytes=64)
-        woven_product(hidden[:], z[0], sigmoid[0], slice(P, N))
-        group_w2(scalar_copy, rounded, half(1, 1), (0, 1))
-        scalar_gather(dy_both[:, 1], dy_plane[1][:].indirect(offsets[:]))
-        gather(vector_copy, dy_plane, dy_picked, 2, 0)
-        h_q = [operand("h_0", E4M3)]
-        quantize_part(first_block[:], E4M3, h_q[0], slice(0, P))
-        quantize_part(hidden[:], E4M3, h_q[0], slice(P, N))
-        woven_product(half(1, 0)[:, : 3 * N], z[1], sigmoid[1], slice(0, 3 * P))
-        gather(vector_copy, dy_plane, dy_picked, 3, 0)
-        mirrored = [big_tile("dy_1", "mirrored")]
-        of_z(ACT.Silu, mirrored[0], 0)
-        h_second = operand("h_1", E4M3)
-        quantize_part(half(1, 0)[:, : 3 * N], E4M3, h_second, slice(0, 3 * P))
-        along_features(vector_copy, dy_picked[0], half(0, 0))
-        w2_q = [quantize(half(1, 1), E4M3, "w2_0")[0]]
-        dy_feat = [quantize(half(0, 0), E5M2, "dy_feat_0")[0]]
-        slope_of(0, slope)
-        after_slope = big_tile("dy_1", "after_slope", whole + part)
-        dh, late_rounded = after_slope[:, :whole], after_slope[:, whole:].bitcast(BF16)
-        round_w2(gpsimd_copy, 1, late_rounded)
-        scaled_product(dy_feat[0], w2_q[0], by_place(minus_cols[0]), dh, 4)
-        for t in (2, 3):
-            gather(scalar_gather, dy_plane, dy_picked, t, 1)
-        for side in range(2):
-            dy_along_slots(scalar_copy, dy_picked[0], half(3, 0), side, 2 + side)
-        along_features(scalar_copy, dy_picked[1], half(1, 0))
-        mirrored.append(big_tile("tx", "mirrored"))
-        of_z(ACT.Silu, mirrored[1], 1)
-        group_w2(scalar_copy, [late_rounded[:, :part], late_rounded[:, part:]], half(1, 1), (4, 5))
-        late_codes = big.tile([P, 2 * N], U32, name="late_codes", tag="minus_0", align_bytes=64)
-        dy_slot = [quantize(half(3, 0), E5M2, "dy_slot_0", late_codes[:, :N])[0]]
-        gradient = big.tile([P, whole], BF16, name="gradient", tag="first_codes", align_bytes=64)
-        woven_product(gradient[:], slope, dh)
-        dy_feat.append(quantize(half(1, 0), E5M2, "dy_feat_1", late_codes[:, N:])[0])
-        da = quantize(gradient[:], E5M2, "da_0")[0]
-        w2_q.append(quantize(half(1, 1), E4M3, "w2_1")[0])
-        for side in range(2):
-            dy_along_slots(scalar_copy, dy_picked[1], half(3, 1), side, 6 + side)
-        dy_slot.append(quantize(half(3, 1), E5M2, "dy_slot_1")[0])
-        slope_of(1, slope)
-        after_slope = big_tile("tx", "after_slope", whole + N // 2)
-        dh, last_block = after_slope[:, :whole], after_slope[:, whole:].bitcast(BF16)
-        paired_product(last_block, z[1], sigmoid[1], slice(3 * P, N))
-        result([scalar_copy] * PACK, h_q[:1], dy_slot[0], out_1[0].rearrange("(c p) e -> c p e", c=PACK), "x_1", 0)
-        scaled_product(dy_feat[1], w2_q[1], by_place(minus_cols[1]), dh, 4)
-        result([scalar_copy] * PACK, x_slot[:1], da, out_0[0].rearrange("(p t) f -> t p f", t=PACK), "x_2", 0)
-        last_codes = big.tile([P, P], U32, name="last_codes", tag="minus_1", align_bytes=64)
-        blocks = [tuple(part_[:, c * P : (c + 1) * P] for part_ in h_second[:2]) + (E4M3,) for c in range(PACK - 1)]
-        blocks.extend(quantize(last_block, E4M3, "h_1_last", last_codes))
-        result([scalar_copy] * PACK, blocks, dy_slot[1], out_1[1].rearrange("(c p) e -> c p e", c=PACK), "w1_0", 0)
+        y = [placed("y", X_AT + 8 - 8 * b) for b in range(EXPERTS)]
+        sigmoid = [placed("sigmoid", XB_AT - 8 * b) for b in range(EXPERTS)]
+        x_turned.append(placed("x_turned", W1_AT + 4, BF16))
+        x_along_slots(vector_copy, 2, 6)
+        x_along_slots(vector_copy, 3, 7)
+        products(x_feat[0], w1_q[0])
+        late_grouped = placed("late_grouped", FREE_AT + 16, BF16)
+        group_w1(gpsimd_copy, 1, late_grouped, slice(0, N), 1)
+        scaled(y[0], of_expert(both, 0))
+        of_z(ACT.Sigmoid, sigmoid[0], 0, inverse)
+        x_feat.append(operand("x_feat_1", E4M3, W1_AT + 8))
+        w1_q.append(operand("w1_q_1", E4M3))
+        quantize(x_grouped[1][:], x_feat[1])
+        quantize(late_grouped[:], w1_q[1])
+        first, rest = slice(0, P), slice(P, N)
+        first_block = placed("first_block", W1_AT + 10, BF16, N)
+        woven_product(first_block[:], y[0], sigmoid[0], first)
+        x_slot.append(operand("x_slot_1", E4M3, W1_AT + 12))
+        quantize(x_turned[1][:], x_slot[1])
+        dy_picked = [planes("dy_picked", FREE_AT + 20 + 4 * b) for b in range(EXPERTS)]
+        for t in (0, 1):
+            scalar_gather(dy_picked[0][:, t], listed(dy_plane[t], 0))
+
+        products(x_feat[1], w1_q[1])
+        rounded = placed("rounded", W1_AT + 4, BF16)
+        gpsimd_copy(rounded[:], w2_raw[0][:])
+        scaled(y[1], of_expert(both, 1))
+        of_z(ACT.Sigmoid, sigmoid[1], 1, inverse)
+        vector_copy(dy_picked[0][:, 2], listed(dy_plane[2], 0))
+        first_hidden = placed("first_hidden", W2_AT, BF16, 3 * N)
+        woven_product(first_hidden[:], y[0], sigmoid[0], rest)
+        scalar_gather(dy_picked[1][:, 0], listed(dy_plane[0], 1))
+        scalar_gather(dy_picked[0][:, 3], listed(dy_plane[3], 0))
+        early = slice(0, 3 * P)
+        hidden = placed("hidden", W2_AT + 3, BF16, 3 * N)
+        woven_product(hidden[:], y[1], sigmoid[1], early)
+        h_q = [operand("h_0", E4M3, W2_AT + 6), operand("h_1", E4M3)]
+        quantize(first_block[:], h_q[0], first)
+        quantize(first_hidden[:], h_q[0], rest)
+        quantize(hidden[:], h_q[1], early)
+        w2_grouped = placed("w2_grouped", FREE_AT + 8, BF16)
+        turn_w2(rounded, w2_grouped, (4, 5))
+        dy_grouped = placed("dy_grouped", FREE_AT + 16, BF16)
+        along_features(vector_copy, dy_picked[0], dy_grouped)
+        turn_dy(dy_picked[0], (6, 7))
+        w2_q, dy_feat = [operand("w2_0", E4M3, FREE_AT + 20)], [operand("dy_feat_0", E5M2)]
+        quantize(w2_grouped[:], w2_q[0])
+        quantize(dy_grouped[:], dy_feat[0])
+        for t in (1, 2, 3):
+            scalar_gather(dy_picked[1][:, t], listed(dy_plane[t], 1))
+        rounded = placed("rounded", X_AT + 8, BF16)
+
+        dy_turned = placed("dy_turned", FREE_AT + 8, BF16)
+        dy_along_slots(vector_copy, dy_turned, (6, 7))
+        products(dy_feat[0], w2_q[0])
+        dy_grouped = placed("dy_grouped", FREE_AT + 16, BF16)
+        gpsimd_copy(
+            dy_grouped[:].rearrange("p (r s t) -> p r s t", r=PACK, t=PACK),
+            dy_picked[1].rearrange("p t (s r) -> p r s t", r=PACK),
+        )
+        dh = [placed("dh", DY_AT + 8 * b) for b in range(EXPERTS)]
+        turn_dy(dy_picked[1], (6, 7))
+        scaled(dh[0], of_expert(minus_both, 0))
+        mirrored = [placed("mirrored", DY_AT + 24)]
+        of_z(ACT.Silu, mirrored[0], 0, minus_inverse)
+        scalar_copy(rounded[:], w2_raw[1][:])
+        dy_feat.append(operand("dy_feat_1", E5M2))
+        quantize(dy_grouped[:], dy_feat[1])
+        slope = placed("slope", FREE_AT + 26)
+        slope_of(slope, 0)
+        mirrored.append(placed("mirrored", X_AT + 12))
+        of_z(ACT.Silu, mirrored[1], 1, minus_inverse)
+        w2_grouped = placed("w2_grouped", FREE_AT + 12, BF16)
+        turn_w2(rounded, w2_grouped, (4, 5))
+        dy_slot = [operand("dy_slot_0", E5M2, FREE_AT + 24)]
+        quantize(dy_turned[:], dy_slot[0])
+        gradient = placed("gradient", FREE_AT, BF16)
+        woven_product(gradient[:], slope, dh[0])
+        dy_turned = placed("dy_turned", FREE_AT + 4, BF16)
+        dy_along_slots(scalar_copy, dy_turned, (6, 7))
+
+        def blocks(whole):
+            return [(whole, j) for j in range(PACK)]
+
+        def x_blocks(b):
+            return [(x_slot[t // 2], t % 2 * EXPERTS + b) for t in range(PACK)]
+
+        result(blocks(h_q[0]), dy_slot[0], out_1[0].rearrange("(c p) e -> c p e", c=PACK), placed("staged", FREE_AT + 34), (4, 5, 6, 7))
+        w2_q.append(operand("w2_1", E4M3))
+        dy_slot.append(operand("dy_slot_1", E5M2))
+        da = operand("da_0", E5M2)
+        quantize(gradient[:], da)
+        quantize(w2_grouped[:], w2_q[1])
+        products(dy_feat[1], w2_q[1])
+        slope = placed("slope", FREE_AT + 26)
+        slope_of(slope, 1)
+        quantize(dy_turned[:], dy_slot[1])
+        last_block = placed("last_block", FREE_AT + 4, BF16, N)
+        paired_product(last_block[:], y[1], sigmoid[1], slice(3 * P, N))
+        result(x_blocks(0), da, out_0[0].rearrange("(p t) f -> t p f", t=PACK), placed("staged", TS_AT), (4, 5, 6, 7))
+        scaled(dh[1], of_expert(minus_both, 1))
+        quantize(last_block[:], h_q[1], slice(3 * P, N))
+        result(blocks(h_q[1]), dy_slot[1], out_1[1].rearrange("(c p) e -> c p e", c=PACK), placed("staged", X_AT + 24), (4, 5, 6, 7))
 
         da = operand("da_1", E5M2)
-        staged = big_tile("dy_2", "staged")
+        staged = placed("staged", DY_AT + 16)
         rows = out_0[1].rearrange("(p t) f -> p t f", t=PACK)
-        g = half(1, 0)
+        gradient = placed("gradient", FREE_AT + 8, BF16)
         pieces = [slice(c * P, (c + 1) * P) for c in range(PACK)]
-        free = list(range(4, 8))
-        for cols in pieces:
-            src = g[:, cols.start * PACK : cols.stop * PACK]
-            woven_product(src, slope, dh, cols)
-            quantize_part(src, E5M2, da, cols)
-        for cols in pieces:
-            n = cols.stop - cols.start
-            per_bank = N // n
-            for first in range(0, PACK, per_bank):
-                which = free.pop(0)
-                for v in range(per_bank):
-                    product(bank[which][:, v * n : (v + 1) * n], x_slot[1], first + v, (da[0][:, cols], da[1][:, cols], E5M2))
-                if len(free) == 1:
-                    piece = g[:, part:].bitcast(F32)
-                    vector_copy(piece, bank[which][:])
-                else:
-                    piece = staged[:, (which - 4) * N : (which - 3) * N]
-                    scalar_copy(piece, bank[which][:])
-                nc.sync.dma_start(rows[:, first : first + per_bank, cols], piece.rearrange("p (v f) -> p v f", v=per_bank))
+        for c, cols in enumerate(pieces):
+            woven_product(gradient[:, c * N : (c + 1) * N], slope, dh[1], cols)
+            if c:
+                quantize(gradient[:, (c - 1) * N : c * N], da, pieces[c - 1])
+        quantize(gradient[:, (PACK - 1) * N :], da, pieces[-1])
+        for c, cols in enumerate(pieces):
+            for t, (whole, j) in enumerate(x_blocks(1)):
+                product(bank[c][:, t * P : (t + 1) * P], whole, j, da, cols)
+            piece = staged[:, c * N : (c + 1) * N]
+            (vector_copy if c == PACK - 1 else scalar_copy)(piece, bank[c][:])
+            nc.sync.dma_start(rows[:, :, cols], piece.rearrange("p (t f) -> p t f", t=PACK))

@@ -223,17 +223,18 @@ def tile_attend_gxfull_sil_W_kernel(tc, xT, dyT, w1, w2, ts, tx, cf, offs, out_0
         tx_dealt = gather_tokens(scalar_gather, tx_win, "tx_picked")
         ts_dealt = gather_tokens(vector_copy, ts_win, "ts_picked")
         width = EXPERTS * PACK
-        tx_cols = held.tile([P, width], F32, name="tx_cols")
-        ts_cols = held.tile([P, width], F32, name="ts_cols")
+        tx_cols = placed("tx_cols", FREE_AT + 4, F32, width)
+        ts_cols = placed("ts_cols", FREE_AT + 4.0625, F32, width)
+        gates = placed("gates", FREE_AT + 4.125, F32, width)
         cf_row = held.tile([P, N], F32, name="cf_row")
         for j in range(PACK):
             nc.tensor.transpose(bank[2][:, j * P : (j + 1) * P], cf_cols[:, j : j + 1].to_broadcast([P, P]), ident[:])
 
         x_both = placed("x_both", TS_AT, BF16, 2 * WIDE)[:].rearrange("p (t n) -> p t n", t=PACK)
         x_picked = [x_both[:, :, b * N : (b + 1) * N] for b in range(EXPERTS)]
-        x_turned = [placed("x_turned", FREE_AT, BF16)]
-        x_grouped = [placed("x_grouped", FREE_AT + 4, BF16)]
-        w1_grouped = placed("w1_grouped", FREE_AT + 16, BF16)
+        x_turned = [placed("x_turned", FREE_AT + 4.25, BF16)]
+        x_grouped = [placed("x_grouped", FREE_AT + 16, BF16)]
+        w1_grouped = placed("w1_grouped", FREE_AT, BF16)
 
         def gather_x(t):
             vector_copy(x_picked[0][:, t], listed(x_plane[t], 0))
@@ -247,13 +248,13 @@ def tile_attend_gxfull_sil_W_kernel(tc, xT, dyT, w1, w2, ts, tx, cf, offs, out_0
         x_along_slots(scalar_copy, 1, 5)
         token_columns(ts_dealt, ts_cols, (2, 3))
         gather_x(2)
-        columns = held.tile([P, 5 * width], F32, name="columns")
-        both, minus_both, gates, inverse, minus_inverse = (columns[:, k * width : (k + 1) * width] for k in range(5))
-        nc.vector.scalar_tensor_tensor(gates, ts_cols[:], 0.0, ts_cols[:], ALU.is_equal, ALU.add)
+        columns = held.tile([P, 2 * width], F32, name="columns")
+        both, inverse = columns[:, :width], columns[:, width:]
+        nc.vector.scalar_tensor_tensor(gates[:], ts_cols[:], 0.0, ts_cols[:], ALU.is_equal, ALU.add)
         nc.vector.tensor_tensor(both, tx_cols[:], ts_cols[:], ALU.mult)
-        nc.vector.reciprocal(inverse, gates)
-        nc.vector.tensor_scalar(minus_both, both, -1.0, None, ALU.mult)
-        nc.vector.tensor_scalar(minus_inverse, inverse, -1.0, None, ALU.mult)
+        nc.vector.reciprocal(inverse, gates[:])
+        minus_columns = held.tile([P, 2 * width], F32, name="minus_columns")
+        minus_both, minus_inverse = minus_columns[:, :width], minus_columns[:, width:]
         x_slot = [operand("x_slot_0", E4M3)]
         quantize(x_turned[0][:], x_slot[0])
         gather_x(3)
@@ -268,6 +269,7 @@ def tile_attend_gxfull_sil_W_kernel(tc, xT, dyT, w1, w2, ts, tx, cf, offs, out_0
         x_grouped.append(placed("x_grouped", W1_AT, BF16))
         along_features(scalar_copy, x_picked[1], x_grouped[1])
         quantize(w1_grouped[:], w1_q[0])
+        nc.scalar.activation(minus_columns[:], columns[:], ACT.Copy, scale=-1.0)
 
         def planes(name, at):
             return placed(name, at, BF16)[:].rearrange("p (t n) -> p t n", t=PACK)
@@ -281,7 +283,7 @@ def tile_attend_gxfull_sil_W_kernel(tc, xT, dyT, w1, w2, ts, tx, cf, offs, out_0
         x_along_slots(vector_copy, 2, 6)
         x_along_slots(vector_copy, 3, 7)
         products(x_feat[0], w1_q[0])
-        late_grouped = placed("late_grouped", FREE_AT + 16, BF16)
+        late_grouped = placed("late_grouped", FREE_AT + 2, BF16)
         group_w1(gpsimd_copy, 1, late_grouped, slice(0, N), 1)
         scaled(y[0], of_expert(both, 0))
         of_z(ACT.Sigmoid, sigmoid[0], 0, inverse)
@@ -289,9 +291,6 @@ def tile_attend_gxfull_sil_W_kernel(tc, xT, dyT, w1, w2, ts, tx, cf, offs, out_0
         w1_q.append(operand("w1_q_1", E4M3))
         quantize(x_grouped[1][:], x_feat[1])
         quantize(late_grouped[:], w1_q[1])
-        first, rest = slice(0, P), slice(P, N)
-        first_block = placed("first_block", W1_AT + 10, BF16, N)
-        woven_product(first_block[:], y[0], sigmoid[0], first)
         x_slot.append(operand("x_slot_1", E4M3, W1_AT + 12))
         quantize(x_turned[1][:], x_slot[1])
         dy_picked = [planes("dy_picked", FREE_AT + 20 + 4 * b) for b in range(EXPERTS)]
@@ -304,20 +303,19 @@ def tile_attend_gxfull_sil_W_kernel(tc, xT, dyT, w1, w2, ts, tx, cf, offs, out_0
         scaled(y[1], of_expert(both, 1))
         of_z(ACT.Sigmoid, sigmoid[1], 1, inverse)
         vector_copy(dy_picked[0][:, 2], listed(dy_plane[2], 0))
-        first_hidden = placed("first_hidden", W2_AT, BF16, 3 * N)
-        woven_product(first_hidden[:], y[0], sigmoid[0], rest)
+        first_hidden = placed("first_hidden", W2_AT, BF16)
+        woven_product(first_hidden[:], y[0], sigmoid[0])
         scalar_gather(dy_picked[1][:, 0], listed(dy_plane[0], 1))
         scalar_gather(dy_picked[0][:, 3], listed(dy_plane[3], 0))
         early = slice(0, 3 * P)
-        hidden = placed("hidden", W2_AT + 3, BF16, 3 * N)
+        hidden = placed("hidden", W2_AT + 4, BF16, 3 * N)
         woven_product(hidden[:], y[1], sigmoid[1], early)
-        h_q = [operand("h_0", E4M3, W2_AT + 6), operand("h_1", E4M3)]
-        quantize(first_block[:], h_q[0], first)
-        quantize(first_hidden[:], h_q[0], rest)
+        h_q = [operand("h_0", E4M3), operand("h_1", E4M3)]
+        quantize(first_hidden[:], h_q[0])
         quantize(hidden[:], h_q[1], early)
-        w2_grouped = placed("w2_grouped", FREE_AT + 8, BF16)
+        w2_grouped = placed("w2_grouped", FREE_AT + 10, BF16)
         turn_w2(rounded, w2_grouped, (4, 5))
-        dy_grouped = placed("dy_grouped", FREE_AT + 16, BF16)
+        dy_grouped = placed("dy_grouped", FREE_AT + 14, BF16)
         along_features(vector_copy, dy_picked[0], dy_grouped)
         turn_dy(dy_picked[0], (6, 7))
         w2_q, dy_feat = [operand("w2_0", E4M3, FREE_AT + 20)], [operand("dy_feat_0", E5M2)]
@@ -330,7 +328,7 @@ def tile_attend_gxfull_sil_W_kernel(tc, xT, dyT, w1, w2, ts, tx, cf, offs, out_0
         dy_turned = placed("dy_turned", FREE_AT + 8, BF16)
         dy_along_slots(vector_copy, dy_turned, (6, 7))
         products(dy_feat[0], w2_q[0])
-        dy_grouped = placed("dy_grouped", FREE_AT + 16, BF16)
+        dy_grouped = placed("dy_grouped", FREE_AT + 12, BF16)
         gpsimd_copy(
             dy_grouped[:].rearrange("p (r s t) -> p r s t", r=PACK, t=PACK),
             dy_picked[1].rearrange("p t (s r) -> p r s t", r=PACK),
@@ -347,13 +345,13 @@ def tile_attend_gxfull_sil_W_kernel(tc, xT, dyT, w1, w2, ts, tx, cf, offs, out_0
         slope_of(slope, 0)
         mirrored.append(placed("mirrored", X_AT + 12))
         of_z(ACT.Silu, mirrored[1], 1, minus_inverse)
-        w2_grouped = placed("w2_grouped", FREE_AT + 12, BF16)
+        w2_grouped = placed("w2_grouped", FREE_AT + 4, BF16)
         turn_w2(rounded, w2_grouped, (4, 5))
         dy_slot = [operand("dy_slot_0", E5M2, FREE_AT + 24)]
         quantize(dy_turned[:], dy_slot[0])
         gradient = placed("gradient", FREE_AT, BF16)
         woven_product(gradient[:], slope, dh[0])
-        dy_turned = placed("dy_turned", FREE_AT + 4, BF16)
+        dy_turned = placed("dy_turned", X_AT + 20, BF16)
         dy_along_slots(scalar_copy, dy_turned, (6, 7))
 
         def blocks(whole):
@@ -369,10 +367,10 @@ def tile_attend_gxfull_sil_W_kernel(tc, xT, dyT, w1, w2, ts, tx, cf, offs, out_0
         quantize(gradient[:], da)
         quantize(w2_grouped[:], w2_q[1])
         products(dy_feat[1], w2_q[1])
-        slope = placed("slope", FREE_AT + 26)
-        slope_of(slope, 1)
         quantize(dy_turned[:], dy_slot[1])
-        last_block = placed("last_block", FREE_AT + 4, BF16, N)
+        slope = placed("slope", FREE_AT)
+        slope_of(slope, 1)
+        last_block = placed("last_block", X_AT + 19.5, BF16, N)
         paired_product(last_block[:], y[1], sigmoid[1], slice(3 * P, N))
         result(x_blocks(0), da, out_0[0].rearrange("(p t) f -> t p f", t=PACK), placed("staged", TS_AT), (4, 5, 6, 7))
         scaled(dh[1], of_expert(minus_both, 1))

@@ -73,7 +73,7 @@ def tile_attend_gxfull_sil_W_kernel(tc, xT, dyT, w1, w2, ts, tx, cf, offs, out_0
         ts_win, tx_win = placed("ts_win", TS_AT), placed("tx_win", TX_AT)
         warm = held.tile([P, 1], F32, name="warm")
         nc.vector.memset(warm[:], 0.0)
-        nc.gpsimd.memset(tx_win[0 : P - 1, :].bitcast(I32), 0)
+        nc.vector.memset(tx_win[0 : P - 1, :].bitcast(I32), 0)
         nc.vector.memset(ts_win[0 : P - 1, :].bitcast(I32), 0)
         cf_cols = held.tile([P, PACK], F32, name="cf_cols")
         nc.scalar.dma_start(tx_win[P - 1 : P, :], tx[0:1, :])
@@ -111,21 +111,17 @@ def tile_attend_gxfull_sil_W_kernel(tc, xT, dyT, w1, w2, ts, tx, cf, offs, out_0
         load_plane(dy_plane, dyT, 3)
         load_w2(1)
 
-        def gather_tokens(gather, window, name):
+        def gather_tokens(window, name, banks):
             picked = held.tile([P, EXPERTS * N], F32, name=name)
-            gather(picked[:], window[:].indirect(offsets[:]))
-            dealt = held.tile([P, EXPERTS * N], F32, name=name + "_dealt")
-            gpsimd_copy(
-                dealt[:].rearrange("p (b r c i) -> p b c r i", b=EXPERTS, r=PACK, i=PACK),
-                picked[:].rearrange("p (b c i r) -> p b c r i", b=EXPERTS, r=PACK, i=PACK),
-            )
-            return dealt
-
-        def token_columns(dealt, cols, banks):
+            scalar_gather(picked[:], window[:].indirect(offsets[:]))
             for b in range(EXPERTS):
                 for r in range(PACK):
-                    first = b * N + r * P
-                    nc.tensor.transpose(bank[banks[b]][:, r * P : (r + 1) * P], dealt[:, first : first + P], ident[:])
+                    nc.tensor.transpose(
+                        bank[banks[b]][:, r * P : (r + 1) * P], picked[:, b * N + r : (b + 1) * N : PACK], ident[:]
+                    )
+
+        def token_columns(cols, banks):
+            for b in range(EXPERTS):
                 scalar_copy(cols[:, b * PACK : (b + 1) * PACK], bank[banks[b]][:, P - 1 : N : P])
 
         def group_w1(copy, b, g, cols, run=PACK):
@@ -220,56 +216,50 @@ def tile_attend_gxfull_sil_W_kernel(tc, xT, dyT, w1, w2, ts, tx, cf, offs, out_0
                 scalar_copy(staged[:, j * N : (j + 1) * N], acc[:])
                 nc.sync.dma_start(rows[j], staged[:, j * N : (j + 1) * N])
 
-        tx_dealt = gather_tokens(scalar_gather, tx_win, "tx_picked")
-        ts_dealt = gather_tokens(vector_copy, ts_win, "ts_picked")
+        gather_tokens(tx_win, "tx_picked", (0, 1))
+        gather_tokens(ts_win, "ts_picked", (6, 7))
         width = EXPERTS * PACK
-        tx_cols = placed("tx_cols", FREE_AT + 4, F32, width)
-        ts_cols = placed("ts_cols", FREE_AT + 4.0625, F32, width)
-        gates = placed("gates", FREE_AT + 4.125, F32, width)
-        cf_row = held.tile([P, N], F32, name="cf_row")
         for j in range(PACK):
             nc.tensor.transpose(bank[2][:, j * P : (j + 1) * P], cf_cols[:, j : j + 1].to_broadcast([P, P]), ident[:])
 
-        x_both = placed("x_both", TS_AT, BF16, 2 * WIDE)[:].rearrange("p (t n) -> p t n", t=PACK)
+        x_both = placed("x_both", FREE_AT + 54, BF16, 2 * WIDE)[:].rearrange("p (t n) -> p t n", t=PACK)
         x_picked = [x_both[:, :, b * N : (b + 1) * N] for b in range(EXPERTS)]
-        x_turned = [placed("x_turned", FREE_AT + 4.25, BF16)]
         x_grouped = [placed("x_grouped", FREE_AT + 16, BF16)]
-        w1_grouped = placed("w1_grouped", FREE_AT, BF16)
 
         def gather_x(t):
             vector_copy(x_picked[0][:, t], listed(x_plane[t], 0))
             scalar_gather(x_picked[1][:, t], listed(x_plane[t], 1))
 
-        gather_x(0)
+        vector_copy(x_both[:, 0], x_plane[0][:].indirect(offsets[:]))
+        vector_copy(x_both[:, 1], x_plane[1][:].indirect(offsets[:]))
+        cf_row = held.tile([P, N], F32, name="cf_row")
         scalar_copy(cf_row[:].rearrange("p (m j) -> p m j", j=PACK), bank[2][:].rearrange("p (j m) -> p m j", j=PACK))
-        gather_x(1)
+        x_turned = [placed("x_turned", X_AT + 4, BF16)]
         x_along_slots(scalar_copy, 0, 4)
-        token_columns(tx_dealt, tx_cols, (0, 1))
         x_along_slots(scalar_copy, 1, 5)
-        token_columns(ts_dealt, ts_cols, (2, 3))
         gather_x(2)
-        columns = held.tile([P, 2 * width], F32, name="columns")
+        gather_x(3)
+        tx_cols = placed("tx_cols", X_AT + 24.25, F32, width)
+        ts_cols = placed("ts_cols", X_AT + 24.3125, F32, width)
+        token_columns(tx_cols, (0, 1))
+        token_columns(ts_cols, (6, 7))
+        gates = placed("gates", X_AT + 24, F32, width)
+        columns = placed("columns", X_AT + 26, F32, 2 * width)
         both, inverse = columns[:, :width], columns[:, width:]
         nc.vector.scalar_tensor_tensor(gates[:], ts_cols[:], 0.0, ts_cols[:], ALU.is_equal, ALU.add)
         nc.vector.tensor_tensor(both, tx_cols[:], ts_cols[:], ALU.mult)
+        along_features(vector_copy, x_picked[0], x_grouped[0])
         nc.vector.reciprocal(inverse, gates[:])
-        minus_columns = held.tile([P, 2 * width], F32, name="minus_columns")
-        minus_both, minus_inverse = minus_columns[:, :width], minus_columns[:, width:]
-        x_slot = [operand("x_slot_0", E4M3)]
-        quantize(x_turned[0][:], x_slot[0])
-        gather_x(3)
-        along_features(vector_copy, x_picked[0], x_grouped[0], slice(0, PACK - 1))
-        along_features(scalar_copy, x_picked[0], x_grouped[0], slice(PACK - 1, PACK))
         low, high = slice(0, N // 2), slice(N // 2, N)
+        w1_grouped = placed("w1_grouped", X_AT + 8, BF16)
         group_w1(scalar_copy, 0, w1_grouped, high)
         group_w1(vector_copy, 0, w1_grouped, low)
         x_feat = [operand("x_feat_0", E4M3)]
-        w1_q = [operand("w1_q_0", E4M3)]
+        w1_q = [operand("w1_q_0", E4M3, X_AT + 23.5)]
         quantize(x_grouped[0][:], x_feat[0])
         x_grouped.append(placed("x_grouped", W1_AT, BF16))
         along_features(scalar_copy, x_picked[1], x_grouped[1])
         quantize(w1_grouped[:], w1_q[0])
-        nc.scalar.activation(minus_columns[:], columns[:], ACT.Copy, scale=-1.0)
 
         def planes(name, at):
             return placed(name, at, BF16)[:].rearrange("p (t n) -> p t n", t=PACK)
@@ -277,13 +267,15 @@ def tile_attend_gxfull_sil_W_kernel(tc, xT, dyT, w1, w2, ts, tx, cf, offs, out_0
         def of_expert(cols, b):
             return cols[:, b * PACK : (b + 1) * PACK]
 
-        y = [placed("y", X_AT + 8 - 8 * b) for b in range(EXPERTS)]
+        y = [placed("y", at) for at in (FREE_AT + 42, TS_AT)]
         sigmoid = [placed("sigmoid", XB_AT - 8 * b) for b in range(EXPERTS)]
         x_turned.append(placed("x_turned", W1_AT + 4, BF16))
-        x_along_slots(vector_copy, 2, 6)
-        x_along_slots(vector_copy, 3, 7)
+        x_slot = [operand("x_slot_0", E4M3, FREE_AT + 16)]
+        quantize(x_turned[0][:], x_slot[0])
+        x_along_slots(vector_copy, 2, 4)
+        x_along_slots(scalar_copy, 3, 5)
         products(x_feat[0], w1_q[0])
-        late_grouped = placed("late_grouped", FREE_AT + 2, BF16)
+        late_grouped = placed("late_grouped", X_AT + 6, BF16)
         group_w1(gpsimd_copy, 1, late_grouped, slice(0, N), 1)
         scaled(y[0], of_expert(both, 0))
         of_z(ACT.Sigmoid, sigmoid[0], 0, inverse)
@@ -305,6 +297,9 @@ def tile_attend_gxfull_sil_W_kernel(tc, xT, dyT, w1, w2, ts, tx, cf, offs, out_0
         vector_copy(dy_picked[0][:, 2], listed(dy_plane[2], 0))
         first_hidden = placed("first_hidden", W2_AT, BF16)
         woven_product(first_hidden[:], y[0], sigmoid[0])
+        minus_columns = placed("minus_columns", W2_AT + 7, F32, 2 * width)
+        minus_both, minus_inverse = minus_columns[:, :width], minus_columns[:, width:]
+        nc.scalar.activation(minus_columns[:], columns[:], ACT.Copy, scale=-1.0)
         scalar_gather(dy_picked[1][:, 0], listed(dy_plane[0], 1))
         scalar_gather(dy_picked[0][:, 3], listed(dy_plane[3], 0))
         early = slice(0, 3 * P)
@@ -313,9 +308,9 @@ def tile_attend_gxfull_sil_W_kernel(tc, xT, dyT, w1, w2, ts, tx, cf, offs, out_0
         h_q = [operand("h_0", E4M3), operand("h_1", E4M3)]
         quantize(first_hidden[:], h_q[0])
         quantize(hidden[:], h_q[1], early)
-        w2_grouped = placed("w2_grouped", FREE_AT + 10, BF16)
+        w2_grouped = placed("w2_grouped", FREE_AT + 4, BF16)
         turn_w2(rounded, w2_grouped, (4, 5))
-        dy_grouped = placed("dy_grouped", FREE_AT + 14, BF16)
+        dy_grouped = placed("dy_grouped", FREE_AT + 8, BF16)
         along_features(vector_copy, dy_picked[0], dy_grouped)
         turn_dy(dy_picked[0], (6, 7))
         w2_q, dy_feat = [operand("w2_0", E4M3, FREE_AT + 20)], [operand("dy_feat_0", E5M2)]
@@ -323,12 +318,12 @@ def tile_attend_gxfull_sil_W_kernel(tc, xT, dyT, w1, w2, ts, tx, cf, offs, out_0
         quantize(dy_grouped[:], dy_feat[0])
         for t in (1, 2, 3):
             scalar_gather(dy_picked[1][:, t], listed(dy_plane[t], 1))
-        rounded = placed("rounded", X_AT + 8, BF16)
+        rounded = placed("rounded", FREE_AT + 42, BF16)
 
-        dy_turned = placed("dy_turned", FREE_AT + 8, BF16)
+        dy_turned = placed("dy_turned", FREE_AT + 2, BF16)
         dy_along_slots(vector_copy, dy_turned, (6, 7))
         products(dy_feat[0], w2_q[0])
-        dy_grouped = placed("dy_grouped", FREE_AT + 12, BF16)
+        dy_grouped = placed("dy_grouped", FREE_AT + 6, BF16)
         gpsimd_copy(
             dy_grouped[:].rearrange("p (r s t) -> p r s t", r=PACK, t=PACK),
             dy_picked[1].rearrange("p t (s r) -> p r s t", r=PACK),
@@ -343,15 +338,15 @@ def tile_attend_gxfull_sil_W_kernel(tc, xT, dyT, w1, w2, ts, tx, cf, offs, out_0
         quantize(dy_grouped[:], dy_feat[1])
         slope = placed("slope", FREE_AT + 26)
         slope_of(slope, 0)
-        mirrored.append(placed("mirrored", X_AT + 12))
+        mirrored.append(placed("mirrored", FREE_AT + 46))
         of_z(ACT.Silu, mirrored[1], 1, minus_inverse)
-        w2_grouped = placed("w2_grouped", FREE_AT + 4, BF16)
+        w2_grouped = placed("w2_grouped", X_AT + 12, BF16)
         turn_w2(rounded, w2_grouped, (4, 5))
         dy_slot = [operand("dy_slot_0", E5M2, FREE_AT + 24)]
         quantize(dy_turned[:], dy_slot[0])
-        gradient = placed("gradient", FREE_AT, BF16)
+        gradient = placed("gradient", X_AT + 8, BF16)
         woven_product(gradient[:], slope, dh[0])
-        dy_turned = placed("dy_turned", X_AT + 20, BF16)
+        dy_turned = placed("dy_turned", FREE_AT + 42, BF16)
         dy_along_slots(scalar_copy, dy_turned, (6, 7))
 
         def blocks(whole):
@@ -368,14 +363,14 @@ def tile_attend_gxfull_sil_W_kernel(tc, xT, dyT, w1, w2, ts, tx, cf, offs, out_0
         quantize(w2_grouped[:], w2_q[1])
         products(dy_feat[1], w2_q[1])
         quantize(dy_turned[:], dy_slot[1])
-        slope = placed("slope", FREE_AT)
+        slope = placed("slope", X_AT + 8)
         slope_of(slope, 1)
-        last_block = placed("last_block", X_AT + 19.5, BF16, N)
+        last_block = placed("last_block", FREE_AT + 45.5, BF16, N)
         paired_product(last_block[:], y[1], sigmoid[1], slice(3 * P, N))
-        result(x_blocks(0), da, out_0[0].rearrange("(p t) f -> t p f", t=PACK), placed("staged", TS_AT), (4, 5, 6, 7))
+        result(x_blocks(0), da, out_0[0].rearrange("(p t) f -> t p f", t=PACK), placed("staged", X_AT), (4, 5, 6, 7))
         scaled(dh[1], of_expert(minus_both, 1))
         quantize(last_block[:], h_q[1], slice(3 * P, N))
-        result(blocks(h_q[1]), dy_slot[1], out_1[1].rearrange("(c p) e -> c p e", c=PACK), placed("staged", X_AT + 24), (4, 5, 6, 7))
+        result(blocks(h_q[1]), dy_slot[1], out_1[1].rearrange("(c p) e -> c p e", c=PACK), placed("staged", W1_AT), (4, 5, 6, 7))
 
         da = operand("da_1", E5M2)
         staged = placed("staged", DY_AT + 16)

@@ -168,9 +168,9 @@ def tile_attend_gxfull_sil_W_kernel(tc, xT, dyT, w1, w2, ts, tx, cf, offs, out_0
                         k = 2 * tt + v
                         nc.tensor.transpose(bank[banks[side]][:, k * P : (k + 1) * P], words[:, v::2], ident[:])
 
-        def dy_along_slots(copy, g, banks):
+        def dy_along_slots(copies, g, banks):
             for side in range(2):
-                copy(
+                copies[side](
                     g[:].bitcast(F32).rearrange("s (p h k) -> s h p k", h=2, k=4)[:, side],
                     bank[banks[side]][:].rearrange("s (k p) -> s p k", k=4),
                 )
@@ -194,7 +194,7 @@ def tile_attend_gxfull_sil_W_kernel(tc, xT, dyT, w1, w2, ts, tx, cf, offs, out_0
         def of_z(func, dst, b, scale):
             for r in range(PACK):
                 cols = slice(r * N, (r + 1) * N)
-                nc.scalar.activation(dst[:, cols], y[b][:, cols], func, scale=scale[:, b * PACK + r : b * PACK + r + 1])
+                nc.scalar.activation(dst[:, cols], y[b][:, cols], func, scale=scale[:, r : r + 1])
 
         def woven_product(g, left, right, cols=slice(0, N)):
             nc.vector.tensor_tensor(woven(g), strands(left, cols), strands(right, cols), ALU.mult)
@@ -261,13 +261,10 @@ def tile_attend_gxfull_sil_W_kernel(tc, xT, dyT, w1, w2, ts, tx, cf, offs, out_0
         along_features(scalar_copy, x_picked[1], x_grouped[1])
         quantize(w1_grouped[:], w1_q[0])
 
-        def planes(name, at):
-            return placed(name, at, BF16)[:].rearrange("p (t n) -> p t n", t=PACK)
-
         def of_expert(cols, b):
             return cols[:, b * PACK : (b + 1) * PACK]
 
-        y = [placed("y", at) for at in (FREE_AT + 42, TS_AT)]
+        y = [placed("y", at) for at in (FREE_AT + 42, FREE_AT + 54)]
         sigmoid = [placed("sigmoid", XB_AT - 8 * b) for b in range(EXPERTS)]
         x_turned.append(placed("x_turned", W1_AT + 4, BF16))
         x_slot = [operand("x_slot_0", E4M3, FREE_AT + 16)]
@@ -278,14 +275,15 @@ def tile_attend_gxfull_sil_W_kernel(tc, xT, dyT, w1, w2, ts, tx, cf, offs, out_0
         late_grouped = placed("late_grouped", X_AT + 6, BF16)
         group_w1(gpsimd_copy, 1, late_grouped, slice(0, N), 1)
         scaled(y[0], of_expert(both, 0))
-        of_z(ACT.Sigmoid, sigmoid[0], 0, inverse)
+        of_z(ACT.Sigmoid, sigmoid[0], 0, of_expert(inverse, 0))
         x_feat.append(operand("x_feat_1", E4M3, W1_AT + 8))
         w1_q.append(operand("w1_q_1", E4M3))
         quantize(x_grouped[1][:], x_feat[1])
         quantize(late_grouped[:], w1_q[1])
         x_slot.append(operand("x_slot_1", E4M3, W1_AT + 12))
         quantize(x_turned[1][:], x_slot[1])
-        dy_picked = [planes("dy_picked", FREE_AT + 20 + 4 * b) for b in range(EXPERTS)]
+        dy_tiles = [placed("dy_picked", FREE_AT + 20 + 4 * b, BF16) for b in range(EXPERTS)]
+        dy_picked = [g[:].rearrange("p (t n) -> p t n", t=PACK) for g in dy_tiles]
         for t in (0, 1):
             scalar_gather(dy_picked[0][:, t], listed(dy_plane[t], 0))
 
@@ -293,61 +291,61 @@ def tile_attend_gxfull_sil_W_kernel(tc, xT, dyT, w1, w2, ts, tx, cf, offs, out_0
         rounded = placed("rounded", W1_AT + 4, BF16)
         gpsimd_copy(rounded[:], w2_raw[0][:])
         scaled(y[1], of_expert(both, 1))
-        of_z(ACT.Sigmoid, sigmoid[1], 1, inverse)
+        of_z(ACT.Sigmoid, sigmoid[1], 1, of_expert(inverse, 1))
         vector_copy(dy_picked[0][:, 2], listed(dy_plane[2], 0))
         first_hidden = placed("first_hidden", W2_AT, BF16)
         woven_product(first_hidden[:], y[0], sigmoid[0])
         minus_columns = placed("minus_columns", W2_AT + 7, F32, 2 * width)
         minus_both, minus_inverse = minus_columns[:, :width], minus_columns[:, width:]
         nc.scalar.activation(minus_columns[:], columns[:], ACT.Copy, scale=-1.0)
+        first_inverse = dy_tiles[1][:].bitcast(F32)[:, N - 2 : N + 2]
+        scalar_copy(first_inverse, of_expert(minus_inverse, 0))
         scalar_gather(dy_picked[1][:, 0], listed(dy_plane[0], 1))
         scalar_gather(dy_picked[0][:, 3], listed(dy_plane[3], 0))
         early = slice(0, 3 * P)
         hidden = placed("hidden", W2_AT + 4, BF16, 3 * N)
         woven_product(hidden[:], y[1], sigmoid[1], early)
-        h_q = [operand("h_0", E4M3), operand("h_1", E4M3)]
-        quantize(first_hidden[:], h_q[0])
-        quantize(hidden[:], h_q[1], early)
         w2_grouped = placed("w2_grouped", FREE_AT + 4, BF16)
         turn_w2(rounded, w2_grouped, (4, 5))
+        scalar_gather(dy_picked[1][:, 3], listed(dy_plane[3], 1))
         dy_grouped = placed("dy_grouped", FREE_AT + 8, BF16)
         along_features(vector_copy, dy_picked[0], dy_grouped)
         turn_dy(dy_picked[0], (6, 7))
-        w2_q, dy_feat = [operand("w2_0", E4M3, FREE_AT + 20)], [operand("dy_feat_0", E5M2)]
+        w2_q, dy_feat = [operand("w2_0", E4M3, FREE_AT + 19)], [operand("dy_feat_0", E5M2)]
         quantize(w2_grouped[:], w2_q[0])
         quantize(dy_grouped[:], dy_feat[0])
-        for t in (1, 2, 3):
-            scalar_gather(dy_picked[1][:, t], listed(dy_plane[t], 1))
-        rounded = placed("rounded", FREE_AT + 42, BF16)
-
-        dy_turned = placed("dy_turned", FREE_AT + 2, BF16)
-        dy_along_slots(vector_copy, dy_turned, (6, 7))
-        products(dy_feat[0], w2_q[0])
-        dy_grouped = placed("dy_grouped", FREE_AT + 6, BF16)
-        gpsimd_copy(
-            dy_grouped[:].rearrange("p (r s t) -> p r s t", r=PACK, t=PACK),
-            dy_picked[1].rearrange("p t (s r) -> p r s t", r=PACK),
-        )
-        dh = [placed("dh", DY_AT + 8 * b) for b in range(EXPERTS)]
-        turn_dy(dy_picked[1], (6, 7))
-        scaled(dh[0], of_expert(minus_both, 0))
+        h_q = [operand("h_0", E4M3, FREE_AT + 7), operand("h_1", E4M3, FREE_AT + 21)]
+        quantize(hidden[:], h_q[1], early)
+        quantize(first_hidden[:], h_q[0])
         mirrored = [placed("mirrored", DY_AT + 24)]
-        of_z(ACT.Silu, mirrored[0], 0, minus_inverse)
-        scalar_copy(rounded[:], w2_raw[1][:])
-        dy_feat.append(operand("dy_feat_1", E5M2))
-        quantize(dy_grouped[:], dy_feat[1])
-        slope = placed("slope", FREE_AT + 26)
+        of_z(ACT.Silu, mirrored[0], 0, first_inverse)
+
+        products(dy_feat[0], w2_q[0])
+        rounded = placed("rounded", W2_AT, BF16)
+        gpsimd_copy(rounded[:], w2_raw[1][:])
+        dh = [placed("dh", DY_AT)]
+        scaled(dh[0], of_expert(minus_both, 0))
+        dy_turned = placed("dy_turned", FREE_AT + 42, BF16)
+        dy_along_slots((vector_copy, scalar_copy), dy_turned, (6, 7))
+        for t in (1, 2):
+            scalar_gather(dy_picked[1][:, t], listed(dy_plane[t], 1))
+        turn_dy(dy_picked[1], (6, 7))
+        slope = placed("slope", W2_AT + 10)
         slope_of(slope, 0)
-        mirrored.append(placed("mirrored", FREE_AT + 46))
-        of_z(ACT.Silu, mirrored[1], 1, minus_inverse)
         w2_grouped = placed("w2_grouped", X_AT + 12, BF16)
         turn_w2(rounded, w2_grouped, (4, 5))
-        dy_slot = [operand("dy_slot_0", E5M2, FREE_AT + 24)]
+        dy_grouped = placed("dy_grouped", FREE_AT, BF16)
+        along_features(scalar_copy, dy_picked[1], dy_grouped)
+        mirrored.append(placed("mirrored", FREE_AT + 46))
+        of_z(ACT.Silu, mirrored[1], 1, of_expert(minus_inverse, 1))
+        dy_slot = [operand("dy_slot_0", E5M2, W2_AT + 8)]
         quantize(dy_turned[:], dy_slot[0])
         gradient = placed("gradient", X_AT + 8, BF16)
         woven_product(gradient[:], slope, dh[0])
         dy_turned = placed("dy_turned", FREE_AT + 42, BF16)
-        dy_along_slots(scalar_copy, dy_turned, (6, 7))
+        dy_along_slots((scalar_copy, scalar_copy), dy_turned, (6, 7))
+        dh.append(placed("dh", DY_AT + 8))
+        dy_feat.append(operand("dy_feat_1", E5M2))
 
         def blocks(whole):
             return [(whole, j) for j in range(PACK)]
@@ -360,6 +358,7 @@ def tile_attend_gxfull_sil_W_kernel(tc, xT, dyT, w1, w2, ts, tx, cf, offs, out_0
         dy_slot.append(operand("dy_slot_1", E5M2))
         da = operand("da_0", E5M2)
         quantize(gradient[:], da)
+        quantize(dy_grouped[:], dy_feat[1])
         quantize(w2_grouped[:], w2_q[1])
         products(dy_feat[1], w2_q[1])
         quantize(dy_turned[:], dy_slot[1])

@@ -267,12 +267,10 @@ def tile_attend_gxfull_sil_W_kernel(tc, xT, dyT, w1, w2, ts, tx, cf, offs, out_0
         y = [placed("y", at) for at in (FREE_AT + 42, FREE_AT + 54)]
         sigmoid = [placed("sigmoid", XB_AT - 8 * b) for b in range(EXPERTS)]
         x_turned.append(placed("x_turned", W1_AT + 4, BF16))
-        x_slot = [operand("x_slot_0", E4M3, FREE_AT + 16)]
-        quantize(x_turned[0][:], x_slot[0])
         x_along_slots(vector_copy, 2, 4)
-        x_along_slots(scalar_copy, 3, 5)
+        x_along_slots(vector_copy, 3, 5)
         products(x_feat[0], w1_q[0])
-        late_grouped = placed("late_grouped", X_AT + 6, BF16)
+        late_grouped = placed("late_grouped", X_AT + 8, BF16)
         group_w1(gpsimd_copy, 1, late_grouped, slice(0, N), 1)
         scaled(y[0], of_expert(both, 0))
         of_z(ACT.Sigmoid, sigmoid[0], 0, of_expert(inverse, 0))
@@ -280,8 +278,9 @@ def tile_attend_gxfull_sil_W_kernel(tc, xT, dyT, w1, w2, ts, tx, cf, offs, out_0
         w1_q.append(operand("w1_q_1", E4M3))
         quantize(x_grouped[1][:], x_feat[1])
         quantize(late_grouped[:], w1_q[1])
-        x_slot.append(operand("x_slot_1", E4M3, W1_AT + 12))
-        quantize(x_turned[1][:], x_slot[1])
+        x_slot = [operand("x_slot_%d" % k, E4M3, W1_AT + 10 + 2 * k) for k in range(2)]
+        for k in range(2):
+            quantize(x_turned[k][:], x_slot[k])
         dy_tiles = [placed("dy_picked", FREE_AT + 20 + 4 * b, BF16) for b in range(EXPERTS)]
         dy_picked = [g[:].rearrange("p (t n) -> p t n", t=PACK) for g in dy_tiles]
         for t in (0, 1):

@@ -38,12 +38,12 @@ def tile_attend_gxfull_sil_W_kernel(tc, xT, dyT, w1, w2, ts, tx, cf, offs, out_0
         bank = [psum.tile([P, N], F32, name="bank_%d" % j) for j in range(8)]
         vector_copy, scalar_copy, gpsimd_copy = nc.vector.tensor_copy, nc.scalar.copy, nc.gpsimd.tensor_copy
 
-        def operand(name, fmt, at=None):
+        def operand(name, fmt, at=None, width=N):
             if at is None:
-                codes = held.tile([P, N], U32, name=name + "_codes", align_bytes=64)
+                codes = held.tile([P, width], U32, name=name + "_codes", align_bytes=64)
             else:
-                codes = placed(name + "_codes", at, U32, N)
-            scales = held.tile([P, N], U8, name=name + "_scales", align_bytes=64)
+                codes = placed(name + "_codes", at, U32, width)
+            scales = held.tile([P, width], U8, name=name + "_scales", align_bytes=64)
             return codes[:], scales[:], fmt
 
         def quantize(src, dst, cols=slice(0, N)):
@@ -144,7 +144,7 @@ def tile_attend_gxfull_sil_W_kernel(tc, xT, dyT, w1, w2, ts, tx, cf, offs, out_0
 
         def along_features(copy, picked, g, places=slice(0, PACK)):
             copy(
-                g[:, places.start * N : places.stop * N].rearrange("p (r s i t) -> p s r i t", s=P // 2, i=2, t=PACK),
+                g[:].rearrange("p (r s i t) -> p s r i t", s=P // 2, i=2, t=PACK),
                 picked.rearrange("p t (s i r) -> p s r i t", r=PACK, i=2)[:, :, places],
             )
 
@@ -206,8 +206,8 @@ def tile_attend_gxfull_sil_W_kernel(tc, xT, dyT, w1, w2, ts, tx, cf, offs, out_0
             )
             nc.gpsimd.tensor_tensor(g.rearrange("p (c i r) -> p c r i", i=2, r=PACK), left, right, ALU.mult)
 
-        def slope_of(dst, b):
-            nc.vector.scalar_tensor_tensor(dst[:], mirrored[b][:], 1.0, sigmoid[b][:], ALU.subtract, ALU.mult)
+        def slope_of(dst, mirror, gate):
+            nc.vector.scalar_tensor_tensor(dst, mirror, 1.0, gate, ALU.subtract, ALU.mult)
 
         def result(stationary, moving, rows, staged, banks):
             for j in range(PACK):
@@ -313,11 +313,11 @@ def tile_attend_gxfull_sil_W_kernel(tc, xT, dyT, w1, w2, ts, tx, cf, offs, out_0
         w2_q, dy_feat = [operand("w2_0", E4M3, FREE_AT + 19)], [operand("dy_feat_0", E5M2)]
         quantize(w2_grouped[:], w2_q[0])
         quantize(dy_grouped[:], dy_feat[0])
-        h_q = [operand("h_0", E4M3, FREE_AT + 7), operand("h_1", E4M3, FREE_AT + 21)]
+        h_q = [operand("h_0", E4M3, FREE_AT + 7), operand("h_1", E4M3, FREE_AT + 21, 3 * P)]
         quantize(hidden[:], h_q[1], early)
         quantize(first_hidden[:], h_q[0])
-        mirrored = [placed("mirrored", DY_AT + 24)]
-        of_z(ACT.Silu, mirrored[0], 0, first_inverse)
+        mirrored = placed("mirrored", DY_AT + 24)
+        of_z(ACT.Silu, mirrored, 0, first_inverse)
 
         products(dy_feat[0], w2_q[0])
         rounded = placed("rounded", W2_AT, BF16)
@@ -330,21 +330,15 @@ def tile_attend_gxfull_sil_W_kernel(tc, xT, dyT, w1, w2, ts, tx, cf, offs, out_0
             scalar_gather(dy_picked[1][:, t], listed(dy_plane[t], 1))
         turn_dy(dy_picked[1], (6, 7))
         slope = placed("slope", W2_AT + 10)
-        slope_of(slope, 0)
+        slope_of(slope[:], mirrored[:], sigmoid[0][:])
+        dy_grouped = placed("dy_grouped", X_AT + 8, BF16)
+        along_features(scalar_copy, dy_picked[1], dy_grouped)
         w2_grouped = placed("w2_grouped", X_AT + 12, BF16)
         turn_w2(rounded, w2_grouped, (4, 5))
-        dy_grouped = placed("dy_grouped", FREE_AT, BF16)
-        along_features(scalar_copy, dy_picked[1], dy_grouped)
-        mirrored.append(placed("mirrored", FREE_AT + 46))
-        of_z(ACT.Silu, mirrored[1], 1, of_expert(minus_inverse, 1))
         dy_slot = [operand("dy_slot_0", E5M2, W2_AT + 8)]
         quantize(dy_turned[:], dy_slot[0])
-        gradient = placed("gradient", X_AT + 8, BF16)
+        gradient = placed("gradient", FREE_AT + 38, BF16)
         woven_product(gradient[:], slope, dh[0])
-        dy_turned = placed("dy_turned", FREE_AT + 42, BF16)
-        dy_along_slots((scalar_copy, scalar_copy), dy_turned, (6, 7))
-        dh.append(placed("dh", DY_AT + 8))
-        dy_feat.append(operand("dy_feat_1", E5M2))
 
         def blocks(whole):
             return [(whole, j) for j in range(PACK)]
@@ -352,23 +346,33 @@ def tile_attend_gxfull_sil_W_kernel(tc, xT, dyT, w1, w2, ts, tx, cf, offs, out_0
         def x_blocks(b):
             return [(x_slot[t // 2], t % 2 * EXPERTS + b) for t in range(PACK)]
 
-        result(blocks(h_q[0]), dy_slot[0], out_1[0].rearrange("(c p) e -> c p e", c=PACK), placed("staged", FREE_AT + 34), (4, 5, 6, 7))
+        dy_turned = placed("dy_turned", FREE_AT + 42, BF16)
+        dy_along_slots((scalar_copy, scalar_copy), dy_turned, (6, 7))
+        result(blocks(h_q[0]), dy_slot[0], out_1[0].rearrange("(c p) e -> c p e", c=PACK), placed("staged", X_AT + 16), (4, 5, 6, 7))
+        dh.append(placed("dh", DY_AT + 8))
+        dy_feat.append(operand("dy_feat_1", E5M2))
         w2_q.append(operand("w2_1", E4M3))
         dy_slot.append(operand("dy_slot_1", E5M2))
-        da = operand("da_0", E5M2)
-        quantize(gradient[:], da)
         quantize(dy_grouped[:], dy_feat[1])
         quantize(w2_grouped[:], w2_q[1])
         products(dy_feat[1], w2_q[1])
+        da = operand("da_0", E5M2, X_AT + 11)
+        quantize(gradient[:], da)
         quantize(dy_turned[:], dy_slot[1])
-        slope = placed("slope", X_AT + 8)
-        slope_of(slope, 1)
-        last_block = placed("last_block", FREE_AT + 45.5, BF16, N)
+        last_block = placed("last_block", FREE_AT + 41.5, BF16, N)
         paired_product(last_block[:], y[1], sigmoid[1], slice(3 * P, N))
+        late_mirrored = [placed("late_mirrored", FREE_AT + at, F32, N) for at in (36.5, 38.5, 42.5, 44.5)]
+        for r in range(PACK):
+            nc.scalar.activation(late_mirrored[r][:], y[1][:, r * N : (r + 1) * N], ACT.Silu, scale=of_expert(minus_inverse, 1)[:, r : r + 1])
         result(x_blocks(0), da, out_0[0].rearrange("(p t) f -> t p f", t=PACK), placed("staged", X_AT), (4, 5, 6, 7))
         scaled(dh[1], of_expert(minus_both, 1))
-        quantize(last_block[:], h_q[1], slice(3 * P, N))
-        result(blocks(h_q[1]), dy_slot[1], out_1[1].rearrange("(c p) e -> c p e", c=PACK), placed("staged", W1_AT), (4, 5, 6, 7))
+        slope = placed("slope", FREE_AT + 12)
+        for r in range(PACK):
+            cols = slice(r * N, (r + 1) * N)
+            slope_of(slope[:, cols], late_mirrored[r][:], sigmoid[1][:, cols])
+        h_last = operand("h_last", E4M3, FREE_AT + 42.5, P)
+        quantize(last_block[:], h_last, slice(0, P))
+        result(blocks(h_q[1])[:3] + [(h_last, 0)], dy_slot[1], out_1[1].rearrange("(c p) e -> c p e", c=PACK), placed("staged", W1_AT), (4, 5, 6, 7))
 
         da = operand("da_1", E5M2)
         staged = placed("staged", DY_AT + 16)

from contextlib import ExitStack

import concourse.mybir as mybir
from concourse.masks import make_identity

F32 = mybir.dt.float32
BF16 = mybir.dt.bfloat16
U32 = mybir.dt.uint32
I32 = mybir.dt.int32
U16 = mybir.dt.uint16
U8 = mybir.dt.uint8
E4M3 = mybir.dt.float8_e4m3fn_x4
E5M2 = mybir.dt.float8_e5m2_x4
ALU = mybir.AluOpType
ACT = mybir.ActivationFunctionType

P = 128
PACK = 4
N = 512
WIDE = PACK * N
EXPERTS = 2
KIB = 1024
FLOPS = 4 * 2 * EXPERTS * N * N * N


def tile_attend_gxfull_sil_W_kernel(tc, xT, dyT, w1, w2, ts, tx, cf, offs, out_0, out_1):
    nc = tc.nc
    with ExitStack() as ctx:
        held = ctx.enter_context(tc.tile_pool(name="held", bufs=1))
        arena = ctx.enter_context(tc.tile_pool(name="arena", bufs=1))
        psum = ctx.enter_context(tc.psum_pool(name="psum", bufs=1))

        def placed(name, at, dtype=F32, width=WIDE):
            return arena.tile([P, width], dtype, name=name, offset=int(at * KIB), align_bytes=64)

        X_AT, DY_AT, W1_AT, W2_AT, TS_AT, TX_AT, XB_AT, FREE_AT = 0, 32, 64, 80, 96, 104, 112, 120

        bank = [psum.tile([P, N], F32, name="bank_%d" % j) for j in range(8)]
        vector_copy, scalar_copy, gpsimd_copy = nc.vector.tensor_copy, nc.scalar.copy, nc.gpsimd.tensor_copy

        def operand(name, fmt, at=None, width=N):
            if at is None:
                codes = held.tile([P, width], U32, name=name + "_codes", align_bytes=64)
            else:
                codes = placed(name + "_codes", at, U32, width)
            scales = held.tile([P, width], U8, name=name + "_scales", align_bytes=64)
            return codes[:], scales[:], fmt

        def quantize(src, dst, cols=slice(0, N)):
            nc.vector.quantize_mx(out=dst[0][:, cols].bitcast(dst[2]), scales=dst[1][:, cols], in_=src)

        def product(dst, stationary, j, moving, cols=slice(0, N)):
            rows = slice(j * P, (j + 1) * P)
            nc.tensor.matmul_mx(
                out=dst,
                lhsT=stationary[0][:, rows].bitcast(stationary[2]),
                lhsT_scale=stationary[1][:, rows],
                rhs=moving[0][:, cols].bitcast(moving[2]),
                rhs_scale=moving[1][:, cols],
                start=True,
                stop=True,
            )

        offsets = held.tile([P, EXPERTS * N // 16], U16, name="offsets")
        nc.sync.dma_start(offsets[:], offs)

        def listed(window, b):
            return window[:].indirect(offsets[:, b * N // 16 : (b + 1) * N // 16])

        def scalar_gather(dst, src):
            nc.scalar.activation(dst, src, ACT.Copy)

        ts_win, tx_win = placed("ts_win", TS_AT), placed("tx_win", TX_AT)
        warm = held.tile([P, 1], F32, name="warm")
        nc.vector.memset(warm[:], 0.0)
        nc.vector.memset(tx_win[0 : P - 1, :].bitcast(I32), 0)
        nc.vector.memset(ts_win[0 : P - 1, :].bitcast(I32), 0)
        cf_cols = held.tile([P, PACK], F32, name="cf_cols")
        nc.scalar.dma_start(tx_win[P - 1 : P, :], tx[0:1, :])
        nc.scalar.dma_start(ts_win[P - 1 : P, :], ts[0:1, :])
        nc.scalar.dma_start(cf_cols[:], cf.rearrange("(p j) o -> p (j o)", j=PACK))
        warmed = held.tile([P, 1], F32, name="warmed")
        nc.scalar.activation(warmed[:], warm[:], ACT.Sigmoid)
        ident = held.tile([P, P], F32, name="ident")
        make_identity(nc, ident[:])

        x_plane = [placed("x_plane", X_AT + 8 * t) for t in range(PACK)]
        dy_plane = [placed("dy_plane", DY_AT + 8 * t) for t in range(PACK)]
        w1_raw = [placed("w1_raw", W1_AT + 8 * b) for b in range(EXPERTS)]
        w2_raw = [placed("w2_raw", W2_AT + 8 * b) for b in range(EXPERTS)]

        def load_plane(planes, src, t):
            nc.sync.dma_start(planes[t][:], src.rearrange("(p t) n -> t p n", t=PACK)[t])

        def load_w1(b):
            nc.sync.dma_start(w1_raw[b][:], w1[b].rearrange("(p j) f -> p (j f)", j=PACK))

        def load_w2(b):
            nc.sync.dma_start(
                w2_raw[b][:].rearrange("p (c e) -> p c e", c=PACK), w2[b].rearrange("(c p) e -> p c e", c=PACK)
            )

        for t in range(PACK):
            load_plane(x_plane, xT, t)
        load_w1(0)
        load_w1(1)
        load_plane(dy_plane, dyT, 0)
        load_plane(dy_plane, dyT, 1)
        load_w2(0)
        load_plane(dy_plane, dyT, 2)
        load_plane(dy_plane, dyT, 3)
        load_w2(1)

        def gather_tokens(window, name, banks):
            picked = held.tile([P, EXPERTS * N], F32, name=name)
            scalar_gather(picked[:], window[:].indirect(offsets[:]))
            for b in range(EXPERTS):
                for r in range(PACK):
                    nc.tensor.transpose(
                        bank[banks[b]][:, r * P : (r + 1) * P], picked[:, b * N + r : (b + 1) * N : PACK], ident[:]
                    )

        def token_columns(cols, banks):
            for b in range(EXPERTS):
                scalar_copy(cols[:, b * PACK : (b + 1) * PACK], bank[banks[b]][:, P - 1 : N : P])

        def group_w1(copy, b, g, cols, run=PACK):
            copy(
                g[:, cols.start * PACK : cols.stop * PACK].rearrange("p (c i j) -> p c j i", i=run, j=PACK),
                w1_raw[b][:].rearrange("p (j f) -> p j f", j=PACK)[:, :, cols].rearrange("p j (c i) -> p c j i", i=run),
            )

        def turn_w2(rounded, g, banks):
            g_words, words = g[:].bitcast(F32), rounded[:].bitcast(F32)
            for side in range(2):
                turned = bank[banks[side]]
                for k in range(PACK):
                    first = (2 * side + k // 2) * 2 * P
                    nc.tensor.transpose(turned[:, k * P : (k + 1) * P], words[:, first + k % 2 : first + 2 * P : 2], ident[:])
                scalar_copy(
                    g_words[:, side * N : (side + 1) * N].rearrange("p (c f u) -> p c f u", c=2, u=2),
                    turned[:].rearrange("p (c u f) -> p c f u", c=2, u=2),
                )

        def along_features(copy, picked, g, places=slice(0, PACK)):
            copy(
                g[:].rearrange("p (r s i t) -> p s r i t", s=P // 2, i=2, t=PACK),
                picked.rearrange("p t (s i r) -> p s r i t", r=PACK, i=2)[:, :, places],
            )

        def x_along_slots(copy, t, which):
            words = x_both[:, t].bitcast(F32)
            turned = bank[which]
            for b in range(EXPERTS):
                for v in range(2):
                    k = 2 * b + v
                    nc.tensor.transpose(turned[:, k * P : (k + 1) * P], words[:, b * 256 + v : (b + 1) * 256 : 2], ident[:])
            copy(
                x_turned[t // 2][:].bitcast(F32).rearrange("s (t b p v) -> s t b p v", t=2, b=EXPERTS, v=2)[:, t % 2],
                turned[:].rearrange("s (b v p) -> s b p v", b=EXPERTS, v=2),
            )

        def turn_dy(picked, banks):
            for side in range(2):
                for tt in range(2):
                    words = picked[:, 2 * side + tt].bitcast(F32)
                    for v in range(2):
                        k = 2 * tt + v
                        nc.tensor.transpose(bank[banks[side]][:, k * P : (k + 1) * P], words[:, v::2], ident[:])

        def dy_along_slots(copies, g, banks):
            for side in range(2):
                copies[side](
                    g[:].bitcast(F32).rearrange("s (p h k) -> s h p k", h=2, k=4)[:, side],
                    bank[banks[side]][:].rearrange("s (k p) -> s p k", k=4),
                )

        def products(stationary, moving):
            for r in range(PACK):
                product(bank[r][:], stationary, r, moving)

        def scaled(dst, cols):
            for r in range(PACK):
                nc.vector.scalar_tensor_tensor(
                    dst[:, r * N : (r + 1) * N], bank[r][:], cols[:, r : r + 1], cf_row[:], ALU.mult, ALU.mult
                )

        def woven(dst):
            return dst.rearrange("p (c i r) -> p c r i", i=PACK, r=PACK)

        def strands(src, cols=slice(0, N)):
            return src[:].rearrange("p (r n) -> p r n", r=PACK)[:, :, cols].rearrange("p r (c i) -> p c r i", i=PACK)

        def of_z(func, dst, b, scale):
            for r in range(PACK):
                cols = slice(r * N, (r + 1) * N)
                nc.scalar.activation(dst[:, cols], y[b][:, cols], func, scale=scale[:, r : r + 1])

        def woven_product(g, left, right, cols=slice(0, N)):
            nc.vector.tensor_tensor(woven(g), strands(left, cols), strands(right, cols), ALU.mult)

        def paired_product(g, left, right, cols):
            left, right = (
                src[:].rearrange("p (r n) -> p r n", r=PACK)[:, :, cols].rearrange("p r (c i) -> p c r i", i=2)
                for src in (left, right)
            )
            nc.gpsimd.tensor_tensor(g.rearrange("p (c i r) -> p c r i", i=2, r=PACK), left, right, ALU.mult)

        def slope_of(dst, mirror, gate):
            nc.vector.scalar_tensor_tensor(dst, mirror, 1.0, gate, ALU.subtract, ALU.mult)

        def result(stationary, moving, rows, staged, banks):
            for j in range(PACK):
                acc = bank[banks[j]]
                product(acc[:], stationary[j][0], stationary[j][1], moving)
                scalar_copy(staged[:, j * N : (j + 1) * N], acc[:])
                nc.sync.dma_start(rows[j], staged[:, j * N : (j + 1) * N])

        gather_tokens(tx_win, "tx_picked", (0, 1))
        gather_tokens(ts_win, "ts_picked", (6, 7))
        width = EXPERTS * PACK
        for j in range(PACK):
            nc.tensor.transpose(bank[2][:, j * P : (j + 1) * P], cf_cols[:, j : j + 1].to_broadcast([P, P]), ident[:])

        x_both = placed("x_both", FREE_AT + 54, BF16, 2 * WIDE)[:].rearrange("p (t n) -> p t n", t=PACK)
        x_picked = [x_both[:, :, b * N : (b + 1) * N] for b in range(EXPERTS)]
        x_grouped = [placed("x_grouped", FREE_AT + 16, BF16)]

        def gather_x(t):
            vector_copy(x_picked[0][:, t], listed(x_plane[t], 0))
            scalar_gather(x_picked[1][:, t], listed(x_plane[t], 1))

        vector_copy(x_both[:, 0], x_plane[0][:].indirect(offsets[:]))
        vector_copy(x_both[:, 1], x_plane[1][:].indirect(offsets[:]))
        cf_row = held.tile([P, N], F32, name="cf_row")
        scalar_copy(cf_row[:].rearrange("p (m j) -> p m j", j=PACK), bank[2][:].rearrange("p (j m) -> p m j", j=PACK))
        x_turned = [placed("x_turned", X_AT + 4, BF16)]
        x_along_slots(scalar_copy, 0, 4)
        x_along_slots(scalar_copy, 1, 5)
        gather_x(2)
        gather_x(3)
        tx_cols = placed("tx_cols", X_AT + 24.25, F32, width)
        ts_cols = placed("ts_cols", X_AT + 24.3125, F32, width)
        token_columns(tx_cols, (0, 1))
        token_columns(ts_cols, (6, 7))
        gates = placed("gates", X_AT + 24, F32, width)
        columns = placed("columns", X_AT + 26, F32, 2 * width)
        both, inverse = columns[:, :width], columns[:, width:]
        nc.vector.scalar_tensor_tensor(gates[:], ts_cols[:], 0.0, ts_cols[:], ALU.is_equal, ALU.add)
        nc.vector.tensor_tensor(both, tx_cols[:], ts_cols[:], ALU.mult)
        along_features(vector_copy, x_picked[0], x_grouped[0])
        nc.vector.reciprocal(inverse, gates[:])
        low, high = slice(0, N // 2), slice(N // 2, N)
        w1_grouped = placed("w1_grouped", X_AT + 8, BF16)
        group_w1(scalar_copy, 0, w1_grouped, high)
        group_w1(vector_copy, 0, w1_grouped, low)
        x_feat = [operand("x_feat_0", E4M3)]
        w1_q = [operand("w1_q_0", E4M3, X_AT + 23.5)]
        quantize(x_grouped[0][:], x_feat[0])
        x_grouped.append(placed("x_grouped", W1_AT, BF16))
        along_features(scalar_copy, x_picked[1], x_grouped[1])
        quantize(w1_grouped[:], w1_q[0])

        def of_expert(cols, b):
            return cols[:, b * PACK : (b + 1) * PACK]

        y = [placed("y", at) for at in (FREE_AT + 42, FREE_AT + 54)]
        sigmoid = [placed("sigmoid", XB_AT - 8 * b) for b in range(EXPERTS)]
        x_turned.append(placed("x_turned", W1_AT + 4, BF16))
        x_along_slots(vector_copy, 2, 4)
        x_along_slots(vector_copy, 3, 5)
        products(x_feat[0], w1_q[0])
        late_grouped = placed("late_grouped", X_AT + 8, BF16)
        group_w1(gpsimd_copy, 1, late_grouped, slice(0, N), 1)
        scaled(y[0], of_expert(both, 0))
        of_z(ACT.Sigmoid, sigmoid[0], 0, of_expert(inverse, 0))
        x_feat.append(operand("x_feat_1", E4M3, W1_AT + 8))
        w1_q.append(operand("w1_q_1", E4M3))
        quantize(x_grouped[1][:], x_feat[1])
        quantize(late_grouped[:], w1_q[1])
        x_slot = [operand("x_slot_%d" % k, E4M3, W1_AT + 10 + 2 * k) for k in range(2)]
        for k in range(2):
            quantize(x_turned[k][:], x_slot[k])
        dy_tiles = [placed("dy_picked", FREE_AT + 20 + 4 * b, BF16) for b in range(EXPERTS)]
        dy_picked = [g[:].rearrange("p (t n) -> p t n", t=PACK) for g in dy_tiles]
        for t in (0, 1):
            scalar_gather(dy_picked[0][:, t], listed(dy_plane[t], 0))

        products(x_feat[1], w1_q[1])
        rounded = placed("rounded", W1_AT + 4, BF16)
        gpsimd_copy(rounded[:], w2_raw[0][:])
        scaled(y[1], of_expert(both, 1))
        of_z(ACT.Sigmoid, sigmoid[1], 1, of_expert(inverse, 1))
        vector_copy(dy_picked[0][:, 2], listed(dy_plane[2], 0))
        first_hidden = placed("first_hidden", W2_AT, BF16)
        woven_product(first_hidden[:], y[0], sigmoid[0])
        minus_columns = placed("minus_columns", W2_AT + 7, F32, 2 * width)
        minus_both, minus_inverse = minus_columns[:, :width], minus_columns[:, width:]
        nc.scalar.activation(minus_columns[:], columns[:], ACT.Copy, scale=-1.0)
        first_inverse = dy_tiles[1][:].bitcast(F32)[:, N - 2 : N + 2]
        scalar_copy(first_inverse, of_expert(minus_inverse, 0))
        scalar_gather(dy_picked[1][:, 0], listed(dy_plane[0], 1))
        scalar_gather(dy_picked[0][:, 3], listed(dy_plane[3], 0))
        early = slice(0, 3 * P)
        hidden = placed("hidden", W2_AT + 4, BF16, 3 * N)
        woven_product(hidden[:], y[1], sigmoid[1], early)
        w2_grouped = placed("w2_grouped", FREE_AT + 4, BF16)
        turn_w2(rounded, w2_grouped, (4, 5))
        scalar_gather(dy_picked[1][:, 3], listed(dy_plane[3], 1))
        dy_grouped = placed("dy_grouped", FREE_AT + 8, BF16)
        along_features(vector_copy, dy_picked[0], dy_grouped)
        turn_dy(dy_picked[0], (6, 7))
        w2_q, dy_feat = [operand("w2_0", E4M3, FREE_AT + 19)], [operand("dy_feat_0", E5M2)]
        quantize(w2_grouped[:], w2_q[0])
        quantize(dy_grouped[:], dy_feat[0])
        h_q = [operand("h_0", E4M3, FREE_AT + 7), operand("h_1", E4M3, FREE_AT + 21, 3 * P)]
        quantize(hidden[:], h_q[1], early)
        quantize(first_hidden[:], h_q[0])
        mirrored = placed("mirrored", DY_AT + 24)
        of_z(ACT.Silu, mirrored, 0, first_inverse)

        products(dy_feat[0], w2_q[0])
        rounded = placed("rounded", W2_AT, BF16)
        gpsimd_copy(rounded[:], w2_raw[1][:])
        dh = [placed("dh", DY_AT)]
        scaled(dh[0], of_expert(minus_both, 0))
        dy_turned = placed("dy_turned", FREE_AT + 42, BF16)
        dy_along_slots((vector_copy, scalar_copy), dy_turned, (6, 7))
        for t in (1, 2):
            scalar_gather(dy_picked[1][:, t], listed(dy_plane[t], 1))
        turn_dy(dy_picked[1], (6, 7))
        slope = placed("slope", W2_AT + 10)
        slope_of(slope[:], mirrored[:], sigmoid[0][:])
        dy_grouped = placed("dy_grouped", X_AT + 8, BF16)
        along_features(scalar_copy, dy_picked[1], dy_grouped)
        w2_grouped = placed("w2_grouped", X_AT + 12, BF16)
        turn_w2(rounded, w2_grouped, (4, 5))
        dy_slot = [operand("dy_slot_0", E5M2, W2_AT + 8)]
        quantize(dy_turned[:], dy_slot[0])
        gradient = placed("gradient", FREE_AT + 38, BF16)
        woven_product(gradient[:], slope, dh[0])

        def blocks(whole):
            return [(whole, j) for j in range(PACK)]

        def x_blocks(b):
            return [(x_slot[t // 2], t % 2 * EXPERTS + b) for t in range(PACK)]

        dy_turned = placed("dy_turned", FREE_AT + 42, BF16)
        dy_along_slots((scalar_copy, scalar_copy), dy_turned, (6, 7))
        result(blocks(h_q[0]), dy_slot[0], out_1[0].rearrange("(c p) e -> c p e", c=PACK), placed("staged", X_AT + 16), (4, 5, 6, 7))
        dh.append(placed("dh", DY_AT + 8))
        dy_feat.append(operand("dy_feat_1", E5M2))
        w2_q.append(operand("w2_1", E4M3))
        dy_slot.append(operand("dy_slot_1", E5M2))
        quantize(dy_grouped[:], dy_feat[1])
        quantize(w2_grouped[:], w2_q[1])
        products(dy_feat[1], w2_q[1])
        da = operand("da_0", E5M2, X_AT + 11)
        quantize(gradient[:], da)
        quantize(dy_turned[:], dy_slot[1])
        last_block = placed("last_block", FREE_AT + 41.5, BF16, N)
        paired_product(last_block[:], y[1], sigmoid[1], slice(3 * P, N))
        late_mirrored = [placed("late_mirrored", FREE_AT + at, F32, N) for at in (36.5, 38.5, 42.5, 44.5)]
        for r in range(PACK):
            nc.scalar.activation(late_mirrored[r][:], y[1][:, r * N : (r + 1) * N], ACT.Silu, scale=of_expert(minus_inverse, 1)[:, r : r + 1])
        result(x_blocks(0), da, out_0[0].rearrange("(p t) f -> t p f", t=PACK), placed("staged", X_AT), (4, 5, 6, 7))
        scaled(dh[1], of_expert(minus_both, 1))
        slope = placed("slope", FREE_AT + 12)
        for r in range(PACK):
            cols = slice(r * N, (r + 1) * N)
            slope_of(slope[:, cols], late_mirrored[r][:], sigmoid[1][:, cols])
        h_last = operand("h_last", E4M3, FREE_AT + 42.5, P)
        quantize(last_block[:], h_last, slice(0, P))
        result(blocks(h_q[1])[:3] + [(h_last, 0)], dy_slot[1], out_1[1].rearrange("(c p) e -> c p e", c=PACK), placed("staged", W1_AT), (4, 5, 6, 7))

        da = operand("da_1", E5M2)
        staged = placed("staged", DY_AT + 16)
        rows = out_0[1].rearrange("(p t) f -> p t f", t=PACK)
        gradient = placed("gradient", FREE_AT + 8, BF16)
        pieces = [slice(c * P, (c + 1) * P) for c in range(PACK)]
        for c, cols in enumerate(pieces):
            woven_product(gradient[:, c * N : (c + 1) * N], slope, dh[1], cols)
            if c:
                quantize(gradient[:, (c - 1) * N : c * N], da, pieces[c - 1])
        quantize(gradient[:, (PACK - 1) * N :], da, pieces[-1])
        for c, cols in enumerate(pieces):
            for t, (whole, j) in enumerate(x_blocks(1)):
                product(bank[c][:, t * P : (t + 1) * P], whole, j, da, cols)
            piece = staged[:, c * N : (c + 1) * N]
            (vector_copy if c == PACK - 1 else scalar_copy)(piece, bank[c][:])
            nc.sync.dma_start(rows[:, :, cols], piece.rearrange("p (t f) -> p t f", t=PACK))
